import numpy as np
import ml_dtypes


def mxq(x, axis, fmt="e4m3"):
    dtype, down = {"e4m3": (ml_dtypes.float8_e4m3fn, 7), "e5m2": (ml_dtypes.float8_e5m2, 14)}[fmt]
    v = np.moveaxis(np.asarray(x, np.float32).astype(ml_dtypes.bfloat16).astype(np.float64), axis, -1)
    blocks = v.reshape(v.shape[:-1] + (-1, 32))
    amax = np.abs(blocks).max(-1, keepdims=True)
    byte = np.maximum(np.where(amax > 0, np.frexp(amax)[1] - 1 + 127, 0) - down, 1)
    scale = np.exp2(byte - 127.0)
    codes = (blocks / scale).astype(np.float32).astype(dtype).astype(np.float64)
    return np.moveaxis((codes * scale).reshape(v.shape), -1, axis)


WIDE = False


def mx_kscale(k):
    if not WIDE:
        return np.ones(k)
    levels = np.array([10, -10, 5, -5, 0])
    if k % 512:
        return np.exp2(np.random.permutation(np.resize(levels, k // 32))).repeat(32)
    a = np.empty((k // 512, 16))
    for p in range(k // 512):
        a[p, :8] = np.random.permutation(np.resize(levels, 8))
        for g in range(8):
            far = levels[np.abs(levels - a[p, g]) >= 10]
            a[p, g + 8] = far[np.random.randint(len(far))]
    return np.exp2(a.ravel()).repeat(32)


def f64(x):
    return np.asarray(x).astype(np.float64)


def striped(idx):
    return np.tile(idx.reshape(-1, 16).T, (8, 1)).astype(np.uint16)


def unstriped(offs):
    return offs[:16].T.reshape(-1).astype(np.int64)


E2M1 = np.array([0.0, 0.5, 1.0, 1.5, 2.0, 3.0, 4.0, 6.0, -0.0, -0.5, -1.0, -1.5, -2.0, -3.0, -4.0, -6.0])


def pack_weight(w, fmt):
    k, n = w.shape
    w = f64(np.asarray(w, np.float32).astype(ml_dtypes.bfloat16)).reshape(k // 32, 32, n)
    amax = np.abs(w).max(1)
    if fmt == "e4m3":
        byte = np.frexp(amax)[1] - 1 + 127 - 7
    else:
        mant, ex = np.frexp(amax / 6.0)
        byte = np.where(mant > 0.5, ex, ex - 1) + 127
    byte = np.clip(np.where(amax > 0, byte, 1), 1, 254)
    scaled = (w * np.exp2(127.0 - byte)[:, None, :]).reshape(k, n).astype(np.float32)
    by_word = np.ascontiguousarray(scaled.reshape(k // 512, 128, 4, n).transpose(0, 1, 3, 2))
    if fmt == "e4m3":
        words = by_word.astype(ml_dtypes.float8_e4m3fn).view(np.uint8)
    else:
        c = by_word.astype(ml_dtypes.float4_e2m1fn).view(np.uint8) & 0xF
        words = (c[..., 0::2] | (c[..., 1::2] << 4)).reshape(k // 512, 128, 2 * n)
    return np.ascontiguousarray(words), np.ascontiguousarray(byte.astype(np.uint8).reshape(k // 512, 16, n))


def unpack_weight(words, scales, fmt):
    g, _, n = scales.shape
    words = np.ascontiguousarray(words).reshape(g, 128, n, -1)
    if fmt == "e4m3":
        vals = words.view(ml_dtypes.float8_e4m3fn).astype(np.float64)
    else:
        nib = np.empty((g, 128, n, 4), np.uint8)
        nib[..., 0::2] = words & 0xF
        nib[..., 1::2] = words >> 4
        vals = E2M1[nib]
    vals = vals * np.repeat(np.exp2(scales.astype(np.float64) - 127.0), 8, axis=1)[..., None]
    return vals.transpose(0, 1, 3, 2).reshape(g * 512, n)


def gelu(v):
    return 0.5 * v * (1.0 + np.tanh(np.sqrt(2.0 / np.pi) * (v + 0.044715 * v**3)))


def bf(x):
    return np.asarray(x, np.float32).astype(ml_dtypes.bfloat16)

def planes(Y):
    n, m = Y.shape
    b = f64(bf(Y)).reshape(n // 32, 32, m)
    amax = np.abs(b).max(1)
    byte = np.clip(np.where(amax > 0, np.frexp(amax)[1] - 1 + 127 - 7, 1), 1, 254)
    codes = (b * np.exp2(127.0 - byte)[:, None, :]).reshape(n, m).astype(np.float32).astype(ml_dtypes.float8_e4m3fn).view(np.uint8)
    words = codes.reshape(n // 512, 128, 4, m).transpose(0, 1, 3, 2)
    return np.ascontiguousarray(words), np.ascontiguousarray(byte.astype(np.uint8).reshape(n // 512, 16, m))


K, K2, T, T2, S, H, N = 1024, 512, 4096, 2048, 1024, 1024, 1024


def setup_inputs():
    n = np.random.standard_normal
    s = mx_kscale(K)[:, None]
    s2 = mx_kscale(K2)[:, None]
    u = mx_kscale(H)[:, None]
    row = np.exp(0.8 * n(N))[None, :]
    tab_words, tab_scales = pack_weight(n((K, T)) * s, "e4m3")
    tab2_words, tab2_scales = pack_weight(n((K2, T2)) * s2, "e4m3")
    wi_words, wi_scales = pack_weight(n((K2, H)) / np.sqrt(K2) / s2, "e2m1")
    wr_words, wr_scales = pack_weight(n((H, N)) / np.sqrt(H) * row / u, "e4m3")
    return {
        "tab_words": tab_words, "tab_scales": tab_scales,
        "tab2_words": tab2_words, "tab2_scales": tab2_scales,
        "offs": striped(np.random.permutation(T)[:S]),
        "offs2": striped(np.random.permutation(T2)[:S]),
        "we": (n((K, H)) / np.sqrt(K) / s).astype(np.float32),
        "wi_words": wi_words, "wi_scales": wi_scales,
        "gain": (np.exp(0.3 * n(H)) * u[:, 0]).astype(np.float32),
        "wr_words": wr_words, "wr_scales": wr_scales,
    }


def reference(tab_words, tab_scales, tab2_words, tab2_scales, offs, offs2, we, wi_words, wi_scales, gain, wr_words, wr_scales):
    v = unpack_weight(tab_words, tab_scales, "e4m3")[:, unstriped(offs)]
    v2 = unpack_weight(tab2_words, tab2_scales, "e4m3")[:, unstriped(offs2)]
    wi = unpack_weight(wi_words, wi_scales, "e2m1")
    wr = unpack_weight(wr_words, wr_scales, "e4m3")
    e = mxq(f64(we), 0, "e4m3").T @ v
    i = wi.T @ v2
    h = np.log(1.0 + np.exp(e - i)) * f64(gain)[:, None]
    y = wr.T @ mxq(h, 0, "e4m3")
    words, scales = planes(y)
    return y, words, scales

@@ -1,0 +1,279 @@
+from contextlib import ExitStack
+
+import concourse.mybir as mybir
+
+F32 = mybir.dt.float32
+BF16 = mybir.dt.bfloat16
+I32 = mybir.dt.int32
+U32 = mybir.dt.uint32
+U16 = mybir.dt.uint16
+U8 = mybir.dt.uint8
+FP8X4 = mybir.dt.float8_e4m3fn_x4
+FP4X4 = mybir.dt.float4_e2m1fn_x4
+ACT = mybir.ActivationFunctionType
+ALU = mybir.AluOpType
+
+P = 128
+PACK = 4
+GROUP = 512
+T, T2, S, H, N = 4096, 2048, 1024, 1024, 1024
+HALF = 512
+CHUNK = 256
+TINY = 2.0 ** -60
+FLOPS = 5368709120
+
+
+def tile_list_cortical_softplus_currents_kernel(
+    tc, tab_words, tab_scales, tab2_words, tab2_scales, offs, offs2, we, wi_words, wi_scales, gain,
+    wr_words, wr_scales, out_0, out_1, out_2,
+):
+    nc = tc.nc
+    with ExitStack() as ctx:
+        lists = ctx.enter_context(tc.tile_pool(name="lists", bufs=1))
+        keep = ctx.enter_context(tc.tile_pool(name="keep", bufs=1))
+        big = ctx.enter_context(tc.tile_pool(name="big", bufs=4))
+        ring = ctx.enter_context(tc.tile_pool(name="ring", bufs=4))
+        psum = ctx.enter_context(tc.psum_pool(name="psum", bufs=8))
+
+        def held(shape, dtype, name):
+            return keep.tile(shape, dtype, name=name, align_bytes=64)
+
+        idx = lists.tile([P, S // 16], U16, name="idx")
+        idx2 = lists.tile([P, S // 16], U16, name="idx2")
+
+        tab_sc = held([P, T], U8, "tab_sc")
+        tab2_sc = held([P, T2], U8, "tab2_sc")
+        w_sc_raw = held([P, H], U8, "w_sc_raw")
+        nc.vector.memset(tab_sc[:].bitcast(I32), 0)
+        nc.vector.memset(tab2_sc[:].bitcast(I32), 0)
+        nc.gpsimd.memset(w_sc_raw[:].bitcast(I32), 0)
+        tiny = held([P, 1], F32, "tiny")
+        nc.gpsimd.memset(tiny[:], TINY)
+
+        def load_we(a, g, pieces=1):
+            raw = held([P, PACK, GROUP], F32, "we_raw_%d_%d" % (a, g))
+            rows = we[a * GROUP:(a + 1) * GROUP, g * GROUP:(g + 1) * GROUP].rearrange("(p i) c -> p i c", i=PACK)
+            step = PACK // pieces
+            for i in range(0, PACK, step):
+                nc.sync.dma_start(out=raw[:, i:i + step, :], in_=rows[:, i:i + step, :])
+            return raw
+
+        def load_words(tile, words, pieces=1):
+            src = words.rearrange("p c i -> p (c i)").bitcast(I32)
+            step = src.shape[1] // pieces
+            for c in range(0, src.shape[1], step):
+                nc.sync.dma_start(out=tile[:, c:c + step], in_=src[:, c:c + step])
+
+        def load_scale_rows(tile, scales, first):
+            passes = scales.shape[0]
+            for q in range(4):
+                rows = tile[32 * q + first:32 * q + first + 4 * passes, :]
+                nc.sync.dma_start(out=rows.bitcast(I32), in_=scales[:, 4 * q:4 * q + 4, :].bitcast(I32))
+
+        we_raw = {}
+        nc.sync.dma_start(idx[:], offs)
+        nc.sync.dma_start(idx2[:], offs2)
+        gain_sb = held([P, 2, PACK], F32, "gain_sb")
+        nc.sync.dma_start(out=gain_sb[:], in_=gain.rearrange("(g p t) -> p g t", g=2, t=PACK))
+        wi_raw = held([P, 2 * H], U8, "wi_raw")
+        nc.sync.dma_start(out=wi_raw[:].bitcast(I32), in_=wi_words[0].bitcast(I32))
+        tab2_w = held([P, T2], I32, "tab2_w")
+        load_words(tab2_w, tab2_words[0], 2)
+        we_raw[0, 0] = load_we(0, 0, 2)
+        load_scale_rows(tab_sc, tab_scales, 4)
+        we_raw[0, 1] = load_we(0, 1)
+        load_scale_rows(tab2_sc, tab2_scales, 0)
+        tab_w = [big.tile([P, T], I32, name="tab_w", tag="big", align_bytes=64) for a in range(2)]
+        load_words(tab_w[0], tab_words[0])
+        load_scale_rows(w_sc_raw, wi_scales, 0)
+        we_raw[1, 0] = load_we(1, 0)
+        load_scale_rows(w_sc_raw, wr_scales, 8)
+        we_raw[1, 1] = load_we(1, 1)
+        load_words(tab_w[1], tab_words[1])
+        wr_raw = [held([P, N], I32, "wr_raw_%d" % a) for a in range(2)]
+        for a in range(2):
+            load_words(wr_raw[a], wr_words[a])
+
+        def gather_words(table, offsets, half, name):
+            picked = held([P, HALF], U32, name)
+            cols = HALF // 16
+            nc.vector.tensor_copy(picked[:], table[:].bitcast(U32).indirect(offsets[:, half * cols:(half + 1) * cols]))
+            return picked
+
+        def quantise_we(a, g):
+            dealt = ring.tile([P, PACK, P, PACK], BF16, name="we_bf", bufs=2, align_bytes=64)
+            nc.scalar.activation(
+                out=dealt[:].rearrange("p t m i -> p m i t"),
+                in_=we_raw[a, g][:].rearrange("p i (m t) -> p m i t", t=PACK),
+                func=ACT.Copy, scale=-1.0,
+            )
+            codes = held([P, GROUP], U32, "we_codes_%d_%d" % (a, g))
+            scales = held([P, GROUP], U8, "we_scales_%d_%d" % (a, g))
+            nc.vector.quantize_mx(out=codes[:].bitcast(FP8X4), scales=scales[:],
+                                  in_=dealt[:].rearrange("p t m i -> p (t m i)"))
+            return codes, scales
+
+        v2_w = [gather_words(tab2_w, idx2, half, "v2_w_%d" % half) for half in range(2)]
+        we_q = {}
+        we_q[0, 0] = quantise_we(0, 0)
+
+        wi_w = held([P, 2 * H], U8, "wi_w")
+        for g in range(2):
+            cols = slice(g * 2 * GROUP, (g + 1) * 2 * GROUP)
+            nc.vector.tensor_copy(
+                out=wi_w[:, cols].rearrange("p (t c i b) -> p c t i b", t=PACK, i=8, b=2),
+                in_=wi_raw[:, cols].rearrange("p (c i t b) -> p c t i b", t=PACK, i=8, b=2),
+            )
+        neg_gain = held([P, 2 * PACK], F32, "neg_gain")
+        nc.vector.tensor_scalar(out=neg_gain[:], in0=gain_sb[:].rearrange("p g t -> p (g t)"),
+                                scalar1=-1.0, scalar2=None, op0=ALU.mult)
+
+        v_sc = held([P, S], U8, "v_sc")
+        nc.vector.tensor_copy(v_sc[:], tab_sc[:].indirect(idx[:]))
+        v2_sc = held([P, S], U8, "v2_sc")
+        nc.vector.tensor_copy(v2_sc[:], tab2_sc[:].indirect(idx2[:]))
+
+        we_q[0, 1] = quantise_we(0, 1)
+        v_w = {}
+        for half in range(2):
+            v_w[0, half] = gather_words(tab_w[0], idx, half, "v_w_0_%d" % half)
+        w_sc = held([P, H], U8, "w_sc")
+        nc.vector.tensor_copy(
+            out=w_sc[:].rearrange("p (g t c i) -> p g c t i", g=2, t=PACK, i=16),
+            in_=w_sc_raw[:].rearrange("p (g c i t) -> p g c t i", g=2, t=PACK, i=16),
+        )
+        we_q[1, 0] = quantise_we(1, 0)
+        we_q[1, 1] = quantise_we(1, 1)
+        for half in range(2):
+            v_w[1, half] = gather_words(tab_w[1], idx, half, "v_w_1_%d" % half)
+
+        wr_w = [held([P, N], I32, "wr_w_%d" % a) for a in range(2)]
+
+        def deal_wr(a):
+            nc.vector.tensor_copy(
+                out=wr_w[a][:].rearrange("p (g t c i) -> p g c t i", g=2, t=PACK, i=4),
+                in_=wr_raw[a][:].rearrange("p (g c i t) -> p g c t i", g=2, t=PACK, i=4),
+            )
+
+        y_codes = held([P, 2, S], I32, "y_codes")
+        y_scales = held([P, 2, S], U8, "y_scales")
+
+        def drives(half):
+            js = slice(half * HALF, (half + 1) * HALF)
+            banks = [psum.tile([P, HALF], F32, name="bank", tag="bank") for u in range(8)]
+
+            def excite(a, u):
+                g, t = divmod(u, PACK)
+                codes, scales = we_q[a, g]
+                nc.tensor.matmul_mx(
+                    out=banks[u][:], lhsT=codes[:, t * P:(t + 1) * P].bitcast(FP8X4),
+                    lhsT_scale=scales[:, t * P:(t + 1) * P],
+                    rhs=v_w[a, half][:].bitcast(FP8X4), rhs_scale=v_sc[4 + 4 * a:, js],
+                    start=(a == 0), stop=(a == 1))
+
+            def inhibit(u):
+                nc.tensor.matmul_mx(
+                    out=banks[u][:], lhsT=wi_w[:, u * 2 * P:(u + 1) * 2 * P].bitcast(FP4X4),
+                    lhsT_scale=w_sc[:, u * P:(u + 1) * P],
+                    rhs=v2_w[half][:].bitcast(FP8X4), rhs_scale=v2_sc[:, js], start=False, stop=False)
+
+            if half == 0:
+                for u in range(8):
+                    excite(0, u)
+                for u in range(8):
+                    inhibit(u)
+                for u in range(8):
+                    excite(1, u)
+            else:
+                for u in range(8):
+                    excite(0, u)
+                    inhibit(u)
+                    excite(1, u)
+            sig = big.tile([P, 8, HALF], F32, name="sig", tag="big", align_bytes=64)
+            lin = big.tile([P, 8, HALF], F32, name="lin", tag="big", align_bytes=64)
+            for u in range(8):
+                nc.scalar.activation(out=sig[:, u, :], in_=banks[u][:], func=ACT.Sigmoid)
+                nc.vector.tensor_scalar(out=lin[:, u, :], in0=banks[u][:], scalar1=neg_gain[:, u:u + 1],
+                                        scalar2=None, op0=ALU.mult)
+            return sig, lin
+
+        def logs(sig, part):
+            cols = slice(part * CHUNK, (part + 1) * CHUNK)
+            nc.scalar.activation(out=sig[:, :, cols], in_=sig[:, :, cols], func=ACT.Ln, bias=tiny[:])
+
+        def rates(sig, lin, part):
+            cols = slice(part * CHUNK, (part + 1) * CHUNK)
+            flat = [ring.tile([P, PACK, CHUNK], BF16, name="h_flat", align_bytes=64) for g in range(2)]
+            for u in range(8):
+                g, t = divmod(u, PACK)
+                nc.vector.scalar_tensor_tensor(
+                    out=flat[g][:, t, :], in0=sig[:, u, cols], scalar=neg_gain[:, u:u + 1], in1=lin[:, u, cols],
+                    op0=ALU.mult, op1=ALU.max)
+            woven = [ring.tile([P, CHUNK, PACK], BF16, name="h_woven", align_bytes=64) for g in range(2)]
+            for g in range(2):
+                nc.vector.tensor_copy(out=woven[g][:].rearrange("p (c i) t -> p c t i", i=4),
+                                      in_=flat[g][:].rearrange("p t (c i) -> p c t i", i=4))
+            h_q = []
+            for g in range(2):
+                codes = ring.tile([P, CHUNK], U32, name="h_codes", align_bytes=64)
+                scales = ring.tile([P, CHUNK], U8, name="h_scales", align_bytes=64)
+                nc.vector.quantize_mx(out=codes[:].bitcast(FP8X4), scales=scales[:],
+                                      in_=woven[g][:].rearrange("p c t -> p (c t)"))
+                h_q.append((codes, scales))
+            return h_q
+
+        def currents(h_q, chunk):
+            js = slice(chunk * CHUNK, (chunk + 1) * CHUNK)
+            ys = []
+            for g in range(2):
+                y = ring.tile([P, PACK, CHUNK], F32, name="y", align_bytes=64)
+                for pair in range(2):
+                    bank = psum.tile([P, 2, CHUNK], F32, name="bank", tag="bank")
+                    for s in range(2):
+                        u = g * PACK + 2 * pair + s
+                        for a in range(2):
+                            codes, scales = h_q[a]
+                            nc.tensor.matmul_mx(
+                                out=bank[:, s, :], lhsT=wr_w[a][:, u * P:(u + 1) * P].bitcast(FP8X4),
+                                lhsT_scale=w_sc[8 + 4 * a:, u * P:(u + 1) * P],
+                                rhs=codes[:].bitcast(FP8X4), rhs_scale=scales[:],
+                                start=(a == 0), stop=(a == 1))
+                    nc.scalar.copy(out=y[:, 2 * pair:2 * pair + 2, :], in_=bank[:])
+                rows = out_0[g * GROUP:(g + 1) * GROUP, js].rearrange("(p t) j -> p t j", t=PACK)
+                nc.sync.dma_start(out=rows, in_=y[:])
+                ys.append(y)
+            woven = [ring.tile([P, CHUNK, PACK], BF16, name="y_woven", align_bytes=64) for g in range(2)]
+            for g in range(2):
+                nc.vector.tensor_copy(out=woven[g][:].rearrange("p (c i) t -> p c t i", i=4),
+                                      in_=ys[g][:].rearrange("p t (c i) -> p c t i", i=4))
+            for g in range(2):
+                nc.vector.quantize_mx(out=y_codes[:, g, js].bitcast(FP8X4), scales=y_scales[:, g, js],
+                                      in_=woven[g][:].rearrange("p c t -> p (c t)"))
+            words = out_1.rearrange("g p j t -> p g (j t)").bitcast(I32)
+            nc.sync.dma_start(out=words[:, :, js], in_=y_codes[:, :, js])
+
+        def store_scales(half):
+            cols = slice(half * HALF // 4, (half + 1) * HALF // 4)
+            for q in range(4):
+                nc.sync.dma_start(
+                    out=out_2[:, 4 * q:4 * q + 4, :].bitcast(I32).rearrange("g r c -> r g c")[:, :, cols],
+                    in_=y_scales[32 * q:32 * q + 4, :, :].bitcast(I32)[:, :, cols])
+
+        sig0, lin0 = drives(0)
+        deal_wr(0)
+        deal_wr(1)
+        logs(sig0, 0)
+        logs(sig0, 1)
+        h0 = rates(sig0, lin0, 0)
+        sig1, lin1 = drives(1)
+        h1 = rates(sig0, lin0, 1)
+        currents(h0, 0)
+        logs(sig1, 0)
+        logs(sig1, 1)
+        currents(h1, 1)
+        store_scales(0)
+        h2 = rates(sig1, lin1, 0)
+        h3 = rates(sig1, lin1, 1)
+        currents(h2, 2)
+        currents(h3, 3)
+        store_scales(1)

@@ -18,7 +18,9 @@ PACK = 4
 GROUP = 512
 T, T2, S, H, N = 4096, 2048, 1024, 1024, 1024
 HALF = 512
-CHUNK = 256
+SUB = 128
+WIDTHS = [128,256,128,256,128,128]
+SCALAR_WEAVES = [0,0,0,1,1,1,1,2]
 TINY = 2.0 ** -60
 FLOPS = 5368709120
 
@@ -38,17 +40,23 @@ def tile_list_cortical_softplus_currents_kernel(
         def held(shape, dtype, name):
             return keep.tile(shape, dtype, name=name, align_bytes=64)
 
+        def clock(ap, name):
+            c = held([P, 1], ap.dtype, name)
+            nc.gpsimd.tensor_copy(out=c[:], in_=ap)
+
         idx = lists.tile([P, S // 16], U16, name="idx")
         idx2 = lists.tile([P, S // 16], U16, name="idx2")
 
         tab_sc = held([P, T], U8, "tab_sc")
         tab2_sc = held([P, T2], U8, "tab2_sc")
         w_sc_raw = held([P, H], U8, "w_sc_raw")
+        zero = keep.tile([P, 1], F32, name="zero", tag="bias")
+        nc.gpsimd.memset(zero[:], 0.0)
         nc.vector.memset(tab_sc[:].bitcast(I32), 0)
         nc.vector.memset(tab2_sc[:].bitcast(I32), 0)
         nc.gpsimd.memset(w_sc_raw[:].bitcast(I32), 0)
-        tiny = held([P, 1], F32, "tiny")
-        nc.gpsimd.memset(tiny[:], TINY)
+        warm = held([P, 1], F32, "warm")
+        nc.scalar.activation(out=warm[:], in_=zero[:], func=ACT.Sigmoid)
 
         def load_we(a, g, pieces=1):
             raw = held([P, PACK, GROUP], F32, "we_raw_%d_%d" % (a, g))
@@ -58,41 +66,41 @@ def tile_list_cortical_softplus_currents_kernel(
                 nc.sync.dma_start(out=raw[:, i:i + step, :], in_=rows[:, i:i + step, :])
             return raw
 
-        def load_words(tile, words, pieces=1):
+        def load_words(tile, words, first, last):
             src = words.rearrange("p c i -> p (c i)").bitcast(I32)
-            step = src.shape[1] // pieces
-            for c in range(0, src.shape[1], step):
-                nc.sync.dma_start(out=tile[:, c:c + step], in_=src[:, c:c + step])
+            nc.sync.dma_start(out=tile[:, first:last], in_=src[:, first:last])
 
-        def load_scale_rows(tile, scales, first):
+        def load_scale_rows(queue, tile, scales, first):
             passes = scales.shape[0]
             for q in range(4):
                 rows = tile[32 * q + first:32 * q + first + 4 * passes, :]
-                nc.sync.dma_start(out=rows.bitcast(I32), in_=scales[:, 4 * q:4 * q + 4, :].bitcast(I32))
+                queue.dma_start(out=rows.bitcast(I32), in_=scales[:, 4 * q:4 * q + 4, :].bitcast(I32))
 
         we_raw = {}
-        nc.sync.dma_start(idx[:], offs)
         nc.sync.dma_start(idx2[:], offs2)
-        gain_sb = held([P, 2, PACK], F32, "gain_sb")
-        nc.sync.dma_start(out=gain_sb[:], in_=gain.rearrange("(g p t) -> p g t", g=2, t=PACK))
+        nc.sync.dma_start(idx[:], offs)
+        tab2_w = held([P, T2], I32, "tab2_w")
+        load_words(tab2_w, tab2_words[0], 0, T2 // 2)
+        load_words(tab2_w, tab2_words[0], T2 // 2, T2)
         wi_raw = held([P, 2 * H], U8, "wi_raw")
         nc.sync.dma_start(out=wi_raw[:].bitcast(I32), in_=wi_words[0].bitcast(I32))
-        tab2_w = held([P, T2], I32, "tab2_w")
-        load_words(tab2_w, tab2_words[0], 2)
+        gain_sb = held([P, 2, PACK], F32, "gain_sb")
+        nc.sync.dma_start(out=gain_sb[:], in_=gain.rearrange("(g p t) -> p g t", g=2, t=PACK))
         we_raw[0, 0] = load_we(0, 0, 2)
-        load_scale_rows(tab_sc, tab_scales, 4)
-        we_raw[0, 1] = load_we(0, 1)
-        load_scale_rows(tab2_sc, tab2_scales, 0)
+        load_scale_rows(nc.sync, tab_sc, tab_scales, 4)
         tab_w = [big.tile([P, T], I32, name="tab_w", tag="big", align_bytes=64) for a in range(2)]
-        load_words(tab_w[0], tab_words[0])
-        load_scale_rows(w_sc_raw, wi_scales, 0)
+        load_words(tab_w[0], tab_words[0], 0, T // 2)
+        load_scale_rows(nc.sync, tab2_sc, tab2_scales, 0)
+        load_words(tab_w[0], tab_words[0], T // 2, T)
+        load_scale_rows(nc.sync, w_sc_raw, wi_scales, 0)
+        load_scale_rows(nc.gpsimd, w_sc_raw, wr_scales, 8)
         we_raw[1, 0] = load_we(1, 0)
-        load_scale_rows(w_sc_raw, wr_scales, 8)
+        load_words(tab_w[1], tab_words[1], 0, T)
+        we_raw[0, 1] = load_we(0, 1)
         we_raw[1, 1] = load_we(1, 1)
-        load_words(tab_w[1], tab_words[1])
         wr_raw = [held([P, N], I32, "wr_raw_%d" % a) for a in range(2)]
         for a in range(2):
-            load_words(wr_raw[a], wr_words[a])
+            load_words(wr_raw[a], wr_words[a], 0, N)
 
         def gather_words(table, offsets, half, name):
             picked = held([P, HALF], U32, name)
@@ -100,13 +108,17 @@ def tile_list_cortical_softplus_currents_kernel(
             nc.vector.tensor_copy(picked[:], table[:].bitcast(U32).indirect(offsets[:, half * cols:(half + 1) * cols]))
             return picked
 
-        def quantise_we(a, g):
+        def round_we(a, g, on_vector):
             dealt = ring.tile([P, PACK, P, PACK], BF16, name="we_bf", bufs=2, align_bytes=64)
-            nc.scalar.activation(
-                out=dealt[:].rearrange("p t m i -> p m i t"),
-                in_=we_raw[a, g][:].rearrange("p i (m t) -> p m i t", t=PACK),
-                func=ACT.Copy, scale=-1.0,
-            )
+            dst = dealt[:].rearrange("p t m i -> p m t i")
+            src = we_raw[a, g][:].rearrange("p i (m t) -> p m t i", t=PACK)
+            if on_vector:
+                nc.vector.tensor_scalar(out=dst, in0=src, scalar1=-1.0, scalar2=None, op0=ALU.mult)
+            else:
+                nc.scalar.activation(out=dst, in_=src, func=ACT.Copy, scale=-1.0)
+            return dealt
+
+        def quantise_we(a, g, dealt):
             codes = held([P, GROUP], U32, "we_codes_%d_%d" % (a, g))
             scales = held([P, GROUP], U8, "we_scales_%d_%d" % (a, g))
             nc.vector.quantize_mx(out=codes[:].bitcast(FP8X4), scales=scales[:],
@@ -114,166 +126,185 @@ def tile_list_cortical_softplus_currents_kernel(
             return codes, scales
 
         v2_w = [gather_words(tab2_w, idx2, half, "v2_w_%d" % half) for half in range(2)]
-        we_q = {}
-        we_q[0, 0] = quantise_we(0, 0)
-
         wi_w = held([P, 2 * H], U8, "wi_w")
-        for g in range(2):
-            cols = slice(g * 2 * GROUP, (g + 1) * 2 * GROUP)
-            nc.vector.tensor_copy(
-                out=wi_w[:, cols].rearrange("p (t c i b) -> p c t i b", t=PACK, i=8, b=2),
-                in_=wi_raw[:, cols].rearrange("p (c i t b) -> p c t i b", t=PACK, i=8, b=2),
-            )
+        nc.vector.tensor_copy(
+            out=wi_w[:].bitcast(U16).rearrange("p (g t c i) -> p g c t i", g=2, t=PACK, i=8),
+            in_=wi_raw[:].bitcast(U16).rearrange("p (g c i t) -> p g c t i", g=2, t=PACK, i=8),
+        )
         neg_gain = held([P, 2 * PACK], F32, "neg_gain")
         nc.vector.tensor_scalar(out=neg_gain[:], in0=gain_sb[:].rearrange("p g t -> p (g t)"),
                                 scalar1=-1.0, scalar2=None, op0=ALU.mult)
-
         v_sc = held([P, S], U8, "v_sc")
         nc.vector.tensor_copy(v_sc[:], tab_sc[:].indirect(idx[:]))
+        we_q = {}
+        we_q[0, 0] = quantise_we(0, 0, round_we(0, 0, False))
         v2_sc = held([P, S], U8, "v2_sc")
         nc.vector.tensor_copy(v2_sc[:], tab2_sc[:].indirect(idx2[:]))
-
-        we_q[0, 1] = quantise_we(0, 1)
         v_w = {}
-        for half in range(2):
-            v_w[0, half] = gather_words(tab_w[0], idx, half, "v_w_0_%d" % half)
+        v_w[0, 0] = gather_words(tab_w[0], idx, 0, "v_w_0_0")
         w_sc = held([P, H], U8, "w_sc")
         nc.vector.tensor_copy(
             out=w_sc[:].rearrange("p (g t c i) -> p g c t i", g=2, t=PACK, i=16),
             in_=w_sc_raw[:].rearrange("p (g c i t) -> p g c t i", g=2, t=PACK, i=16),
         )
-        we_q[1, 0] = quantise_we(1, 0)
-        we_q[1, 1] = quantise_we(1, 1)
+        v_w[0, 1] = gather_words(tab_w[0], idx, 1, "v_w_0_1")
+        we_q[1, 0] = quantise_we(1, 0, round_we(1, 0, False))
         for half in range(2):
             v_w[1, half] = gather_words(tab_w[1], idx, half, "v_w_1_%d" % half)
 
-        wr_w = [held([P, N], I32, "wr_w_%d" % a) for a in range(2)]
 
-        def deal_wr(a):
+        sig = [big.tile([P, 8, HALF], F32, name="sig", tag="big", align_bytes=64) for half in range(2)]
+        lin = [big.tile([P, 8, HALF], F32, name="lin", tag="big", align_bytes=64) for half in range(2)]
+
+        def excite(bank, a, g, t, half):
+            codes, scales = we_q[a, g]
+            nc.tensor.matmul_mx(
+                out=bank[:], lhsT=codes[:, t * P:(t + 1) * P].bitcast(FP8X4),
+                lhsT_scale=scales[:, t * P:(t + 1) * P],
+                rhs=v_w[a, half][:].bitcast(FP8X4), rhs_scale=v_sc[4 + 4 * a:, half * HALF:(half + 1) * HALF],
+                start=(a == 0 and g == 0), stop=(a == 1))
+
+        def inhibit(bank, g, t, half):
+            u = g * PACK + t
+            nc.tensor.matmul_mx(
+                out=bank[:], lhsT=wi_w[:, u * 2 * P:(u + 1) * 2 * P].bitcast(FP4X4),
+                lhsT_scale=w_sc[:, u * P:(u + 1) * P],
+                rhs=v2_w[half][:].bitcast(FP8X4), rhs_scale=v2_sc[:, half * HALF:(half + 1) * HALF],
+                start=(g == 1), stop=False)
+
+        def drain(bank, g, t, half):
+            u = g * PACK + t
+            nc.scalar.activation(out=sig[half][:, u, :], in_=bank[:], func=ACT.Sigmoid, bias=zero[:])
+            nc.vector.tensor_scalar(out=lin[half][:, u, :], in0=bank[:], scalar1=neg_gain[:, u:u + 1],
+                                    scalar2=None, op0=ALU.mult)
+
+        units = [(t, half) for half in range(2) for t in range(PACK)]
+        banks = [psum.tile([P, HALF], F32, name="bank", tag="bank") for u in units]
+        for half in range(2):
+            for t in range(PACK):
+                excite(banks[half * PACK + t], 0, 0, t, half)
+            for t in range(PACK):
+                inhibit(banks[half * PACK + t], 0, t, half)
+        for bank, (t, half) in zip(banks, units):
+            excite(bank, 1, 0, t, half)
+        for t in range(PACK):
+            drain(banks[t], 0, t, 0)
+        dealt = [round_we(a, 1, a == 1) for a in range(2)]
+        for a in range(2):
+            we_q[a, 1] = quantise_we(a, 1, dealt[a])
+        for t in range(PACK):
+            drain(banks[PACK + t], 0, t, 1)
+
+        banks = [psum.tile([P, HALF], F32, name="bank", tag="bank") for u in units]
+        for t in range(PACK):
+            inhibit(banks[t], 1, t, 0)
+        for a in range(2):
+            for t in range(PACK):
+                excite(banks[t], a, 1, t, 0)
+        for t in range(PACK):
+            inhibit(banks[PACK + t], 1, t, 1)
+            for a in range(2):
+                excite(banks[PACK + t], a, 1, t, 1)
+        for bank, (t, half) in zip(banks, units):
+            drain(bank, 1, t, half)
+        wr_w = [held([P, N], I32, "wr_w_%d" % a) for a in range(2)]
+        for a in range(2):
             nc.vector.tensor_copy(
                 out=wr_w[a][:].rearrange("p (g t c i) -> p g c t i", g=2, t=PACK, i=4),
                 in_=wr_raw[a][:].rearrange("p (g c i t) -> p g c t i", g=2, t=PACK, i=4),
             )
 
+
+        tiny = keep.tile([P, 1], F32, name="tiny", tag="bias")
+        nc.gpsimd.memset(tiny[:], TINY)
         y_codes = held([P, 2, S], I32, "y_codes")
         y_scales = held([P, 2, S], U8, "y_scales")
 
-        def drives(half):
-            js = slice(half * HALF, (half + 1) * HALF)
-            banks = [psum.tile([P, HALF], F32, name="bank", tag="bank") for u in range(8)]
+        def logs(first, width):
+            half, c = divmod(first, HALF)
+            part = sig[half][:, :, c:c + width]
+            nc.scalar.activation(out=part, in_=part, func=ACT.Ln, bias=tiny[:])
 
-            def excite(a, u):
-                g, t = divmod(u, PACK)
-                codes, scales = we_q[a, g]
-                nc.tensor.matmul_mx(
-                    out=banks[u][:], lhsT=codes[:, t * P:(t + 1) * P].bitcast(FP8X4),
-                    lhsT_scale=scales[:, t * P:(t + 1) * P],
-                    rhs=v_w[a, half][:].bitcast(FP8X4), rhs_scale=v_sc[4 + 4 * a:, js],
-                    start=(a == 0), stop=(a == 1))
-
-            def inhibit(u):
-                nc.tensor.matmul_mx(
-                    out=banks[u][:], lhsT=wi_w[:, u * 2 * P:(u + 1) * 2 * P].bitcast(FP4X4),
-                    lhsT_scale=w_sc[:, u * P:(u + 1) * P],
-                    rhs=v2_w[half][:].bitcast(FP8X4), rhs_scale=v2_sc[:, js], start=False, stop=False)
-
-            if half == 0:
-                for u in range(8):
-                    excite(0, u)
-                for u in range(8):
-                    inhibit(u)
-                for u in range(8):
-                    excite(1, u)
-            else:
-                for u in range(8):
-                    excite(0, u)
-                    inhibit(u)
-                    excite(1, u)
-            sig = big.tile([P, 8, HALF], F32, name="sig", tag="big", align_bytes=64)
-            lin = big.tile([P, 8, HALF], F32, name="lin", tag="big", align_bytes=64)
-            for u in range(8):
-                nc.scalar.activation(out=sig[:, u, :], in_=banks[u][:], func=ACT.Sigmoid)
-                nc.vector.tensor_scalar(out=lin[:, u, :], in0=banks[u][:], scalar1=neg_gain[:, u:u + 1],
-                                        scalar2=None, op0=ALU.mult)
-            return sig, lin
-
-        def logs(sig, part):
-            cols = slice(part * CHUNK, (part + 1) * CHUNK)
-            nc.scalar.activation(out=sig[:, :, cols], in_=sig[:, :, cols], func=ACT.Ln, bias=tiny[:])
-
-        def rates(sig, lin, part):
-            cols = slice(part * CHUNK, (part + 1) * CHUNK)
-            flat = [ring.tile([P, PACK, CHUNK], BF16, name="h_flat", align_bytes=64) for g in range(2)]
+        def rates(first, width):
+            half, c = divmod(first, HALF)
+            cols = slice(c, c + width)
+            flat = [ring.tile([P, PACK, width], BF16, name="h_flat", align_bytes=64) for g in range(2)]
             for u in range(8):
                 g, t = divmod(u, PACK)
                 nc.vector.scalar_tensor_tensor(
-                    out=flat[g][:, t, :], in0=sig[:, u, cols], scalar=neg_gain[:, u:u + 1], in1=lin[:, u, cols],
-                    op0=ALU.mult, op1=ALU.max)
-            woven = [ring.tile([P, CHUNK, PACK], BF16, name="h_woven", align_bytes=64) for g in range(2)]
+                    out=flat[g][:, t, :], in0=sig[half][:, u, cols], scalar=neg_gain[:, u:u + 1],
+                    in1=lin[half][:, u, cols], op0=ALU.mult, op1=ALU.max)
+            woven = [ring.tile([P, width, PACK], BF16, name="h_woven", align_bytes=64) for g in range(2)]
             for g in range(2):
                 nc.vector.tensor_copy(out=woven[g][:].rearrange("p (c i) t -> p c t i", i=4),
                                       in_=flat[g][:].rearrange("p t (c i) -> p c t i", i=4))
             h_q = []
             for g in range(2):
-                codes = ring.tile([P, CHUNK], U32, name="h_codes", align_bytes=64)
-                scales = ring.tile([P, CHUNK], U8, name="h_scales", align_bytes=64)
+                codes = ring.tile([P, width], U32, name="h_codes", align_bytes=64)
+                scales = ring.tile([P, width], U8, name="h_scales", align_bytes=64)
                 nc.vector.quantize_mx(out=codes[:].bitcast(FP8X4), scales=scales[:],
                                       in_=woven[g][:].rearrange("p c t -> p (c t)"))
                 h_q.append((codes, scales))
             return h_q
 
-        def currents(h_q, chunk):
-            js = slice(chunk * CHUNK, (chunk + 1) * CHUNK)
-            ys = []
-            for g in range(2):
-                y = ring.tile([P, PACK, CHUNK], F32, name="y", align_bytes=64)
-                for pair in range(2):
-                    bank = psum.tile([P, 2, CHUNK], F32, name="bank", tag="bank")
-                    for s in range(2):
-                        u = g * PACK + 2 * pair + s
+        def currents(h_q, first, width):
+            js = slice(first, first + width)
+            ys = [ring.tile([P, PACK, width], F32, name="y", align_bytes=64) for g in range(2)]
+            woven = [ring.tile([P, width, PACK], BF16, name="y_woven", align_bytes=64) for g in range(2)]
+            for c in range(0, width, SUB):
+                cols = slice(c, c + SUB)
+                for g in range(2):
+                    bank = psum.tile([P, PACK, SUB], F32, name="bank", tag="bank")
+                    for t in range(PACK):
+                        u = g * PACK + t
                         for a in range(2):
                             codes, scales = h_q[a]
                             nc.tensor.matmul_mx(
-                                out=bank[:, s, :], lhsT=wr_w[a][:, u * P:(u + 1) * P].bitcast(FP8X4),
+                                out=bank[:, t, :], lhsT=wr_w[a][:, u * P:(u + 1) * P].bitcast(FP8X4),
                                 lhsT_scale=w_sc[8 + 4 * a:, u * P:(u + 1) * P],
-                                rhs=codes[:].bitcast(FP8X4), rhs_scale=scales[:],
+                                rhs=codes[:, cols].bitcast(FP8X4), rhs_scale=scales[:, cols],
                                 start=(a == 0), stop=(a == 1))
-                    nc.scalar.copy(out=y[:, 2 * pair:2 * pair + 2, :], in_=bank[:])
-                rows = out_0[g * GROUP:(g + 1) * GROUP, js].rearrange("(p t) j -> p t j", t=PACK)
-                nc.sync.dma_start(out=rows, in_=y[:])
-                ys.append(y)
-            woven = [ring.tile([P, CHUNK, PACK], BF16, name="y_woven", align_bytes=64) for g in range(2)]
+                    mode = SCALAR_WEAVES[(first + c) // SUB]
+                    if mode == 1:
+                        nc.scalar.copy(out=woven[g][:, cols, :], in_=bank[:].rearrange("p t c -> p c t"))
+                    if mode == 2 and g == 1:
+                        nc.vector.tensor_copy(out=woven[g][:, cols, :], in_=bank[:].rearrange("p t c -> p c t"))
+                    nc.scalar.copy(out=ys[g][:, :, cols], in_=bank[:])
+                    if mode == 2 and g == 0:
+                        nc.vector.tensor_copy(out=woven[g][:, cols, :], in_=bank[:].rearrange("p t c -> p c t"))
             for g in range(2):
-                nc.vector.tensor_copy(out=woven[g][:].rearrange("p (c i) t -> p c t i", i=4),
-                                      in_=ys[g][:].rearrange("p t (c i) -> p c t i", i=4))
+                rows = out_0[g * GROUP:(g + 1) * GROUP, js].rearrange("(p t) j -> p t j", t=PACK)
+                nc.sync.dma_start(out=rows, in_=ys[g][:])
+            for c in range(0, width, SUB):
+                cols = slice(c, c + SUB)
+                if not SCALAR_WEAVES[(first + c) // SUB]:
+                    for g in range(2):
+                        nc.vector.tensor_copy(out=woven[g][:, cols, :].rearrange("p (c i) t -> p c t i", i=4),
+                                              in_=ys[g][:, :, cols].rearrange("p t (c i) -> p c t i", i=4))
             for g in range(2):
                 nc.vector.quantize_mx(out=y_codes[:, g, js].bitcast(FP8X4), scales=y_scales[:, g, js],
                                       in_=woven[g][:].rearrange("p c t -> p (c t)"))
-            words = out_1.rearrange("g p j t -> p g (j t)").bitcast(I32)
-            nc.sync.dma_start(out=words[:, :, js], in_=y_codes[:, :, js])
 
-        def store_scales(half):
-            cols = slice(half * HALF // 4, (half + 1) * HALF // 4)
+        def store_planes(first, last):
+            words = out_1.rearrange("g p j t -> p g (j t)").bitcast(I32)
+            nc.sync.dma_start(out=words[:, :, first:last], in_=y_codes[:, :, first:last])
+
+        def store_scales():
             for q in range(4):
                 nc.sync.dma_start(
-                    out=out_2[:, 4 * q:4 * q + 4, :].bitcast(I32).rearrange("g r c -> r g c")[:, :, cols],
-                    in_=y_scales[32 * q:32 * q + 4, :, :].bitcast(I32)[:, :, cols])
+                    out=out_2[:, 4 * q:4 * q + 4, :].bitcast(I32).rearrange("g r c -> r g c"),
+                    in_=y_scales[32 * q:32 * q + 4, :, :].bitcast(I32))
 
-        sig0, lin0 = drives(0)
-        deal_wr(0)
-        deal_wr(1)
-        logs(sig0, 0)
-        logs(sig0, 1)
-        h0 = rates(sig0, lin0, 0)
-        sig1, lin1 = drives(1)
-        h1 = rates(sig0, lin0, 1)
-        currents(h0, 0)
-        logs(sig1, 0)
-        logs(sig1, 1)
-        currents(h1, 1)
-        store_scales(0)
-        h2 = rates(sig1, lin1, 0)
-        h3 = rates(sig1, lin1, 1)
-        currents(h2, 2)
-        currents(h3, 3)
-        store_scales(1)
+        firsts = [sum(WIDTHS[:n]) for n in range(len(WIDTHS))]
+        h_q = {}
+        logs(firsts[0], WIDTHS[0])
+        for n in range(len(WIDTHS) + 1):
+            if n + 1 < len(WIDTHS):
+                logs(firsts[n + 1], WIDTHS[n + 1])
+            if n < len(WIDTHS):
+                h_q[n] = rates(firsts[n], WIDTHS[n])
+
+            if n >= 1:
+                currents(h_q[n - 1], firsts[n - 1], WIDTHS[n - 1])
+                store_planes(firsts[n - 1], firsts[n - 1] + WIDTHS[n - 1])
+        store_scales()

@@ -19,8 +19,8 @@ GROUP = 512
 T, T2, S, H, N = 4096, 2048, 1024, 1024, 1024
 HALF = 512
 SUB = 128
-WIDTHS = [128,256,128,256,128,128]
-SCALAR_WEAVES = [0,0,0,1,1,1,1,2]
+WIDTHS = [128,128,256,256,128,128]
+SCALAR_WEAVES = [1,1,1,1,0,0,0,2]
 TINY = 2.0 ** -60
 FLOPS = 5368709120
 
@@ -49,12 +49,14 @@ def tile_list_cortical_softplus_currents_kernel(
 
         tab_sc = held([P, T], U8, "tab_sc")
         tab2_sc = held([P, T2], U8, "tab2_sc")
-        w_sc_raw = held([P, H], U8, "w_sc_raw")
+        wi_sc_raw = held([P, H], U8, "wi_sc_raw")
+        wr_sc_raw = held([P, N], U8, "wr_sc_raw")
         zero = keep.tile([P, 1], F32, name="zero", tag="bias")
         nc.gpsimd.memset(zero[:], 0.0)
+        nc.gpsimd.memset(tab2_sc[:].bitcast(I32), 0)
         nc.vector.memset(tab_sc[:].bitcast(I32), 0)
-        nc.vector.memset(tab2_sc[:].bitcast(I32), 0)
-        nc.gpsimd.memset(w_sc_raw[:].bitcast(I32), 0)
+        nc.vector.memset(wi_sc_raw[:].bitcast(I32), 0)
+        nc.vector.memset(wr_sc_raw[:].bitcast(I32), 0)
         warm = held([P, 1], F32, "warm")
         nc.scalar.activation(out=warm[:], in_=zero[:], func=ACT.Sigmoid)
 
@@ -70,34 +72,34 @@ def tile_list_cortical_softplus_currents_kernel(
             src = words.rearrange("p c i -> p (c i)").bitcast(I32)
             nc.sync.dma_start(out=tile[:, first:last], in_=src[:, first:last])
 
-        def load_scale_rows(queue, tile, scales, first):
-            passes = scales.shape[0]
+        def load_scale_rows(tile, plane, first):
             for q in range(4):
-                rows = tile[32 * q + first:32 * q + first + 4 * passes, :]
-                queue.dma_start(out=rows.bitcast(I32), in_=scales[:, 4 * q:4 * q + 4, :].bitcast(I32))
+                rows = tile[32 * q + first:32 * q + first + 4, :]
+                nc.sync.dma_start(out=rows.bitcast(I32), in_=plane[4 * q:4 * q + 4, :].bitcast(I32))
 
         we_raw = {}
         nc.sync.dma_start(idx2[:], offs2)
         nc.sync.dma_start(idx[:], offs)
+        load_scale_rows(tab2_sc, tab2_scales[0], 0)
         tab2_w = held([P, T2], I32, "tab2_w")
-        load_words(tab2_w, tab2_words[0], 0, T2 // 2)
-        load_words(tab2_w, tab2_words[0], T2 // 2, T2)
+        load_words(tab2_w, tab2_words[0], 0, T2)
         wi_raw = held([P, 2 * H], U8, "wi_raw")
         nc.sync.dma_start(out=wi_raw[:].bitcast(I32), in_=wi_words[0].bitcast(I32))
+        we_raw[0, 0] = load_we(0, 0)[:]
+        tab_w = [big.tile([P, T], I32, name="tab_w", tag="big", align_bytes=64) for a in range(2)]
+        for a in range(2):
+            load_scale_rows(tab_sc, tab_scales[a], 4 + 4 * a)
+            load_words(tab_w[0], tab_words[0], a * T // 2, (a + 1) * T // 2)
+        load_scale_rows(wi_sc_raw, wi_scales[0], 0)
+        we_raw[1, 0] = load_we(1, 0)[:]
         gain_sb = held([P, 2, PACK], F32, "gain_sb")
         nc.sync.dma_start(out=gain_sb[:], in_=gain.rearrange("(g p t) -> p g t", g=2, t=PACK))
-        we_raw[0, 0] = load_we(0, 0, 2)
-        load_scale_rows(nc.sync, tab_sc, tab_scales, 4)
-        tab_w = [big.tile([P, T], I32, name="tab_w", tag="big", align_bytes=64) for a in range(2)]
-        load_words(tab_w[0], tab_words[0], 0, T // 2)
-        load_scale_rows(nc.sync, tab2_sc, tab2_scales, 0)
-        load_words(tab_w[0], tab_words[0], T // 2, T)
-        load_scale_rows(nc.sync, w_sc_raw, wi_scales, 0)
-        load_scale_rows(nc.gpsimd, w_sc_raw, wr_scales, 8)
-        we_raw[1, 0] = load_we(1, 0)
+        we_raw[0, 1] = load_we(0, 1)[:]
         load_words(tab_w[1], tab_words[1], 0, T)
-        we_raw[0, 1] = load_we(0, 1)
-        we_raw[1, 1] = load_we(1, 1)
+        we_raw[1, 1] = load_we(1, 1)[:]
+        for q in range(4):
+            nc.sync.dma_start(out=wr_sc_raw[32 * q + 8:32 * q + 16, :].bitcast(I32),
+                              in_=wr_scales[:, 4 * q:4 * q + 4, :].bitcast(I32))
         wr_raw = [held([P, N], I32, "wr_raw_%d" % a) for a in range(2)]
         for a in range(2):
             load_words(wr_raw[a], wr_words[a], 0, N)
@@ -109,11 +111,13 @@ def tile_list_cortical_softplus_currents_kernel(
             return picked
 
         def round_we(a, g, on_vector):
-            dealt = ring.tile([P, PACK, P, PACK], BF16, name="we_bf", bufs=2, align_bytes=64)
+            dealt = ring.tile([P, PACK, P, PACK], BF16, name="we_bf", bufs=3, align_bytes=64)
             dst = dealt[:].rearrange("p t m i -> p m t i")
-            src = we_raw[a, g][:].rearrange("p i (m t) -> p m t i", t=PACK)
-            if on_vector:
+            src = we_raw[a, g].rearrange("p i (m t) -> p m t i", t=PACK)
+            if on_vector == 1:
                 nc.vector.tensor_scalar(out=dst, in0=src, scalar1=-1.0, scalar2=None, op0=ALU.mult)
+            elif on_vector == 2:
+                nc.gpsimd.tensor_scalar(out=dst, in0=src, scalar1=-1.0, scalar2=0.0, op0=ALU.mult, op1=ALU.add)
             else:
                 nc.scalar.activation(out=dst, in_=src, func=ACT.Copy, scale=-1.0)
             return dealt
@@ -125,33 +129,37 @@ def tile_list_cortical_softplus_currents_kernel(
                                   in_=dealt[:].rearrange("p t m i -> p (t m i)"))
             return codes, scales
 
+        def deal_scales(raw, name):
+            dealt = held([P, H], U8, name)
+            nc.vector.tensor_copy(
+                out=dealt[:].rearrange("p (g t c i) -> p g c t i", g=2, t=PACK, i=16),
+                in_=raw[:].rearrange("p (g c i t) -> p g c t i", g=2, t=PACK, i=16),
+            )
+            return dealt
+
+        v2_sc = held([P, S], U8, "v2_sc")
+        nc.vector.tensor_copy(v2_sc[:], tab2_sc[:].indirect(idx2[:]))
         v2_w = [gather_words(tab2_w, idx2, half, "v2_w_%d" % half) for half in range(2)]
         wi_w = held([P, 2 * H], U8, "wi_w")
         nc.vector.tensor_copy(
             out=wi_w[:].bitcast(U16).rearrange("p (g t c i) -> p g c t i", g=2, t=PACK, i=8),
             in_=wi_raw[:].bitcast(U16).rearrange("p (g c i t) -> p g c t i", g=2, t=PACK, i=8),
         )
+        we_q = {}
+        we_q[0, 0] = quantise_we(0, 0, round_we(0, 0, 0))
+        v_sc = held([P, S], U8, "v_sc")
+        nc.vector.tensor_copy(v_sc[:], tab_sc[:].indirect(idx[:]))
+        v_w = {}
+        for half in range(2):
+            v_w[0, half] = gather_words(tab_w[0], idx, half, "v_w_0_%d" % half)
+        wi_sc = deal_scales(wi_sc_raw, "wi_sc")
+        we_q[1, 0] = quantise_we(1, 0, round_we(1, 0, 0))
         neg_gain = held([P, 2 * PACK], F32, "neg_gain")
         nc.vector.tensor_scalar(out=neg_gain[:], in0=gain_sb[:].rearrange("p g t -> p (g t)"),
                                 scalar1=-1.0, scalar2=None, op0=ALU.mult)
-        v_sc = held([P, S], U8, "v_sc")
-        nc.vector.tensor_copy(v_sc[:], tab_sc[:].indirect(idx[:]))
-        we_q = {}
-        we_q[0, 0] = quantise_we(0, 0, round_we(0, 0, False))
-        v2_sc = held([P, S], U8, "v2_sc")
-        nc.vector.tensor_copy(v2_sc[:], tab2_sc[:].indirect(idx2[:]))
-        v_w = {}
-        v_w[0, 0] = gather_words(tab_w[0], idx, 0, "v_w_0_0")
-        w_sc = held([P, H], U8, "w_sc")
-        nc.vector.tensor_copy(
-            out=w_sc[:].rearrange("p (g t c i) -> p g c t i", g=2, t=PACK, i=16),
-            in_=w_sc_raw[:].rearrange("p (g c i t) -> p g c t i", g=2, t=PACK, i=16),
-        )
-        v_w[0, 1] = gather_words(tab_w[0], idx, 1, "v_w_0_1")
-        we_q[1, 0] = quantise_we(1, 0, round_we(1, 0, False))
+        we_q[0, 1] = quantise_we(0, 1, round_we(0, 1, 0))
         for half in range(2):
             v_w[1, half] = gather_words(tab_w[1], idx, half, "v_w_1_%d" % half)
-
 
         sig = [big.tile([P, 8, HALF], F32, name="sig", tag="big", align_bytes=64) for half in range(2)]
         lin = [big.tile([P, 8, HALF], F32, name="lin", tag="big", align_bytes=64) for half in range(2)]
@@ -162,51 +170,52 @@ def tile_list_cortical_softplus_currents_kernel(
                 out=bank[:], lhsT=codes[:, t * P:(t + 1) * P].bitcast(FP8X4),
                 lhsT_scale=scales[:, t * P:(t + 1) * P],
                 rhs=v_w[a, half][:].bitcast(FP8X4), rhs_scale=v_sc[4 + 4 * a:, half * HALF:(half + 1) * HALF],
-                start=(a == 0 and g == 0), stop=(a == 1))
+                start=(a == 0), stop=(a == 1))
 
         def inhibit(bank, g, t, half):
             u = g * PACK + t
             nc.tensor.matmul_mx(
                 out=bank[:], lhsT=wi_w[:, u * 2 * P:(u + 1) * 2 * P].bitcast(FP4X4),
-                lhsT_scale=w_sc[:, u * P:(u + 1) * P],
+                lhsT_scale=wi_sc[:, u * P:(u + 1) * P],
                 rhs=v2_w[half][:].bitcast(FP8X4), rhs_scale=v2_sc[:, half * HALF:(half + 1) * HALF],
-                start=(g == 1), stop=False)
+                start=False, stop=False)
 
         def drain(bank, g, t, half):
             u = g * PACK + t
             nc.scalar.activation(out=sig[half][:, u, :], in_=bank[:], func=ACT.Sigmoid, bias=zero[:])
-            nc.vector.tensor_scalar(out=lin[half][:, u, :], in0=bank[:], scalar1=neg_gain[:, u:u + 1],
-                                    scalar2=None, op0=ALU.mult)
+            if g == 0 and half == 1 and t >= PACK - 2:
+                nc.scalar.activation(out=lin[half][:, u, :], in_=bank[:], func=ACT.Copy, scale=neg_gain[:, u:u + 1])
+            else:
+                nc.vector.tensor_scalar(out=lin[half][:, u, :], in0=bank[:], scalar1=neg_gain[:, u:u + 1],
+                                        scalar2=None, op0=ALU.mult)
 
         units = [(t, half) for half in range(2) for t in range(PACK)]
         banks = [psum.tile([P, HALF], F32, name="bank", tag="bank") for u in units]
-        for half in range(2):
-            for t in range(PACK):
-                excite(banks[half * PACK + t], 0, 0, t, half)
-            for t in range(PACK):
-                inhibit(banks[half * PACK + t], 0, t, half)
+        for bank, (t, half) in zip(banks, units):
+            excite(bank, 0, 0, t, half)
+        for bank, (t, half) in zip(banks, units):
+            inhibit(bank, 0, t, half)
         for bank, (t, half) in zip(banks, units):
             excite(bank, 1, 0, t, half)
         for t in range(PACK):
             drain(banks[t], 0, t, 0)
-        dealt = [round_we(a, 1, a == 1) for a in range(2)]
-        for a in range(2):
-            we_q[a, 1] = quantise_we(a, 1, dealt[a])
+        we_q[1, 1] = quantise_we(1, 1, round_we(1, 1, 2))
         for t in range(PACK):
             drain(banks[PACK + t], 0, t, 1)
 
         banks = [psum.tile([P, HALF], F32, name="bank", tag="bank") for u in units]
         for t in range(PACK):
+            excite(banks[t], 0, 1, t, 0)
             inhibit(banks[t], 1, t, 0)
-        for a in range(2):
-            for t in range(PACK):
-                excite(banks[t], a, 1, t, 0)
         for t in range(PACK):
+            excite(banks[t], 1, 1, t, 0)
+            excite(banks[PACK + t], 0, 1, t, 1)
             inhibit(banks[PACK + t], 1, t, 1)
-            for a in range(2):
-                excite(banks[PACK + t], a, 1, t, 1)
+        for t in range(PACK):
+            excite(banks[PACK + t], 1, 1, t, 1)
         for bank, (t, half) in zip(banks, units):
             drain(bank, 1, t, half)
+        wr_sc = deal_scales(wr_sc_raw, "wr_sc")
         wr_w = [held([P, N], I32, "wr_w_%d" % a) for a in range(2)]
         for a in range(2):
             nc.vector.tensor_copy(
@@ -261,7 +270,7 @@ def tile_list_cortical_softplus_currents_kernel(
                             codes, scales = h_q[a]
                             nc.tensor.matmul_mx(
                                 out=bank[:, t, :], lhsT=wr_w[a][:, u * P:(u + 1) * P].bitcast(FP8X4),
-                                lhsT_scale=w_sc[8 + 4 * a:, u * P:(u + 1) * P],
+                                lhsT_scale=wr_sc[8 + 4 * a:, u * P:(u + 1) * P],
                                 rhs=codes[:, cols].bitcast(FP8X4), rhs_scale=scales[:, cols],
                                 start=(a == 0), stop=(a == 1))
                     mode = SCALAR_WEAVES[(first + c) // SUB]

@@ -49,14 +49,12 @@ def tile_list_cortical_softplus_currents_kernel(
 
         tab_sc = held([P, T], U8, "tab_sc")
         tab2_sc = held([P, T2], U8, "tab2_sc")
-        wi_sc_raw = held([P, H], U8, "wi_sc_raw")
-        wr_sc_raw = held([P, N], U8, "wr_sc_raw")
+        w_sc_raw = held([P, H], U8, "w_sc_raw")
         zero = keep.tile([P, 1], F32, name="zero", tag="bias")
         nc.gpsimd.memset(zero[:], 0.0)
-        nc.gpsimd.memset(tab2_sc[:].bitcast(I32), 0)
-        nc.vector.memset(tab_sc[:].bitcast(I32), 0)
-        nc.vector.memset(wi_sc_raw[:].bitcast(I32), 0)
-        nc.vector.memset(wr_sc_raw[:].bitcast(I32), 0)
+        nc.gpsimd.memset(tab_sc[:].bitcast(I32), 0)
+        nc.vector.memset(tab2_sc[:].bitcast(I32), 0)
+        nc.vector.memset(w_sc_raw[:].bitcast(I32), 0)
         warm = held([P, 1], F32, "warm")
         nc.scalar.activation(out=warm[:], in_=zero[:], func=ACT.Sigmoid)
 
@@ -72,34 +70,35 @@ def tile_list_cortical_softplus_currents_kernel(
             src = words.rearrange("p c i -> p (c i)").bitcast(I32)
             nc.sync.dma_start(out=tile[:, first:last], in_=src[:, first:last])
 
-        def load_scale_rows(tile, plane, first):
+        def load_scale_rows(tile, scales, first):
+            passes = scales.shape[0]
             for q in range(4):
-                rows = tile[32 * q + first:32 * q + first + 4, :]
-                nc.sync.dma_start(out=rows.bitcast(I32), in_=plane[4 * q:4 * q + 4, :].bitcast(I32))
+                rows = tile[32 * q + first:32 * q + first + 4 * passes, :]
+                nc.gpsimd.dma_start(out=rows.bitcast(I32), in_=scales[:, 4 * q:4 * q + 4, :].bitcast(I32))
+
+        load_scale_rows(tab_sc, tab_scales, 4)
+        load_scale_rows(w_sc_raw, wr_scales, 8)
 
         we_raw = {}
         nc.sync.dma_start(idx2[:], offs2)
         nc.sync.dma_start(idx[:], offs)
-        load_scale_rows(tab2_sc, tab2_scales[0], 0)
+        for r in range(4):
+            nc.sync.dma_start(out=tab2_sc[r:P:32, :].bitcast(I32), in_=tab2_scales[0, r:16:4, :].bitcast(I32))
         tab2_w = held([P, T2], I32, "tab2_w")
         load_words(tab2_w, tab2_words[0], 0, T2)
         wi_raw = held([P, 2 * H], U8, "wi_raw")
         nc.sync.dma_start(out=wi_raw[:].bitcast(I32), in_=wi_words[0].bitcast(I32))
         we_raw[0, 0] = load_we(0, 0)[:]
         tab_w = [big.tile([P, T], I32, name="tab_w", tag="big", align_bytes=64) for a in range(2)]
-        for a in range(2):
-            load_scale_rows(tab_sc, tab_scales[a], 4 + 4 * a)
-            load_words(tab_w[0], tab_words[0], a * T // 2, (a + 1) * T // 2)
-        load_scale_rows(wi_sc_raw, wi_scales[0], 0)
+        load_words(tab_w[0], tab_words[0], 0, T)
+        for r in range(4):
+            nc.sync.dma_start(out=w_sc_raw[r:P:32, :].bitcast(I32), in_=wi_scales[0, r:16:4, :].bitcast(I32))
         we_raw[1, 0] = load_we(1, 0)[:]
         gain_sb = held([P, 2, PACK], F32, "gain_sb")
         nc.sync.dma_start(out=gain_sb[:], in_=gain.rearrange("(g p t) -> p g t", g=2, t=PACK))
         we_raw[0, 1] = load_we(0, 1)[:]
         load_words(tab_w[1], tab_words[1], 0, T)
         we_raw[1, 1] = load_we(1, 1)[:]
-        for q in range(4):
-            nc.sync.dma_start(out=wr_sc_raw[32 * q + 8:32 * q + 16, :].bitcast(I32),
-                              in_=wr_scales[:, 4 * q:4 * q + 4, :].bitcast(I32))
         wr_raw = [held([P, N], I32, "wr_raw_%d" % a) for a in range(2)]
         for a in range(2):
             load_words(wr_raw[a], wr_words[a], 0, N)
@@ -152,7 +151,7 @@ def tile_list_cortical_softplus_currents_kernel(
         v_w = {}
         for half in range(2):
             v_w[0, half] = gather_words(tab_w[0], idx, half, "v_w_0_%d" % half)
-        wi_sc = deal_scales(wi_sc_raw, "wi_sc")
+        w_sc = deal_scales(w_sc_raw, "w_sc")
         we_q[1, 0] = quantise_we(1, 0, round_we(1, 0, 0))
         neg_gain = held([P, 2 * PACK], F32, "neg_gain")
         nc.vector.tensor_scalar(out=neg_gain[:], in0=gain_sb[:].rearrange("p g t -> p (g t)"),
@@ -176,7 +175,7 @@ def tile_list_cortical_softplus_currents_kernel(
             u = g * PACK + t
             nc.tensor.matmul_mx(
                 out=bank[:], lhsT=wi_w[:, u * 2 * P:(u + 1) * 2 * P].bitcast(FP4X4),
-                lhsT_scale=wi_sc[:, u * P:(u + 1) * P],
+                lhsT_scale=w_sc[:, u * P:(u + 1) * P],
                 rhs=v2_w[half][:].bitcast(FP8X4), rhs_scale=v2_sc[:, half * HALF:(half + 1) * HALF],
                 start=False, stop=False)
 
@@ -215,7 +214,6 @@ def tile_list_cortical_softplus_currents_kernel(
             excite(banks[PACK + t], 1, 1, t, 1)
         for bank, (t, half) in zip(banks, units):
             drain(bank, 1, t, half)
-        wr_sc = deal_scales(wr_sc_raw, "wr_sc")
         wr_w = [held([P, N], I32, "wr_w_%d" % a) for a in range(2)]
         for a in range(2):
             nc.vector.tensor_copy(
@@ -270,7 +268,7 @@ def tile_list_cortical_softplus_currents_kernel(
                             codes, scales = h_q[a]
                             nc.tensor.matmul_mx(
                                 out=bank[:, t, :], lhsT=wr_w[a][:, u * P:(u + 1) * P].bitcast(FP8X4),
-                                lhsT_scale=wr_sc[8 + 4 * a:, u * P:(u + 1) * P],
+                                lhsT_scale=w_sc[8 + 4 * a:, u * P:(u + 1) * P],
                                 rhs=codes[:, cols].bitcast(FP8X4), rhs_scale=scales[:, cols],
                                 start=(a == 0), stop=(a == 1))
                     mode = SCALAR_WEAVES[(first + c) // SUB]
@@ -298,11 +296,12 @@ def tile_list_cortical_softplus_currents_kernel(
             words = out_1.rearrange("g p j t -> p g (j t)").bitcast(I32)
             nc.sync.dma_start(out=words[:, :, first:last], in_=y_codes[:, :, first:last])
 
-        def store_scales():
-            for q in range(4):
+        def store_scales(first, last):
+            cols = slice(first // 4, last // 4)
+            for r in range(4):
                 nc.sync.dma_start(
-                    out=out_2[:, 4 * q:4 * q + 4, :].bitcast(I32).rearrange("g r c -> r g c"),
-                    in_=y_scales[32 * q:32 * q + 4, :, :].bitcast(I32))
+                    out=out_2[:, r:16:4, :].bitcast(I32).rearrange("g q c -> q g c")[:, :, cols],
+                    in_=y_scales[r:P:32, :, :].bitcast(I32)[:, :, cols])
 
         firsts = [sum(WIDTHS[:n]) for n in range(len(WIDTHS))]
         h_q = {}
@@ -316,4 +315,6 @@ def tile_list_cortical_softplus_currents_kernel(
             if n >= 1:
                 currents(h_q[n - 1], firsts[n - 1], WIDTHS[n - 1])
                 store_planes(firsts[n - 1], firsts[n - 1] + WIDTHS[n - 1])
-        store_scales()
+            if n == len(WIDTHS) - 2:
+                store_scales(0, firsts[n])
+        store_scales(firsts[-2], S)

@@ -15,13 +15,16 @@ ALU = mybir.AluOpType
 
 P = 128
 PACK = 4
-GROUP = 512
+GROUP = P * PACK
 T, T2, S, H, N = 4096, 2048, 1024, 1024, 1024
 HALF = 512
 SUB = 128
-WIDTHS = [128,128,256,256,128,128]
-SCALAR_WEAVES = [1,1,1,1,0,0,0,2]
-TINY = 2.0 ** -60
+CHUNKS = (128, 128, 256, 256, 128, 128)
+SCALAR_SUBS = 5
+SCALAR_LINEAR = 2
+TAB_FIRST = 4
+WR_FIRST = 8
+FLOOR = 2.0 ** -60
 FLOPS = 5368709120
 
 
@@ -40,65 +43,64 @@ def tile_list_cortical_softplus_currents_kernel(
         def held(shape, dtype, name):
             return keep.tile(shape, dtype, name=name, align_bytes=64)
 
-        def clock(ap, name):
-            c = held([P, 1], ap.dtype, name)
-            nc.gpsimd.tensor_copy(out=c[:], in_=ap)
-
         idx = lists.tile([P, S // 16], U16, name="idx")
         idx2 = lists.tile([P, S // 16], U16, name="idx2")
 
         tab_sc = held([P, T], U8, "tab_sc")
         tab2_sc = held([P, T2], U8, "tab2_sc")
-        w_sc_raw = held([P, H], U8, "w_sc_raw")
+        wi_sc_raw = held([P, H], U8, "wi_sc_raw")
+        wr_sc_raw = held([P, N], U8, "wr_sc_raw")
         zero = keep.tile([P, 1], F32, name="zero", tag="bias")
         nc.gpsimd.memset(zero[:], 0.0)
         nc.gpsimd.memset(tab_sc[:].bitcast(I32), 0)
         nc.vector.memset(tab2_sc[:].bitcast(I32), 0)
-        nc.vector.memset(w_sc_raw[:].bitcast(I32), 0)
+        nc.vector.memset(wi_sc_raw[:].bitcast(I32), 0)
+        nc.vector.memset(wr_sc_raw[:].bitcast(I32), 0)
         warm = held([P, 1], F32, "warm")
         nc.scalar.activation(out=warm[:], in_=zero[:], func=ACT.Sigmoid)
 
-        def load_we(a, g, pieces=1):
+        def load_we(a, g):
             raw = held([P, PACK, GROUP], F32, "we_raw_%d_%d" % (a, g))
-            rows = we[a * GROUP:(a + 1) * GROUP, g * GROUP:(g + 1) * GROUP].rearrange("(p i) c -> p i c", i=PACK)
-            step = PACK // pieces
-            for i in range(0, PACK, step):
-                nc.sync.dma_start(out=raw[:, i:i + step, :], in_=rows[:, i:i + step, :])
+            rows = we[a * GROUP:(a + 1) * GROUP, g * GROUP:(g + 1) * GROUP]
+            nc.sync.dma_start(out=raw[:], in_=rows.rearrange("(p i) c -> p i c", i=PACK))
             return raw
 
         def load_words(tile, words, first, last):
             src = words.rearrange("p c i -> p (c i)").bitcast(I32)
             nc.sync.dma_start(out=tile[:, first:last], in_=src[:, first:last])
 
-        def load_scale_rows(tile, scales, first):
-            passes = scales.shape[0]
-            for q in range(4):
-                rows = tile[32 * q + first:32 * q + first + 4 * passes, :]
-                nc.gpsimd.dma_start(out=rows.bitcast(I32), in_=scales[:, 4 * q:4 * q + 4, :].bitcast(I32))
+        def load_plane_pair(tile, scales, first, quadrants):
+            for q in quadrants:
+                rows = tile[32 * q + first:32 * q + first + 8, :]
+                nc.sync.dma_start(out=rows.bitcast(I32), in_=scales[:, 4 * q:4 * q + 4, :].bitcast(I32))
 
-        load_scale_rows(tab_sc, tab_scales, 4)
-        load_scale_rows(w_sc_raw, wr_scales, 8)
+        def load_plane(tile, scales):
+            for r in range(4):
+                nc.sync.dma_start(out=tile[r:P:32, :].bitcast(I32), in_=scales[0, r:16:4, :].bitcast(I32))
 
         we_raw = {}
+        tab2_w = held([P, T2], I32, "tab2_w")
+        load_words(tab2_w, tab2_words[0], 0, T2 // 2)
+        load_words(tab2_w, tab2_words[0], T2 // 2, T2)
         nc.sync.dma_start(idx2[:], offs2)
         nc.sync.dma_start(idx[:], offs)
-        for r in range(4):
-            nc.sync.dma_start(out=tab2_sc[r:P:32, :].bitcast(I32), in_=tab2_scales[0, r:16:4, :].bitcast(I32))
-        tab2_w = held([P, T2], I32, "tab2_w")
-        load_words(tab2_w, tab2_words[0], 0, T2)
         wi_raw = held([P, 2 * H], U8, "wi_raw")
         nc.sync.dma_start(out=wi_raw[:].bitcast(I32), in_=wi_words[0].bitcast(I32))
-        we_raw[0, 0] = load_we(0, 0)[:]
         tab_w = [big.tile([P, T], I32, name="tab_w", tag="big", align_bytes=64) for a in range(2)]
-        load_words(tab_w[0], tab_words[0], 0, T)
-        for r in range(4):
-            nc.sync.dma_start(out=w_sc_raw[r:P:32, :].bitcast(I32), in_=wi_scales[0, r:16:4, :].bitcast(I32))
-        we_raw[1, 0] = load_we(1, 0)[:]
+        load_words(tab_w[0], tab_words[0], 0, T // 2)
+        load_plane(tab2_sc, tab2_scales)
+        load_plane_pair(tab_sc, tab_scales, TAB_FIRST, (0, 1))
+        load_words(tab_w[0], tab_words[0], T // 2, T)
+        load_plane_pair(tab_sc, tab_scales, TAB_FIRST, (2, 3))
+        we_raw[0, 0] = load_we(0, 0)
+        load_plane(wi_sc_raw, wi_scales)
+        we_raw[1, 0] = load_we(1, 0)
         gain_sb = held([P, 2, PACK], F32, "gain_sb")
         nc.sync.dma_start(out=gain_sb[:], in_=gain.rearrange("(g p t) -> p g t", g=2, t=PACK))
-        we_raw[0, 1] = load_we(0, 1)[:]
+        we_raw[0, 1] = load_we(0, 1)
         load_words(tab_w[1], tab_words[1], 0, T)
-        we_raw[1, 1] = load_we(1, 1)[:]
+        we_raw[1, 1] = load_we(1, 1)
+        load_plane_pair(wr_sc_raw, wr_scales, WR_FIRST, range(4))
         wr_raw = [held([P, N], I32, "wr_raw_%d" % a) for a in range(2)]
         for a in range(2):
             load_words(wr_raw[a], wr_words[a], 0, N)
@@ -109,16 +111,26 @@ def tile_list_cortical_softplus_currents_kernel(
             nc.vector.tensor_copy(picked[:], table[:].bitcast(U32).indirect(offsets[:, half * cols:(half + 1) * cols]))
             return picked
 
-        def round_we(a, g, on_vector):
+        def deal(dealt, raw, run):
+            nc.vector.tensor_copy(
+                out=dealt.rearrange("p (g t c i) -> p g c t i", g=2, t=PACK, i=run),
+                in_=raw.rearrange("p (g c i t) -> p g c t i", g=2, t=PACK, i=run),
+            )
+
+        def we_views(a, g):
             dealt = ring.tile([P, PACK, P, PACK], BF16, name="we_bf", bufs=3, align_bytes=64)
             dst = dealt[:].rearrange("p t m i -> p m t i")
-            src = we_raw[a, g].rearrange("p i (m t) -> p m t i", t=PACK)
-            if on_vector == 1:
-                nc.vector.tensor_scalar(out=dst, in0=src, scalar1=-1.0, scalar2=None, op0=ALU.mult)
-            elif on_vector == 2:
-                nc.gpsimd.tensor_scalar(out=dst, in0=src, scalar1=-1.0, scalar2=0.0, op0=ALU.mult, op1=ALU.add)
-            else:
-                nc.scalar.activation(out=dst, in_=src, func=ACT.Copy, scale=-1.0)
+            src = we_raw[a, g][:].rearrange("p i (m t) -> p m t i", t=PACK)
+            return dealt, dst, src
+
+        def round_we_on_scalar(a, g):
+            dealt, dst, src = we_views(a, g)
+            nc.scalar.activation(out=dst, in_=src, func=ACT.Copy, scale=-1.0)
+            return dealt
+
+        def round_we_on_gpsimd(a, g):
+            dealt, dst, src = we_views(a, g)
+            nc.gpsimd.tensor_scalar(out=dst, in0=src, scalar1=-1.0, scalar2=0.0, op0=ALU.mult, op1=ALU.add)
             return dealt
 
         def quantise_we(a, g, dealt):
@@ -128,68 +140,59 @@ def tile_list_cortical_softplus_currents_kernel(
                                   in_=dealt[:].rearrange("p t m i -> p (t m i)"))
             return codes, scales
 
-        def deal_scales(raw, name):
-            dealt = held([P, H], U8, name)
-            nc.vector.tensor_copy(
-                out=dealt[:].rearrange("p (g t c i) -> p g c t i", g=2, t=PACK, i=16),
-                in_=raw[:].rearrange("p (g c i t) -> p g c t i", g=2, t=PACK, i=16),
-            )
-            return dealt
-
-        v2_sc = held([P, S], U8, "v2_sc")
-        nc.vector.tensor_copy(v2_sc[:], tab2_sc[:].indirect(idx2[:]))
         v2_w = [gather_words(tab2_w, idx2, half, "v2_w_%d" % half) for half in range(2)]
         wi_w = held([P, 2 * H], U8, "wi_w")
-        nc.vector.tensor_copy(
-            out=wi_w[:].bitcast(U16).rearrange("p (g t c i) -> p g c t i", g=2, t=PACK, i=8),
-            in_=wi_raw[:].bitcast(U16).rearrange("p (g c i t) -> p g c t i", g=2, t=PACK, i=8),
-        )
-        we_q = {}
-        we_q[0, 0] = quantise_we(0, 0, round_we(0, 0, 0))
-        v_sc = held([P, S], U8, "v_sc")
-        nc.vector.tensor_copy(v_sc[:], tab_sc[:].indirect(idx[:]))
+        deal(wi_w[:].bitcast(U16), wi_raw[:].bitcast(U16), 8)
+        v2_sc = held([P, S], U8, "v2_sc")
+        nc.vector.tensor_copy(v2_sc[:], tab2_sc[:].indirect(idx2[:]))
         v_w = {}
         for half in range(2):
             v_w[0, half] = gather_words(tab_w[0], idx, half, "v_w_0_%d" % half)
-        w_sc = deal_scales(w_sc_raw, "w_sc")
-        we_q[1, 0] = quantise_we(1, 0, round_we(1, 0, 0))
+        v_sc = held([P, S], U8, "v_sc")
+        nc.vector.tensor_copy(v_sc[:], tab_sc[:].indirect(idx[:]))
+        we_q = {}
+        we_q[0, 0] = quantise_we(0, 0, round_we_on_scalar(0, 0))
+        wi_sc = held([P, H], U8, "wi_sc")
+        deal(wi_sc[:], wi_sc_raw[:], 16)
+        we_q[1, 0] = quantise_we(1, 0, round_we_on_scalar(1, 0))
         neg_gain = held([P, 2 * PACK], F32, "neg_gain")
         nc.vector.tensor_scalar(out=neg_gain[:], in0=gain_sb[:].rearrange("p g t -> p (g t)"),
                                 scalar1=-1.0, scalar2=None, op0=ALU.mult)
-        we_q[0, 1] = quantise_we(0, 1, round_we(0, 1, 0))
+        we_q[0, 1] = quantise_we(0, 1, round_we_on_scalar(0, 1))
         for half in range(2):
             v_w[1, half] = gather_words(tab_w[1], idx, half, "v_w_1_%d" % half)
 
-        sig = [big.tile([P, 8, HALF], F32, name="sig", tag="big", align_bytes=64) for half in range(2)]
-        lin = [big.tile([P, 8, HALF], F32, name="lin", tag="big", align_bytes=64) for half in range(2)]
+        sig = [big.tile([P, 2 * PACK, HALF], F32, name="sig", tag="big", align_bytes=64) for half in range(2)]
+        lin = [big.tile([P, 2 * PACK, HALF], F32, name="lin", tag="big", align_bytes=64) for half in range(2)]
 
         def excite(bank, a, g, t, half):
             codes, scales = we_q[a, g]
             nc.tensor.matmul_mx(
                 out=bank[:], lhsT=codes[:, t * P:(t + 1) * P].bitcast(FP8X4),
                 lhsT_scale=scales[:, t * P:(t + 1) * P],
-                rhs=v_w[a, half][:].bitcast(FP8X4), rhs_scale=v_sc[4 + 4 * a:, half * HALF:(half + 1) * HALF],
+                rhs=v_w[a, half][:].bitcast(FP8X4),
+                rhs_scale=v_sc[TAB_FIRST + 4 * a:, half * HALF:(half + 1) * HALF],
                 start=(a == 0), stop=(a == 1))
 
         def inhibit(bank, g, t, half):
             u = g * PACK + t
             nc.tensor.matmul_mx(
                 out=bank[:], lhsT=wi_w[:, u * 2 * P:(u + 1) * 2 * P].bitcast(FP4X4),
-                lhsT_scale=w_sc[:, u * P:(u + 1) * P],
+                lhsT_scale=wi_sc[:, u * P:(u + 1) * P],
                 rhs=v2_w[half][:].bitcast(FP8X4), rhs_scale=v2_sc[:, half * HALF:(half + 1) * HALF],
                 start=False, stop=False)
 
         def drain(bank, g, t, half):
             u = g * PACK + t
             nc.scalar.activation(out=sig[half][:, u, :], in_=bank[:], func=ACT.Sigmoid, bias=zero[:])
-            if g == 0 and half == 1 and t >= PACK - 2:
+            if g == 0 and half == 1 and t >= PACK - SCALAR_LINEAR:
                 nc.scalar.activation(out=lin[half][:, u, :], in_=bank[:], func=ACT.Copy, scale=neg_gain[:, u:u + 1])
             else:
                 nc.vector.tensor_scalar(out=lin[half][:, u, :], in0=bank[:], scalar1=neg_gain[:, u:u + 1],
                                         scalar2=None, op0=ALU.mult)
 
         units = [(t, half) for half in range(2) for t in range(PACK)]
-        banks = [psum.tile([P, HALF], F32, name="bank", tag="bank") for u in units]
+        banks = [psum.tile([P, HALF], F32, name="bank", tag="bank") for unit in units]
         for bank, (t, half) in zip(banks, units):
             excite(bank, 0, 0, t, half)
         for bank, (t, half) in zip(banks, units):
@@ -198,11 +201,11 @@ def tile_list_cortical_softplus_currents_kernel(
             excite(bank, 1, 0, t, half)
         for t in range(PACK):
             drain(banks[t], 0, t, 0)
-        we_q[1, 1] = quantise_we(1, 1, round_we(1, 1, 2))
+        we_q[1, 1] = quantise_we(1, 1, round_we_on_gpsimd(1, 1))
         for t in range(PACK):
             drain(banks[PACK + t], 0, t, 1)
 
-        banks = [psum.tile([P, HALF], F32, name="bank", tag="bank") for u in units]
+        banks = [psum.tile([P, HALF], F32, name="bank", tag="bank") for unit in units]
         for t in range(PACK):
             excite(banks[t], 0, 1, t, 0)
             inhibit(banks[t], 1, t, 0)
@@ -214,37 +217,39 @@ def tile_list_cortical_softplus_currents_kernel(
             excite(banks[PACK + t], 1, 1, t, 1)
         for bank, (t, half) in zip(banks, units):
             drain(bank, 1, t, half)
+
+        wr_sc = held([P, N], U8, "wr_sc")
+        deal(wr_sc[:], wr_sc_raw[:], 16)
         wr_w = [held([P, N], I32, "wr_w_%d" % a) for a in range(2)]
         for a in range(2):
-            nc.vector.tensor_copy(
-                out=wr_w[a][:].rearrange("p (g t c i) -> p g c t i", g=2, t=PACK, i=4),
-                in_=wr_raw[a][:].rearrange("p (g c i t) -> p g c t i", g=2, t=PACK, i=4),
-            )
+            deal(wr_w[a][:], wr_raw[a][:], 4)
 
-
-        tiny = keep.tile([P, 1], F32, name="tiny", tag="bias")
-        nc.gpsimd.memset(tiny[:], TINY)
+        floor = keep.tile([P, 1], F32, name="floor", tag="bias")
+        nc.gpsimd.memset(floor[:], FLOOR)
         y_codes = held([P, 2, S], I32, "y_codes")
         y_scales = held([P, 2, S], U8, "y_scales")
+
+        def weave(woven, flat):
+            nc.vector.tensor_copy(out=woven.rearrange("p (c i) t -> p c t i", i=4),
+                                  in_=flat.rearrange("p t (c i) -> p c t i", i=4))
 
         def logs(first, width):
             half, c = divmod(first, HALF)
             part = sig[half][:, :, c:c + width]
-            nc.scalar.activation(out=part, in_=part, func=ACT.Ln, bias=tiny[:])
+            nc.scalar.activation(out=part, in_=part, func=ACT.Ln, bias=floor[:])
 
         def rates(first, width):
             half, c = divmod(first, HALF)
             cols = slice(c, c + width)
             flat = [ring.tile([P, PACK, width], BF16, name="h_flat", align_bytes=64) for g in range(2)]
-            for u in range(8):
+            for u in range(2 * PACK):
                 g, t = divmod(u, PACK)
                 nc.vector.scalar_tensor_tensor(
                     out=flat[g][:, t, :], in0=sig[half][:, u, cols], scalar=neg_gain[:, u:u + 1],
                     in1=lin[half][:, u, cols], op0=ALU.mult, op1=ALU.max)
             woven = [ring.tile([P, width, PACK], BF16, name="h_woven", align_bytes=64) for g in range(2)]
             for g in range(2):
-                nc.vector.tensor_copy(out=woven[g][:].rearrange("p (c i) t -> p c t i", i=4),
-                                      in_=flat[g][:].rearrange("p t (c i) -> p c t i", i=4))
+                weave(woven[g][:], flat[g][:])
             h_q = []
             for g in range(2):
                 codes = ring.tile([P, width], U32, name="h_codes", align_bytes=64)
@@ -258,8 +263,10 @@ def tile_list_cortical_softplus_currents_kernel(
             js = slice(first, first + width)
             ys = [ring.tile([P, PACK, width], F32, name="y", align_bytes=64) for g in range(2)]
             woven = [ring.tile([P, width, PACK], BF16, name="y_woven", align_bytes=64) for g in range(2)]
+            from_sbuf = []
             for c in range(0, width, SUB):
                 cols = slice(c, c + SUB)
+                sub = (first + c) // SUB
                 for g in range(2):
                     bank = psum.tile([P, PACK, SUB], F32, name="bank", tag="bank")
                     for t in range(PACK):
@@ -268,33 +275,27 @@ def tile_list_cortical_softplus_currents_kernel(
                             codes, scales = h_q[a]
                             nc.tensor.matmul_mx(
                                 out=bank[:, t, :], lhsT=wr_w[a][:, u * P:(u + 1) * P].bitcast(FP8X4),
-                                lhsT_scale=w_sc[8 + 4 * a:, u * P:(u + 1) * P],
+                                lhsT_scale=wr_sc[WR_FIRST + 4 * a:, u * P:(u + 1) * P],
                                 rhs=codes[:, cols].bitcast(FP8X4), rhs_scale=scales[:, cols],
                                 start=(a == 0), stop=(a == 1))
-                    mode = SCALAR_WEAVES[(first + c) // SUB]
-                    if mode == 1:
+                    if sub < SCALAR_SUBS:
                         nc.scalar.copy(out=woven[g][:, cols, :], in_=bank[:].rearrange("p t c -> p c t"))
-                    if mode == 2 and g == 1:
+                    elif sub == S // SUB - 1:
                         nc.vector.tensor_copy(out=woven[g][:, cols, :], in_=bank[:].rearrange("p t c -> p c t"))
                     nc.scalar.copy(out=ys[g][:, :, cols], in_=bank[:])
-                    if mode == 2 and g == 0:
-                        nc.vector.tensor_copy(out=woven[g][:, cols, :], in_=bank[:].rearrange("p t c -> p c t"))
+                if SCALAR_SUBS <= sub < S // SUB - 1:
+                    from_sbuf.append(cols)
             for g in range(2):
                 rows = out_0[g * GROUP:(g + 1) * GROUP, js].rearrange("(p t) j -> p t j", t=PACK)
                 nc.sync.dma_start(out=rows, in_=ys[g][:])
-            for c in range(0, width, SUB):
-                cols = slice(c, c + SUB)
-                if not SCALAR_WEAVES[(first + c) // SUB]:
-                    for g in range(2):
-                        nc.vector.tensor_copy(out=woven[g][:, cols, :].rearrange("p (c i) t -> p c t i", i=4),
-                                              in_=ys[g][:, :, cols].rearrange("p t (c i) -> p c t i", i=4))
+            for cols in from_sbuf:
+                for g in range(2):
+                    weave(woven[g][:, cols, :], ys[g][:, :, cols])
             for g in range(2):
                 nc.vector.quantize_mx(out=y_codes[:, g, js].bitcast(FP8X4), scales=y_scales[:, g, js],
                                       in_=woven[g][:].rearrange("p c t -> p (c t)"))
-
-        def store_planes(first, last):
             words = out_1.rearrange("g p j t -> p g (j t)").bitcast(I32)
-            nc.sync.dma_start(out=words[:, :, first:last], in_=y_codes[:, :, first:last])
+            nc.sync.dma_start(out=words[:, :, js], in_=y_codes[:, :, js])
 
         def store_scales(first, last):
             cols = slice(first // 4, last // 4)
@@ -303,18 +304,17 @@ def tile_list_cortical_softplus_currents_kernel(
                     out=out_2[:, r:16:4, :].bitcast(I32).rearrange("g q c -> q g c")[:, :, cols],
                     in_=y_scales[r:P:32, :, :].bitcast(I32)[:, :, cols])
 
-        firsts = [sum(WIDTHS[:n]) for n in range(len(WIDTHS))]
+        count = len(CHUNKS)
+        firsts = [sum(CHUNKS[:n]) for n in range(count)]
         h_q = {}
-        logs(firsts[0], WIDTHS[0])
-        for n in range(len(WIDTHS) + 1):
-            if n + 1 < len(WIDTHS):
-                logs(firsts[n + 1], WIDTHS[n + 1])
-            if n < len(WIDTHS):
-                h_q[n] = rates(firsts[n], WIDTHS[n])
-
+        logs(firsts[0], CHUNKS[0])
+        for n in range(count + 1):
+            if n + 1 < count:
+                logs(firsts[n + 1], CHUNKS[n + 1])
+            if n < count:
+                h_q[n] = rates(firsts[n], CHUNKS[n])
             if n >= 1:
-                currents(h_q[n - 1], firsts[n - 1], WIDTHS[n - 1])
-                store_planes(firsts[n - 1], firsts[n - 1] + WIDTHS[n - 1])
-            if n == len(WIDTHS) - 2:
+                currents(h_q[n - 1], firsts[n - 1], CHUNKS[n - 1])
+            if n == count - 2:
                 store_scales(0, firsts[n])
         store_scales(firsts[-2], S)

@@ -20,8 +20,7 @@ T, T2, S, H, N = 4096, 2048, 1024, 1024, 1024
 HALF = 512
 SUB = 128
 CHUNKS = (128, 128, 256, 256, 128, 128)
-SCALAR_SUBS = 5
-SCALAR_LINEAR = 2
+SCALAR_SUBS = 4
 TAB_FIRST = 4
 WR_FIRST = 8
 FLOOR = 2.0 ** -60
@@ -36,7 +35,6 @@ def tile_list_cortical_softplus_currents_kernel(
     with ExitStack() as ctx:
         lists = ctx.enter_context(tc.tile_pool(name="lists", bufs=1))
         keep = ctx.enter_context(tc.tile_pool(name="keep", bufs=1))
-        big = ctx.enter_context(tc.tile_pool(name="big", bufs=4))
         ring = ctx.enter_context(tc.tile_pool(name="ring", bufs=4))
         psum = ctx.enter_context(tc.psum_pool(name="psum", bufs=8))
 
@@ -59,11 +57,9 @@ def tile_list_cortical_softplus_currents_kernel(
         warm = held([P, 1], F32, "warm")
         nc.scalar.activation(out=warm[:], in_=zero[:], func=ACT.Sigmoid)
 
-        def load_we(a, g):
-            raw = held([P, PACK, GROUP], F32, "we_raw_%d_%d" % (a, g))
-            rows = we[a * GROUP:(a + 1) * GROUP, g * GROUP:(g + 1) * GROUP]
-            nc.sync.dma_start(out=raw[:], in_=rows.rearrange("(p i) c -> p i c", i=PACK))
-            return raw
+        def load_we(a, g, first=0, last=PACK):
+            rows = we[a * GROUP:(a + 1) * GROUP, g * GROUP:(g + 1) * GROUP].rearrange("(p i) c -> p i c", i=PACK)
+            nc.sync.dma_start(out=we_raw[a, g][:, first:last, :], in_=rows[:, first:last, :])
 
         def load_words(tile, words, first, last):
             src = words.rearrange("p c i -> p (c i)").bitcast(I32)
@@ -74,41 +70,44 @@ def tile_list_cortical_softplus_currents_kernel(
                 rows = tile[32 * q + first:32 * q + first + 8, :]
                 nc.sync.dma_start(out=rows.bitcast(I32), in_=scales[:, 4 * q:4 * q + 4, :].bitcast(I32))
 
-        def load_plane(tile, scales):
-            for r in range(4):
-                nc.sync.dma_start(out=tile[r:P:32, :].bitcast(I32), in_=scales[0, r:16:4, :].bitcast(I32))
+        def load_plane_rows(tile, scales, a, first, rows):
+            for r in rows:
+                nc.sync.dma_start(out=tile[first + r:P:32, :].bitcast(I32), in_=scales[a, r:16:4, :].bitcast(I32))
 
-        we_raw = {}
+        we_raw = {(a, g): held([P, PACK, GROUP], F32, "we_raw_%d_%d" % (a, g)) for a in range(2) for g in range(2)}
         tab2_w = held([P, T2], I32, "tab2_w")
-        load_words(tab2_w, tab2_words[0], 0, T2 // 2)
-        load_words(tab2_w, tab2_words[0], T2 // 2, T2)
+        tab_w = [held([P, T], I32, "tab_w_%d" % a) for a in range(2)]
         nc.sync.dma_start(idx2[:], offs2)
+        load_words(tab2_w, tab2_words[0], 0, T2)
         nc.sync.dma_start(idx[:], offs)
+        load_plane_rows(tab2_sc, tab2_scales, 0, 0, range(4))
+        load_words(tab_w[0], tab_words[0], 0, T // 2)
         wi_raw = held([P, 2 * H], U8, "wi_raw")
         nc.sync.dma_start(out=wi_raw[:].bitcast(I32), in_=wi_words[0].bitcast(I32))
-        tab_w = [big.tile([P, T], I32, name="tab_w", tag="big", align_bytes=64) for a in range(2)]
-        load_words(tab_w[0], tab_words[0], 0, T // 2)
-        load_plane(tab2_sc, tab2_scales)
-        load_plane_pair(tab_sc, tab_scales, TAB_FIRST, (0, 1))
+        load_plane_rows(wi_sc_raw, wi_scales, 0, 0, range(4))
         load_words(tab_w[0], tab_words[0], T // 2, T)
-        load_plane_pair(tab_sc, tab_scales, TAB_FIRST, (2, 3))
-        we_raw[0, 0] = load_we(0, 0)
-        load_plane(wi_sc_raw, wi_scales)
-        we_raw[1, 0] = load_we(1, 0)
+        load_plane_rows(tab_sc, tab_scales, 0, TAB_FIRST, range(4))
+        load_we(0, 0, 0, 2)
+        load_plane_rows(tab_sc, tab_scales, 1, TAB_FIRST + 4, range(4))
+        load_we(0, 0, 2, 4)
+        load_we(1, 0)
         gain_sb = held([P, 2, PACK], F32, "gain_sb")
         nc.sync.dma_start(out=gain_sb[:], in_=gain.rearrange("(g p t) -> p g t", g=2, t=PACK))
-        we_raw[0, 1] = load_we(0, 1)
-        load_words(tab_w[1], tab_words[1], 0, T)
-        we_raw[1, 1] = load_we(1, 1)
+        load_words(tab_w[1], tab_words[1], 0, T // 2)
+        load_words(tab_w[1], tab_words[1], T // 2, T)
+        load_we(0, 1)
+        load_we(1, 1)
         load_plane_pair(wr_sc_raw, wr_scales, WR_FIRST, range(4))
         wr_raw = [held([P, N], I32, "wr_raw_%d" % a) for a in range(2)]
         for a in range(2):
             load_words(wr_raw[a], wr_words[a], 0, N)
 
-        def gather_words(table, offsets, half, name):
-            picked = held([P, HALF], U32, name)
+        def gather_words(table, offsets, name):
+            picked = held([P, S], U32, name)
             cols = HALF // 16
-            nc.vector.tensor_copy(picked[:], table[:].bitcast(U32).indirect(offsets[:, half * cols:(half + 1) * cols]))
+            for half in range(2):
+                nc.vector.tensor_copy(picked[:, half * HALF:(half + 1) * HALF],
+                                      table[:].bitcast(U32).indirect(offsets[:, half * cols:(half + 1) * cols]))
             return picked
 
         def deal(dealt, raw, run):
@@ -118,109 +117,94 @@ def tile_list_cortical_softplus_currents_kernel(
             )
 
         def we_views(a, g):
-            dealt = ring.tile([P, PACK, P, PACK], BF16, name="we_bf", bufs=3, align_bytes=64)
+            dealt = held([P, PACK, P, PACK], BF16, "lin_0_%d" % a if g == 1 else "we_bf_%d" % a)
             dst = dealt[:].rearrange("p t m i -> p m t i")
             src = we_raw[a, g][:].rearrange("p i (m t) -> p m t i", t=PACK)
             return dealt, dst, src
 
-        def round_we_on_scalar(a, g):
+        def round_we(a, g, shares):
             dealt, dst, src = we_views(a, g)
-            nc.scalar.activation(out=dst, in_=src, func=ACT.Copy, scale=-1.0)
+            for engine, first, last in shares:
+                if engine is nc.scalar:
+                    engine.activation(out=dst[:, first:last], in_=src[:, first:last], func=ACT.Copy, scale=-1.0)
+                else:
+                    engine.tensor_scalar(out=dst[:, first:last], in0=src[:, first:last], scalar1=-1.0, scalar2=0.0,
+                                         op0=ALU.mult, op1=ALU.add)
             return dealt
 
-        def round_we_on_gpsimd(a, g):
-            dealt, dst, src = we_views(a, g)
-            nc.gpsimd.tensor_scalar(out=dst, in0=src, scalar1=-1.0, scalar2=0.0, op0=ALU.mult, op1=ALU.add)
-            return dealt
-
-        def quantise_we(a, g, dealt):
+        def quantise_we(a, g, dealt, parts):
             codes = held([P, GROUP], U32, "we_codes_%d_%d" % (a, g))
             scales = held([P, GROUP], U8, "we_scales_%d_%d" % (a, g))
-            nc.vector.quantize_mx(out=codes[:].bitcast(FP8X4), scales=scales[:],
-                                  in_=dealt[:].rearrange("p t m i -> p (t m i)"))
+            flat = dealt[:].rearrange("p t m i -> p (t m i)")
+            step = GROUP // parts
+            for c in range(0, GROUP, step):
+                nc.vector.quantize_mx(out=codes[:, c:c + step].bitcast(FP8X4), scales=scales[:, c:c + step],
+                                      in_=flat[:, PACK * c:PACK * (c + step)])
             return codes, scales
 
-        v2_w = [gather_words(tab2_w, idx2, half, "v2_w_%d" % half) for half in range(2)]
-        wi_w = held([P, 2 * H], U8, "wi_w")
-        deal(wi_w[:].bitcast(U16), wi_raw[:].bitcast(U16), 8)
+        v2_w = gather_words(tab2_w, idx2, "v2_w")
         v2_sc = held([P, S], U8, "v2_sc")
         nc.vector.tensor_copy(v2_sc[:], tab2_sc[:].indirect(idx2[:]))
-        v_w = {}
-        for half in range(2):
-            v_w[0, half] = gather_words(tab_w[0], idx, half, "v_w_0_%d" % half)
+        wi_w = held([P, 2 * H], U8, "wi_w")
+        deal(wi_w[:].bitcast(U16), wi_raw[:].bitcast(U16), 8)
+        wi_sc = held([P, H], U8, "wi_sc")
+        deal(wi_sc[:], wi_sc_raw[:], 16)
+        v_w = [gather_words(tab_w[0], idx, "v_w_0")]
         v_sc = held([P, S], U8, "v_sc")
         nc.vector.tensor_copy(v_sc[:], tab_sc[:].indirect(idx[:]))
         we_q = {}
-        we_q[0, 0] = quantise_we(0, 0, round_we_on_scalar(0, 0))
-        wi_sc = held([P, H], U8, "wi_sc")
-        deal(wi_sc[:], wi_sc_raw[:], 16)
-        we_q[1, 0] = quantise_we(1, 0, round_we_on_scalar(1, 0))
+        for a in range(2):
+            we_q[a, 0] = quantise_we(a, 0, round_we(a, 0, [(nc.scalar, 0, P)]), 1)
         neg_gain = held([P, 2 * PACK], F32, "neg_gain")
         nc.vector.tensor_scalar(out=neg_gain[:], in0=gain_sb[:].rearrange("p g t -> p (g t)"),
                                 scalar1=-1.0, scalar2=None, op0=ALU.mult)
-        we_q[0, 1] = quantise_we(0, 1, round_we_on_scalar(0, 1))
-        for half in range(2):
-            v_w[1, half] = gather_words(tab_w[1], idx, half, "v_w_1_%d" % half)
+        v_w.append(gather_words(tab_w[1], idx, "v_w_1"))
+        we_q[0, 1] = quantise_we(0, 1, round_we(0, 1, [(nc.vector, 0, P)]), 1)
+        we_q[1, 1] = quantise_we(1, 1, round_we(1, 1, [(nc.scalar, 0, P)]), 1)
 
-        sig = [big.tile([P, 2 * PACK, HALF], F32, name="sig", tag="big", align_bytes=64) for half in range(2)]
-        lin = [big.tile([P, 2 * PACK, HALF], F32, name="lin", tag="big", align_bytes=64) for half in range(2)]
+        sig = {(g, half): held([P, HALF, PACK], F32, "we_raw_%d_%d" % (g ^ half, half)) for g in range(2) for half in range(2)}
+        lin = {(g, half): held([P, HALF, PACK], BF16, "lin_%d_%d" % (g, half)) for g in range(2) for half in range(2)}
+        ng = neg_gain[:].rearrange("p (g t) -> p g t", g=2)
 
-        def excite(bank, a, g, t, half):
-            codes, scales = we_q[a, g]
-            nc.tensor.matmul_mx(
-                out=bank[:], lhsT=codes[:, t * P:(t + 1) * P].bitcast(FP8X4),
-                lhsT_scale=scales[:, t * P:(t + 1) * P],
-                rhs=v_w[a, half][:].bitcast(FP8X4),
-                rhs_scale=v_sc[TAB_FIRST + 4 * a:, half * HALF:(half + 1) * HALF],
-                start=(a == 0), stop=(a == 1))
+        def drive(bank, kind, g, sub, start, stop):
+            js = slice(sub * SUB, (sub + 1) * SUB)
+            for t in range(PACK):
+                u = g * PACK + t
+                if kind == 2:
+                    lhs, lhs_sc = wi_w[:, u * 2 * P:(u + 1) * 2 * P].bitcast(FP4X4), wi_sc[:, u * P:(u + 1) * P]
+                    rhs, rhs_sc = v2_w[:, js], v2_sc[:, js]
+                else:
+                    codes, scales = we_q[kind, g]
+                    lhs, lhs_sc = codes[:, t * P:(t + 1) * P].bitcast(FP8X4), scales[:, t * P:(t + 1) * P]
+                    rhs, rhs_sc = v_w[kind][:, js], v_sc[TAB_FIRST + 4 * kind:, js]
+                nc.tensor.matmul_mx(out=bank[:, t, :], lhsT=lhs, lhsT_scale=lhs_sc, rhs=rhs.bitcast(FP8X4),
+                                    rhs_scale=rhs_sc, start=(start and t == 0), stop=(stop and t == PACK - 1))
 
-        def inhibit(bank, g, t, half):
-            u = g * PACK + t
-            nc.tensor.matmul_mx(
-                out=bank[:], lhsT=wi_w[:, u * 2 * P:(u + 1) * 2 * P].bitcast(FP4X4),
-                lhsT_scale=wi_sc[:, u * P:(u + 1) * P],
-                rhs=v2_w[half][:].bitcast(FP8X4), rhs_scale=v2_sc[:, half * HALF:(half + 1) * HALF],
-                start=False, stop=False)
+        def drain(bank, g, sub):
+            half, c = divmod(sub * SUB, HALF)
+            woven = bank[:].rearrange("p t j -> p j t")
+            nc.scalar.activation(out=sig[g, half][:, c:c + SUB, :], in_=woven, func=ACT.Sigmoid, bias=zero[:])
+            nc.vector.tensor_tensor(out=lin[g, half][:, c:c + SUB, :], in0=woven,
+                                    in1=ng[:, g:g + 1, :].to_broadcast([P, SUB, PACK]), op=ALU.mult)
 
-        def drain(bank, g, t, half):
-            u = g * PACK + t
-            nc.scalar.activation(out=sig[half][:, u, :], in_=bank[:], func=ACT.Sigmoid, bias=zero[:])
-            if g == 0 and half == 1 and t >= PACK - SCALAR_LINEAR:
-                nc.scalar.activation(out=lin[half][:, u, :], in_=bank[:], func=ACT.Copy, scale=neg_gain[:, u:u + 1])
-            else:
-                nc.vector.tensor_scalar(out=lin[half][:, u, :], in0=bank[:], scalar1=neg_gain[:, u:u + 1],
-                                        scalar2=None, op0=ALU.mult)
+        subs = S // SUB
+        banks = [psum.tile([P, PACK, SUB], F32, name="bank", tag="bank") for sub in range(subs)]
+        for kind in (2, 0, 1):
+            for sub in range(subs):
+                drive(banks[sub], kind, 0, sub, kind == 2, kind == 1)
+        for sub in range(subs):
+            drain(banks[sub], 0, sub)
 
-        units = [(t, half) for half in range(2) for t in range(PACK)]
-        banks = [psum.tile([P, HALF], F32, name="bank", tag="bank") for unit in units]
-        for bank, (t, half) in zip(banks, units):
-            excite(bank, 0, 0, t, half)
-        for bank, (t, half) in zip(banks, units):
-            inhibit(bank, 0, t, half)
-        for bank, (t, half) in zip(banks, units):
-            excite(bank, 1, 0, t, half)
-        for t in range(PACK):
-            drain(banks[t], 0, t, 0)
-        we_q[1, 1] = quantise_we(1, 1, round_we_on_gpsimd(1, 1))
-        for t in range(PACK):
-            drain(banks[PACK + t], 0, t, 1)
+        banks = [psum.tile([P, PACK, SUB], F32, name="bank", tag="bank") for sub in range(subs)]
+        for sub in range(subs):
+            for kind in (2, 0, 1):
+                drive(banks[sub], kind, 1, sub, kind == 2, kind == 1)
+        for sub in range(subs):
+            drain(banks[sub], 1, sub)
 
-        banks = [psum.tile([P, HALF], F32, name="bank", tag="bank") for unit in units]
-        for t in range(PACK):
-            excite(banks[t], 0, 1, t, 0)
-            inhibit(banks[t], 1, t, 0)
-        for t in range(PACK):
-            excite(banks[t], 1, 1, t, 0)
-            excite(banks[PACK + t], 0, 1, t, 1)
-            inhibit(banks[PACK + t], 1, t, 1)
-        for t in range(PACK):
-            excite(banks[PACK + t], 1, 1, t, 1)
-        for bank, (t, half) in zip(banks, units):
-            drain(bank, 1, t, half)
-
-        wr_sc = held([P, N], U8, "wr_sc")
+        wr_sc = held([P, N], U8, "v2_sc")
         deal(wr_sc[:], wr_sc_raw[:], 16)
-        wr_w = [held([P, N], I32, "wr_w_%d" % a) for a in range(2)]
+        wr_w = [held([P, N], I32, name) for name in ("v2_w", "v_w_0")]
         for a in range(2):
             deal(wr_w[a][:], wr_raw[a][:], 4)
 
@@ -235,29 +219,24 @@ def tile_list_cortical_softplus_currents_kernel(
 
         def logs(first, width):
             half, c = divmod(first, HALF)
-            part = sig[half][:, :, c:c + width]
-            nc.scalar.activation(out=part, in_=part, func=ACT.Ln, bias=floor[:])
+            for g in range(2):
+                part = sig[g, half][:, c:c + width, :]
+                nc.scalar.activation(out=part, in_=part, func=ACT.Ln, bias=floor[:])
 
         def rates(first, width):
+            h = ring.tile([P, 2, width, PACK], BF16, name="h", bufs=3, align_bytes=64)
             half, c = divmod(first, HALF)
-            cols = slice(c, c + width)
-            flat = [ring.tile([P, PACK, width], BF16, name="h_flat", align_bytes=64) for g in range(2)]
-            for u in range(2 * PACK):
-                g, t = divmod(u, PACK)
-                nc.vector.scalar_tensor_tensor(
-                    out=flat[g][:, t, :], in0=sig[half][:, u, cols], scalar=neg_gain[:, u:u + 1],
-                    in1=lin[half][:, u, cols], op0=ALU.mult, op1=ALU.max)
-            woven = [ring.tile([P, width, PACK], BF16, name="h_woven", align_bytes=64) for g in range(2)]
             for g in range(2):
-                weave(woven[g][:], flat[g][:])
-            h_q = []
+                nc.vector.tensor_tensor(out=h[:, g], in0=sig[g, half][:, c:c + width, :],
+                                        in1=ng[:, g:g + 1, :].to_broadcast([P, width, PACK]), op=ALU.mult)
             for g in range(2):
-                codes = ring.tile([P, width], U32, name="h_codes", align_bytes=64)
-                scales = ring.tile([P, width], U8, name="h_scales", align_bytes=64)
-                nc.vector.quantize_mx(out=codes[:].bitcast(FP8X4), scales=scales[:],
-                                      in_=woven[g][:].rearrange("p c t -> p (c t)"))
-                h_q.append((codes, scales))
-            return h_q
+                nc.vector.tensor_tensor(out=h[:, g], in0=h[:, g], in1=lin[g, half][:, c:c + width, :], op=ALU.max)
+            codes = ring.tile([P, 2, width], U32, name="h_codes", bufs=3, align_bytes=64)
+            scales = ring.tile([P, 2, width], U8, name="h_scales", bufs=3, align_bytes=64)
+            nc.vector.quantize_mx(out=codes[:].rearrange("p g c -> p (g c)").bitcast(FP8X4),
+                                  scales=scales[:].rearrange("p g c -> p (g c)"),
+                                  in_=h[:].rearrange("p g c t -> p (g c t)"))
+            return [(codes[:, g, :], scales[:, g, :]) for g in range(2)]
 
         def currents(h_q, first, width):
             js = slice(first, first + width)

@@ -20,7 +20,8 @@ T, T2, S, H, N = 4096, 2048, 1024, 1024, 1024
 HALF = 512
 SUB = 128
 CHUNKS = (128, 128, 256, 256, 128, 128)
-SCALAR_SUBS = 4
+AHEAD = 4
+FROM_SBUF = 3
 TAB_FIRST = 4
 WR_FIRST = 8
 FLOOR = 2.0 ** -60
@@ -57,39 +58,37 @@ def tile_list_cortical_softplus_currents_kernel(
         warm = held([P, 1], F32, "warm")
         nc.scalar.activation(out=warm[:], in_=zero[:], func=ACT.Sigmoid)
 
-        def load_we(a, g, first=0, last=PACK):
+        def load_we(a, g):
             rows = we[a * GROUP:(a + 1) * GROUP, g * GROUP:(g + 1) * GROUP].rearrange("(p i) c -> p i c", i=PACK)
-            nc.sync.dma_start(out=we_raw[a, g][:, first:last, :], in_=rows[:, first:last, :])
+            nc.sync.dma_start(out=we_raw[a, g][:], in_=rows)
 
         def load_words(tile, words, first, last):
             src = words.rearrange("p c i -> p (c i)").bitcast(I32)
             nc.sync.dma_start(out=tile[:, first:last], in_=src[:, first:last])
 
-        def load_plane_pair(tile, scales, first, quadrants):
-            for q in quadrants:
+        def load_plane_pair(tile, scales, first):
+            for q in range(4):
                 rows = tile[32 * q + first:32 * q + first + 8, :]
                 nc.sync.dma_start(out=rows.bitcast(I32), in_=scales[:, 4 * q:4 * q + 4, :].bitcast(I32))
 
-        def load_plane_rows(tile, scales, a, first, rows):
-            for r in rows:
-                nc.sync.dma_start(out=tile[first + r:P:32, :].bitcast(I32), in_=scales[a, r:16:4, :].bitcast(I32))
+        def load_plane(tile, scales):
+            for r in range(4):
+                nc.sync.dma_start(out=tile[r:P:32, :].bitcast(I32), in_=scales[0, r:16:4, :].bitcast(I32))
 
         we_raw = {(a, g): held([P, PACK, GROUP], F32, "we_raw_%d_%d" % (a, g)) for a in range(2) for g in range(2)}
         tab2_w = held([P, T2], I32, "tab2_w")
         tab_w = [held([P, T], I32, "tab_w_%d" % a) for a in range(2)]
         nc.sync.dma_start(idx2[:], offs2)
         load_words(tab2_w, tab2_words[0], 0, T2)
-        nc.sync.dma_start(idx[:], offs)
-        load_plane_rows(tab2_sc, tab2_scales, 0, 0, range(4))
         load_words(tab_w[0], tab_words[0], 0, T // 2)
+        nc.sync.dma_start(idx[:], offs)
+        load_plane(tab2_sc, tab2_scales)
+        load_words(tab_w[0], tab_words[0], T // 2, T)
         wi_raw = held([P, 2 * H], U8, "wi_raw")
         nc.sync.dma_start(out=wi_raw[:].bitcast(I32), in_=wi_words[0].bitcast(I32))
-        load_plane_rows(wi_sc_raw, wi_scales, 0, 0, range(4))
-        load_words(tab_w[0], tab_words[0], T // 2, T)
-        load_plane_rows(tab_sc, tab_scales, 0, TAB_FIRST, range(4))
-        load_we(0, 0, 0, 2)
-        load_plane_rows(tab_sc, tab_scales, 1, TAB_FIRST + 4, range(4))
-        load_we(0, 0, 2, 4)
+        load_plane(wi_sc_raw, wi_scales)
+        load_we(0, 0)
+        load_plane_pair(tab_sc, tab_scales, TAB_FIRST)
         load_we(1, 0)
         gain_sb = held([P, 2, PACK], F32, "gain_sb")
         nc.sync.dma_start(out=gain_sb[:], in_=gain.rearrange("(g p t) -> p g t", g=2, t=PACK))
@@ -97,7 +96,7 @@ def tile_list_cortical_softplus_currents_kernel(
         load_words(tab_w[1], tab_words[1], T // 2, T)
         load_we(0, 1)
         load_we(1, 1)
-        load_plane_pair(wr_sc_raw, wr_scales, WR_FIRST, range(4))
+        load_plane_pair(wr_sc_raw, wr_scales, WR_FIRST)
         wr_raw = [held([P, N], I32, "wr_raw_%d" % a) for a in range(2)]
         for a in range(2):
             load_words(wr_raw[a], wr_words[a], 0, N)
@@ -133,7 +132,7 @@ def tile_list_cortical_softplus_currents_kernel(
             return dealt
 
         def quantise_we(a, g, dealt, parts):
-            codes = held([P, GROUP], U32, "we_codes_%d_%d" % (a, g))
+            codes = held([P, GROUP], U32, "tab_sc" if (a, g) == (0, 0) else "we_codes_%d_%d" % (a, g))
             scales = held([P, GROUP], U8, "we_scales_%d_%d" % (a, g))
             flat = dealt[:].rearrange("p t m i -> p (t m i)")
             step = GROUP // parts
@@ -162,30 +161,30 @@ def tile_list_cortical_softplus_currents_kernel(
         we_q[0, 1] = quantise_we(0, 1, round_we(0, 1, [(nc.vector, 0, P)]), 1)
         we_q[1, 1] = quantise_we(1, 1, round_we(1, 1, [(nc.scalar, 0, P)]), 1)
 
-        sig = {(g, half): held([P, HALF, PACK], F32, "we_raw_%d_%d" % (g ^ half, half)) for g in range(2) for half in range(2)}
-        lin = {(g, half): held([P, HALF, PACK], BF16, "lin_%d_%d" % (g, half)) for g in range(2) for half in range(2)}
-        ng = neg_gain[:].rearrange("p (g t) -> p g t", g=2)
+        sig = {(g, half): held([P, PACK, HALF], F32, "we_raw_%d_%d" % (g ^ half, half)) for g in range(2) for half in range(2)}
+        lin = {(g, half): held([P, PACK, HALF], BF16, "lin_%d_%d" % (g, half)) for g in range(2) for half in range(2)}
 
-        def drive(bank, kind, g, sub, start, stop):
-            js = slice(sub * SUB, (sub + 1) * SUB)
-            for t in range(PACK):
-                u = g * PACK + t
-                if kind == 2:
-                    lhs, lhs_sc = wi_w[:, u * 2 * P:(u + 1) * 2 * P].bitcast(FP4X4), wi_sc[:, u * P:(u + 1) * P]
-                    rhs, rhs_sc = v2_w[:, js], v2_sc[:, js]
-                else:
-                    codes, scales = we_q[kind, g]
-                    lhs, lhs_sc = codes[:, t * P:(t + 1) * P].bitcast(FP8X4), scales[:, t * P:(t + 1) * P]
-                    rhs, rhs_sc = v_w[kind][:, js], v_sc[TAB_FIRST + 4 * kind:, js]
-                nc.tensor.matmul_mx(out=bank[:, t, :], lhsT=lhs, lhsT_scale=lhs_sc, rhs=rhs.bitcast(FP8X4),
-                                    rhs_scale=rhs_sc, start=(start and t == 0), stop=(stop and t == PACK - 1))
+        def drive(bank, kind, g, unit, start, stop):
+            half, t = divmod(unit, PACK)
+            js = slice(half * HALF, (half + 1) * HALF)
+            u = g * PACK + t
+            if kind == 2:
+                lhs, lhs_sc = wi_w[:, u * 2 * P:(u + 1) * 2 * P].bitcast(FP4X4), wi_sc[:, u * P:(u + 1) * P]
+                rhs, rhs_sc = v2_w[:, js], v2_sc[:, js]
+            else:
+                codes, scales = we_q[kind, g]
+                lhs, lhs_sc = codes[:, t * P:(t + 1) * P].bitcast(FP8X4), scales[:, t * P:(t + 1) * P]
+                rhs, rhs_sc = v_w[kind][:, js], v_sc[TAB_FIRST + 4 * kind:, js]
+            nc.tensor.matmul_mx(out=bank[:].rearrange("p t j -> p (t j)"), lhsT=lhs, lhsT_scale=lhs_sc, rhs=rhs.bitcast(FP8X4),
+                                rhs_scale=rhs_sc, start=start, stop=stop)
 
-        def drain(bank, g, sub):
-            half, c = divmod(sub * SUB, HALF)
-            woven = bank[:].rearrange("p t j -> p j t")
-            nc.scalar.activation(out=sig[g, half][:, c:c + SUB, :], in_=woven, func=ACT.Sigmoid, bias=zero[:])
-            nc.vector.tensor_tensor(out=lin[g, half][:, c:c + SUB, :], in0=woven,
-                                    in1=ng[:, g:g + 1, :].to_broadcast([P, SUB, PACK]), op=ALU.mult)
+        def drain(bank, g, unit):
+            half, t = divmod(unit, PACK)
+            u = g * PACK + t
+            z = bank[:].rearrange("p t j -> p (t j)")
+            nc.scalar.activation(out=sig[g, half][:, t, :], in_=z, func=ACT.Sigmoid, bias=zero[:])
+            nc.vector.tensor_scalar(out=lin[g, half][:, t, :], in0=z, scalar1=neg_gain[:, u:u + 1],
+                                    scalar2=None, op0=ALU.mult)
 
         subs = S // SUB
         banks = [psum.tile([P, PACK, SUB], F32, name="bank", tag="bank") for sub in range(subs)]
@@ -210,6 +209,8 @@ def tile_list_cortical_softplus_currents_kernel(
 
         floor = keep.tile([P, 1], F32, name="floor", tag="bias")
         nc.gpsimd.memset(floor[:], FLOOR)
+        ys = [held([P, PACK, S], F32, "tab_w_%d" % g) for g in range(2)]
+        woven = [held([P, S, PACK], BF16, "y_woven_%d" % g) for g in range(2)]
         y_codes = held([P, 2, S], I32, "y_codes")
         y_scales = held([P, 2, S], U8, "y_scales")
 
@@ -220,31 +221,36 @@ def tile_list_cortical_softplus_currents_kernel(
         def logs(first, width):
             half, c = divmod(first, HALF)
             for g in range(2):
-                part = sig[g, half][:, c:c + width, :]
+                part = sig[g, half][:, :, c:c + width]
                 nc.scalar.activation(out=part, in_=part, func=ACT.Ln, bias=floor[:])
 
         def rates(first, width):
             h = ring.tile([P, 2, width, PACK], BF16, name="h", bufs=3, align_bytes=64)
             half, c = divmod(first, HALF)
+            flat = ring.tile([P, 2, PACK, width], BF16, name="h_flat", bufs=3, align_bytes=64)
+            for u in range(2 * PACK):
+                g, t = divmod(u, PACK)
+                nc.vector.scalar_tensor_tensor(
+                    out=flat[:, g, t, :], in0=sig[g, half][:, t, c:c + width], scalar=neg_gain[:, u:u + 1],
+                    in1=lin[g, half][:, t, c:c + width], op0=ALU.mult, op1=ALU.max)
             for g in range(2):
-                nc.vector.tensor_tensor(out=h[:, g], in0=sig[g, half][:, c:c + width, :],
-                                        in1=ng[:, g:g + 1, :].to_broadcast([P, width, PACK]), op=ALU.mult)
-            for g in range(2):
-                nc.vector.tensor_tensor(out=h[:, g], in0=h[:, g], in1=lin[g, half][:, c:c + width, :], op=ALU.max)
-            codes = ring.tile([P, 2, width], U32, name="h_codes", bufs=3, align_bytes=64)
-            scales = ring.tile([P, 2, width], U8, name="h_scales", bufs=3, align_bytes=64)
+                weave(h[:, g], flat[:, g])
+            codes = held([P, 2, width], U32, "h_codes_%d" % first)
+            scales = held([P, 2, width], U8, "h_scales_%d" % first)
             nc.vector.quantize_mx(out=codes[:].rearrange("p g c -> p (g c)").bitcast(FP8X4),
                                   scales=scales[:].rearrange("p g c -> p (g c)"),
                                   in_=h[:].rearrange("p g c t -> p (g c t)"))
             return [(codes[:, g, :], scales[:, g, :]) for g in range(2)]
 
+        def store_currents(js):
+            for g in range(2):
+                rows = out_0[g * GROUP:(g + 1) * GROUP, js].rearrange("(p t) j -> p t j", t=PACK)
+                nc.sync.dma_start(out=rows, in_=ys[g][:, :, js])
+
         def currents(h_q, first, width):
-            js = slice(first, first + width)
-            ys = [ring.tile([P, PACK, width], F32, name="y", align_bytes=64) for g in range(2)]
-            woven = [ring.tile([P, width, PACK], BF16, name="y_woven", align_bytes=64) for g in range(2)]
-            from_sbuf = []
             for c in range(0, width, SUB):
                 cols = slice(c, c + SUB)
+                js = slice(first + c, first + c + SUB)
                 sub = (first + c) // SUB
                 for g in range(2):
                     bank = psum.tile([P, PACK, SUB], F32, name="bank", tag="bank")
@@ -257,22 +263,25 @@ def tile_list_cortical_softplus_currents_kernel(
                                 lhsT_scale=wr_sc[WR_FIRST + 4 * a:, u * P:(u + 1) * P],
                                 rhs=codes[:, cols].bitcast(FP8X4), rhs_scale=scales[:, cols],
                                 start=(a == 0), stop=(a == 1))
-                    if sub < SCALAR_SUBS:
-                        nc.scalar.copy(out=woven[g][:, cols, :], in_=bank[:].rearrange("p t c -> p c t"))
-                    elif sub == S // SUB - 1:
-                        nc.vector.tensor_copy(out=woven[g][:, cols, :], in_=bank[:].rearrange("p t c -> p c t"))
-                    nc.scalar.copy(out=ys[g][:, :, cols], in_=bank[:])
-                if SCALAR_SUBS <= sub < S // SUB - 1:
-                    from_sbuf.append(cols)
+                    if sub == S // SUB - 1:
+                        nc.vector.tensor_copy(out=woven[g][:, js, :], in_=bank[:].rearrange("p t c -> p c t"))
+                    nc.scalar.copy(out=ys[g][:, :, js], in_=bank[:])
+                    if FROM_SBUF <= sub < S // SUB - 1:
+                        nc.scalar.copy(out=woven[g][:, js, :], in_=bank[:].rearrange("p t c -> p c t"))
+                if first >= HALF:
+                    store_currents(js)
+            if first < HALF:
+                store_currents(slice(first, first + width))
+
+        def planes(first, width):
+            js = slice(first, first + width)
+            last = min(first + width, FROM_SBUF * SUB)
             for g in range(2):
-                rows = out_0[g * GROUP:(g + 1) * GROUP, js].rearrange("(p t) j -> p t j", t=PACK)
-                nc.sync.dma_start(out=rows, in_=ys[g][:])
-            for cols in from_sbuf:
-                for g in range(2):
-                    weave(woven[g][:, cols, :], ys[g][:, :, cols])
+                if first < last:
+                    weave(woven[g][:, first:last, :], ys[g][:, :, first:last])
             for g in range(2):
                 nc.vector.quantize_mx(out=y_codes[:, g, js].bitcast(FP8X4), scales=y_scales[:, g, js],
-                                      in_=woven[g][:].rearrange("p c t -> p (c t)"))
+                                      in_=woven[g][:, js, :].rearrange("p c t -> p (c t)"))
             words = out_1.rearrange("g p j t -> p g (j t)").bitcast(I32)
             nc.sync.dma_start(out=words[:, :, js], in_=y_codes[:, :, js])
 
@@ -285,15 +294,22 @@ def tile_list_cortical_softplus_currents_kernel(
 
         count = len(CHUNKS)
         firsts = [sum(CHUNKS[:n]) for n in range(count)]
-        h_q = {}
-        logs(firsts[0], CHUNKS[0])
-        for n in range(count + 1):
-            if n + 1 < count:
-                logs(firsts[n + 1], CHUNKS[n + 1])
-            if n < count:
-                h_q[n] = rates(firsts[n], CHUNKS[n])
-            if n >= 1:
-                currents(h_q[n - 1], firsts[n - 1], CHUNKS[n - 1])
+        h_q = []
+        for n in range(AHEAD):
+            logs(firsts[n], CHUNKS[n])
+        for n in range(AHEAD):
+            h_q.append(rates(firsts[n], CHUNKS[n]))
+        for n in range(count - AHEAD):
+            currents(h_q[n], firsts[n], CHUNKS[n])
+        for n in range(AHEAD, count):
+            logs(firsts[n], CHUNKS[n])
+        for n in range(AHEAD, count):
+            if n == count - 1:
+                planes(0, firsts[count - AHEAD])
+            h_q.append(rates(firsts[n], CHUNKS[n]))
+        for n in range(count - AHEAD, count):
+            currents(h_q[n], firsts[n], CHUNKS[n])
             if n == count - 2:
                 store_scales(0, firsts[n])
+            planes(firsts[n], CHUNKS[n])
         store_scales(firsts[-2], S)

@@ -18,10 +18,13 @@ PACK = 4
 GROUP = P * PACK
 T, T2, S, H, N = 4096, 2048, 1024, 1024, 1024
 HALF = 512
+QUARTER = 256
 SUB = 128
 CHUNKS = (128, 128, 256, 256, 128, 128)
+SPLIT = 64
+EARLY = 3
 AHEAD = 4
-FROM_SBUF = 3
+FROM_PSUM = (3, 6, 7)
 TAB_FIRST = 4
 WR_FIRST = 8
 FLOOR = 2.0 ** -60
@@ -58,9 +61,9 @@ def tile_list_cortical_softplus_currents_kernel(
         warm = held([P, 1], F32, "warm")
         nc.scalar.activation(out=warm[:], in_=zero[:], func=ACT.Sigmoid)
 
-        def load_we(a, g):
+        def load_we(a, g, first=0, last=PACK):
             rows = we[a * GROUP:(a + 1) * GROUP, g * GROUP:(g + 1) * GROUP].rearrange("(p i) c -> p i c", i=PACK)
-            nc.sync.dma_start(out=we_raw[a, g][:], in_=rows)
+            nc.sync.dma_start(out=we_raw[a, g][:, first:last, :], in_=rows[:, first:last, :])
 
         def load_words(tile, words, first, last):
             src = words.rearrange("p c i -> p (c i)").bitcast(I32)
@@ -71,9 +74,9 @@ def tile_list_cortical_softplus_currents_kernel(
                 rows = tile[32 * q + first:32 * q + first + 8, :]
                 nc.sync.dma_start(out=rows.bitcast(I32), in_=scales[:, 4 * q:4 * q + 4, :].bitcast(I32))
 
-        def load_plane(tile, scales):
+        def load_plane(tile, scales, first):
             for r in range(4):
-                nc.sync.dma_start(out=tile[r:P:32, :].bitcast(I32), in_=scales[0, r:16:4, :].bitcast(I32))
+                nc.sync.dma_start(out=tile[first + r:P:32, :].bitcast(I32), in_=scales[r:16:4, :].bitcast(I32))
 
         we_raw = {(a, g): held([P, PACK, GROUP], F32, "we_raw_%d_%d" % (a, g)) for a in range(2) for g in range(2)}
         tab2_w = held([P, T2], I32, "tab2_w")
@@ -82,17 +85,19 @@ def tile_list_cortical_softplus_currents_kernel(
         load_words(tab2_w, tab2_words[0], 0, T2)
         load_words(tab_w[0], tab_words[0], 0, T // 2)
         nc.sync.dma_start(idx[:], offs)
-        load_plane(tab2_sc, tab2_scales)
+        load_plane(tab2_sc, tab2_scales[0], 0)
         load_words(tab_w[0], tab_words[0], T // 2, T)
         wi_raw = held([P, 2 * H], U8, "wi_raw")
         nc.sync.dma_start(out=wi_raw[:].bitcast(I32), in_=wi_words[0].bitcast(I32))
-        load_plane(wi_sc_raw, wi_scales)
-        load_we(0, 0)
-        load_plane_pair(tab_sc, tab_scales, TAB_FIRST)
+        load_plane(wi_sc_raw, wi_scales[0], 0)
+        load_we(0, 0, 0, 2)
+        load_plane(tab_sc, tab_scales[0], TAB_FIRST)
+        load_we(0, 0, 2, 4)
+        load_plane(tab_sc, tab_scales[1], TAB_FIRST + 4)
         load_we(1, 0)
+        load_words(tab_w[1], tab_words[1], 0, T // 2)
         gain_sb = held([P, 2, PACK], F32, "gain_sb")
         nc.sync.dma_start(out=gain_sb[:], in_=gain.rearrange("(g p t) -> p g t", g=2, t=PACK))
-        load_words(tab_w[1], tab_words[1], 0, T // 2)
         load_words(tab_w[1], tab_words[1], T // 2, T)
         load_we(0, 1)
         load_we(1, 1)
@@ -116,7 +121,7 @@ def tile_list_cortical_softplus_currents_kernel(
             )
 
         def we_views(a, g):
-            dealt = held([P, PACK, P, PACK], BF16, "lin_0_%d" % a if g == 1 else "we_bf_%d" % a)
+            dealt = held([P, PACK, P, PACK], BF16, "we_bf_%d_%d" % (a, g))
             dst = dealt[:].rearrange("p t m i -> p m t i")
             src = we_raw[a, g][:].rearrange("p i (m t) -> p m t i", t=PACK)
             return dealt, dst, src
@@ -158,33 +163,35 @@ def tile_list_cortical_softplus_currents_kernel(
         nc.vector.tensor_scalar(out=neg_gain[:], in0=gain_sb[:].rearrange("p g t -> p (g t)"),
                                 scalar1=-1.0, scalar2=None, op0=ALU.mult)
         v_w.append(gather_words(tab_w[1], idx, "v_w_1"))
-        we_q[0, 1] = quantise_we(0, 1, round_we(0, 1, [(nc.vector, 0, P)]), 1)
-        we_q[1, 1] = quantise_we(1, 1, round_we(1, 1, [(nc.scalar, 0, P)]), 1)
 
-        sig = {(g, half): held([P, PACK, HALF], F32, "we_raw_%d_%d" % (g ^ half, half)) for g in range(2) for half in range(2)}
-        lin = {(g, half): held([P, PACK, HALF], BF16, "lin_%d_%d" % (g, half)) for g in range(2) for half in range(2)}
+        we_q[0, 1] = quantise_we(0, 1, round_we(0, 1, [(nc.gpsimd, 0, P)]), 1)
 
-        def drive(bank, kind, g, unit, start, stop):
-            half, t = divmod(unit, PACK)
-            js = slice(half * HALF, (half + 1) * HALF)
-            u = g * PACK + t
-            if kind == 2:
-                lhs, lhs_sc = wi_w[:, u * 2 * P:(u + 1) * 2 * P].bitcast(FP4X4), wi_sc[:, u * P:(u + 1) * P]
-                rhs, rhs_sc = v2_w[:, js], v2_sc[:, js]
-            else:
-                codes, scales = we_q[kind, g]
-                lhs, lhs_sc = codes[:, t * P:(t + 1) * P].bitcast(FP8X4), scales[:, t * P:(t + 1) * P]
-                rhs, rhs_sc = v_w[kind][:, js], v_sc[TAB_FIRST + 4 * kind:, js]
-            nc.tensor.matmul_mx(out=bank[:].rearrange("p t j -> p (t j)"), lhsT=lhs, lhsT_scale=lhs_sc, rhs=rhs.bitcast(FP8X4),
-                                rhs_scale=rhs_sc, start=start, stop=stop)
+        sig = {(g, half): held([P, HALF, PACK], F32, "sig_%d_%d" % (g, half) if half else "we_raw_%d_0" % g) for g in range(2) for half in range(2)}
+        lin = {(g, n): held([P, QUARTER, PACK], BF16, "we_bf_0_1" if (g, n) == (0, 3) else "lin_%d_%d" % (g, n))
+               for g in range(2) for n in range(S // QUARTER)}
+        ng = neg_gain[:].rearrange("p (g t) -> p g t", g=2)
 
-        def drain(bank, g, unit):
-            half, t = divmod(unit, PACK)
-            u = g * PACK + t
-            z = bank[:].rearrange("p t j -> p (t j)")
-            nc.scalar.activation(out=sig[g, half][:, t, :], in_=z, func=ACT.Sigmoid, bias=zero[:])
-            nc.vector.tensor_scalar(out=lin[g, half][:, t, :], in0=z, scalar1=neg_gain[:, u:u + 1],
-                                    scalar2=None, op0=ALU.mult)
+        def drive(bank, kind, g, sub, start, stop):
+            js = slice(sub * SUB, (sub + 1) * SUB)
+            for t in range(PACK):
+                u = g * PACK + t
+                if kind == 2:
+                    lhs, lhs_sc = wi_w[:, u * 2 * P:(u + 1) * 2 * P].bitcast(FP4X4), wi_sc[:, u * P:(u + 1) * P]
+                    rhs, rhs_sc = v2_w[:, js], v2_sc[:, js]
+                else:
+                    codes, scales = we_q[kind, g]
+                    lhs, lhs_sc = codes[:, t * P:(t + 1) * P].bitcast(FP8X4), scales[:, t * P:(t + 1) * P]
+                    rhs, rhs_sc = v_w[kind][:, js], v_sc[TAB_FIRST + 4 * kind:, js]
+                nc.tensor.matmul_mx(out=bank[:, t, :], lhsT=lhs, lhsT_scale=lhs_sc, rhs=rhs.bitcast(FP8X4),
+                                    rhs_scale=rhs_sc, start=(start and t == 0), stop=(stop and t == PACK - 1))
+
+        def drain(bank, g, sub):
+            half, c = divmod(sub * SUB, HALF)
+            woven = bank[:].rearrange("p t j -> p j t")
+            nc.scalar.activation(out=sig[g, half][:, c:c + SUB, :], in_=woven, func=ACT.Sigmoid, bias=zero[:])
+            n, c = divmod(sub * SUB, QUARTER)
+            nc.vector.tensor_tensor(out=lin[g, n][:, c:c + SUB, :], in0=woven,
+                                    in1=ng[:, g:g + 1, :].to_broadcast([P, SUB, PACK]), op=ALU.mult)
 
         subs = S // SUB
         banks = [psum.tile([P, PACK, SUB], F32, name="bank", tag="bank") for sub in range(subs)]
@@ -193,19 +200,22 @@ def tile_list_cortical_softplus_currents_kernel(
                 drive(banks[sub], kind, 0, sub, kind == 2, kind == 1)
         for sub in range(subs):
             drain(banks[sub], 0, sub)
+        we_q[1, 1] = quantise_we(1, 1, round_we(1, 1, [(nc.gpsimd, 0, SPLIT), (nc.scalar, SPLIT, P)]), 1)
 
         banks = [psum.tile([P, PACK, SUB], F32, name="bank", tag="bank") for sub in range(subs)]
         for sub in range(subs):
-            for kind in (2, 0, 1):
-                drive(banks[sub], kind, 1, sub, kind == 2, kind == 1)
+            kinds = (2, 0, 1) if sub < subs // 2 else (2, 1, 0)
+            for kind in kinds:
+                drive(banks[sub], kind, 1, sub, kind == kinds[0], kind == kinds[-1])
         for sub in range(subs):
             drain(banks[sub], 1, sub)
 
-        wr_sc = held([P, N], U8, "v2_sc")
-        deal(wr_sc[:], wr_sc_raw[:], 16)
-        wr_w = [held([P, N], I32, name) for name in ("v2_w", "v_w_0")]
+        wr_dealt = held([P, 2 * N + N // 4], I32, "we_bf_1_1")
+        wr_w = [wr_dealt[:, a * N:(a + 1) * N] for a in range(2)]
+        wr_sc = wr_dealt[:, 2 * N:].bitcast(U8)
+        deal(wr_sc, wr_sc_raw[:], 16)
         for a in range(2):
-            deal(wr_w[a][:], wr_raw[a][:], 4)
+            deal(wr_w[a], wr_raw[a][:], 4)
 
         floor = keep.tile([P, 1], F32, name="floor", tag="bias")
         nc.gpsimd.memset(floor[:], FLOOR)
@@ -221,20 +231,18 @@ def tile_list_cortical_softplus_currents_kernel(
         def logs(first, width):
             half, c = divmod(first, HALF)
             for g in range(2):
-                part = sig[g, half][:, :, c:c + width]
+                part = sig[g, half][:, c:c + width, :]
                 nc.scalar.activation(out=part, in_=part, func=ACT.Ln, bias=floor[:])
 
         def rates(first, width):
             h = ring.tile([P, 2, width, PACK], BF16, name="h", bufs=3, align_bytes=64)
             half, c = divmod(first, HALF)
-            flat = ring.tile([P, 2, PACK, width], BF16, name="h_flat", bufs=3, align_bytes=64)
-            for u in range(2 * PACK):
-                g, t = divmod(u, PACK)
-                nc.vector.scalar_tensor_tensor(
-                    out=flat[:, g, t, :], in0=sig[g, half][:, t, c:c + width], scalar=neg_gain[:, u:u + 1],
-                    in1=lin[g, half][:, t, c:c + width], op0=ALU.mult, op1=ALU.max)
             for g in range(2):
-                weave(h[:, g], flat[:, g])
+                nc.vector.tensor_tensor(out=h[:, g], in0=sig[g, half][:, c:c + width, :],
+                                        in1=ng[:, g:g + 1, :].to_broadcast([P, width, PACK]), op=ALU.mult)
+            n, c = divmod(first, QUARTER)
+            for g in range(2):
+                nc.vector.tensor_tensor(out=h[:, g], in0=h[:, g], in1=lin[g, n][:, c:c + width, :], op=ALU.max)
             codes = held([P, 2, width], U32, "h_codes_%d" % first)
             scales = held([P, 2, width], U8, "h_scales_%d" % first)
             nc.vector.quantize_mx(out=codes[:].rearrange("p g c -> p (g c)").bitcast(FP8X4),
@@ -246,6 +254,13 @@ def tile_list_cortical_softplus_currents_kernel(
             for g in range(2):
                 rows = out_0[g * GROUP:(g + 1) * GROUP, js].rearrange("(p t) j -> p t j", t=PACK)
                 nc.sync.dma_start(out=rows, in_=ys[g][:, :, js])
+
+        late = []
+
+        def weave_banks():
+            for dst, src in late:
+                nc.scalar.copy(out=dst, in_=src)
+            late.clear()
 
         def currents(h_q, first, width):
             for c in range(0, width, SUB):
@@ -263,22 +278,18 @@ def tile_list_cortical_softplus_currents_kernel(
                                 lhsT_scale=wr_sc[WR_FIRST + 4 * a:, u * P:(u + 1) * P],
                                 rhs=codes[:, cols].bitcast(FP8X4), rhs_scale=scales[:, cols],
                                 start=(a == 0), stop=(a == 1))
-                    if sub == S // SUB - 1:
-                        nc.vector.tensor_copy(out=woven[g][:, js, :], in_=bank[:].rearrange("p t c -> p c t"))
                     nc.scalar.copy(out=ys[g][:, :, js], in_=bank[:])
-                    if FROM_SBUF <= sub < S // SUB - 1:
-                        nc.scalar.copy(out=woven[g][:, js, :], in_=bank[:].rearrange("p t c -> p c t"))
-                if first >= HALF:
-                    store_currents(js)
-            if first < HALF:
-                store_currents(slice(first, first + width))
+                    if sub in FROM_PSUM:
+                        late.append((woven[g][:, js, :], bank[:].rearrange("p t c -> p c t")))
+            store_currents(slice(first, first + width))
 
         def planes(first, width):
             js = slice(first, first + width)
-            last = min(first + width, FROM_SBUF * SUB)
+            rest = [sub for sub in range(first // SUB, (first + width) // SUB) if sub not in FROM_PSUM]
             for g in range(2):
-                if first < last:
-                    weave(woven[g][:, first:last, :], ys[g][:, :, first:last])
+                if rest:
+                    cols = slice(rest[0] * SUB, (rest[-1] + 1) * SUB)
+                    weave(woven[g][:, cols, :], ys[g][:, :, cols])
             for g in range(2):
                 nc.vector.quantize_mx(out=y_codes[:, g, js].bitcast(FP8X4), scales=y_scales[:, g, js],
                                       in_=woven[g][:, js, :].rearrange("p c t -> p (c t)"))
@@ -294,22 +305,24 @@ def tile_list_cortical_softplus_currents_kernel(
 
         count = len(CHUNKS)
         firsts = [sum(CHUNKS[:n]) for n in range(count)]
-        h_q = []
-        for n in range(AHEAD):
+        h_q = {}
+        for n in range(AHEAD - 1):
             logs(firsts[n], CHUNKS[n])
-        for n in range(AHEAD):
-            h_q.append(rates(firsts[n], CHUNKS[n]))
-        for n in range(count - AHEAD):
-            currents(h_q[n], firsts[n], CHUNKS[n])
-        for n in range(AHEAD, count):
-            logs(firsts[n], CHUNKS[n])
-        for n in range(AHEAD, count):
-            if n == count - 1:
-                planes(0, firsts[count - AHEAD])
-            h_q.append(rates(firsts[n], CHUNKS[n]))
-        for n in range(count - AHEAD, count):
-            currents(h_q[n], firsts[n], CHUNKS[n])
-            if n == count - 2:
-                store_scales(0, firsts[n])
-            planes(firsts[n], CHUNKS[n])
+        for n in range(count):
+            h_q[n] = rates(firsts[n], CHUNKS[n])
+            if n < count - 2:
+                currents(h_q[n], firsts[n], CHUNKS[n])
+                weave_banks()
+            if n + AHEAD - 1 < count:
+                logs(firsts[n + AHEAD - 1], CHUNKS[n + AHEAD - 1])
+            if n == EARLY:
+                planes(0, firsts[2])
+        currents(h_q[count - 2], firsts[-2], CHUNKS[-2])
+        planes(firsts[2], CHUNKS[2])
+        currents(h_q[count - 1], firsts[-1], CHUNKS[-1])
+        weave_banks()
+        planes(firsts[3], CHUNKS[3])
+        store_scales(0, firsts[-2])
+        planes(firsts[-2], CHUNKS[-2])
+        planes(firsts[-1], CHUNKS[-1])
         store_scales(firsts[-2], S)

@@ -20,11 +20,10 @@ T, T2, S, H, N = 4096, 2048, 1024, 1024, 1024
 HALF = 512
 QUARTER = 256
 SUB = 128
-CHUNKS = (128, 128, 256, 256, 128, 128)
-SPLIT = 64
+CHUNKS = (128, 128, 128, 128, 128, 128, 128, 128)
 EARLY = 3
 AHEAD = 4
-FROM_PSUM = (3, 6, 7)
+FROM_PSUM = (2, 3, 4)
 TAB_FIRST = 4
 WR_FIRST = 8
 FLOOR = 2.0 ** -60
@@ -106,119 +105,120 @@ def tile_list_cortical_softplus_currents_kernel(
         for a in range(2):
             load_words(wr_raw[a], wr_words[a], 0, N)
 
-        def gather_words(table, offsets, name):
-            picked = held([P, S], U32, name)
+        def gather_words(table, offsets, names):
+            picked = [held([P, HALF], U32, name) for name in names]
             cols = HALF // 16
             for half in range(2):
-                nc.vector.tensor_copy(picked[:, half * HALF:(half + 1) * HALF],
+                nc.vector.tensor_copy(picked[half][:],
                                       table[:].bitcast(U32).indirect(offsets[:, half * cols:(half + 1) * cols]))
             return picked
 
-        def deal(dealt, raw, run):
-            nc.vector.tensor_copy(
+        def deal(engine, dealt, raw, run):
+            engine.tensor_copy(
                 out=dealt.rearrange("p (g t c i) -> p g c t i", g=2, t=PACK, i=run),
                 in_=raw.rearrange("p (g c i t) -> p g c t i", g=2, t=PACK, i=run),
             )
 
-        def we_views(a, g):
-            dealt = held([P, PACK, P, PACK], BF16, "we_bf_%d_%d" % (a, g))
+        def round_we(engine, a, g, first, last, name):
+            dealt = held([P, last - first, P, PACK], BF16, name)
             dst = dealt[:].rearrange("p t m i -> p m t i")
-            src = we_raw[a, g][:].rearrange("p i (m t) -> p m t i", t=PACK)
-            return dealt, dst, src
+            src = we_raw[a, g][:].rearrange("p i (m t) -> p m t i", t=PACK)[:, :, first:last, :]
+            if engine is nc.scalar:
+                engine.activation(out=dst, in_=src, func=ACT.Copy, scale=-1.0)
+            else:
+                engine.tensor_scalar(out=dst, in0=src, scalar1=-1.0, scalar2=0.0, op0=ALU.mult, op1=ALU.add)
+            return dealt[:].rearrange("p t m i -> p (t m i)")
 
-        def round_we(a, g, shares):
-            dealt, dst, src = we_views(a, g)
-            for engine, first, last in shares:
-                if engine is nc.scalar:
-                    engine.activation(out=dst[:, first:last], in_=src[:, first:last], func=ACT.Copy, scale=-1.0)
-                else:
-                    engine.tensor_scalar(out=dst[:, first:last], in0=src[:, first:last], scalar1=-1.0, scalar2=0.0,
-                                         op0=ALU.mult, op1=ALU.add)
-            return dealt
+        def quantise_we(rounded, name):
+            width = rounded.shape[1] // PACK
+            codes = held([P, width], U32, name)
+            scales = held([P, width], U8, "scales_%d" % len(scale_tiles))
+            scale_tiles.append(scales)
+            nc.vector.quantize_mx(out=codes[:].bitcast(FP8X4), scales=scales[:], in_=rounded)
+            return [(codes[:, c:c + P], scales[:, c:c + P]) for c in range(0, width, P)]
 
-        def quantise_we(a, g, dealt, parts):
-            codes = held([P, GROUP], U32, "tab_sc" if (a, g) == (0, 0) else "we_codes_%d_%d" % (a, g))
-            scales = held([P, GROUP], U8, "we_scales_%d_%d" % (a, g))
-            flat = dealt[:].rearrange("p t m i -> p (t m i)")
-            step = GROUP // parts
-            for c in range(0, GROUP, step):
-                nc.vector.quantize_mx(out=codes[:, c:c + step].bitcast(FP8X4), scales=scales[:, c:c + step],
-                                      in_=flat[:, PACK * c:PACK * (c + step)])
-            return codes, scales
-
-        v2_w = gather_words(tab2_w, idx2, "v2_w")
+        scale_tiles = []
+        v2_w = gather_words(tab2_w, idx2, ("v2_w_0", "v2_w_1"))
         v2_sc = held([P, S], U8, "v2_sc")
         nc.vector.tensor_copy(v2_sc[:], tab2_sc[:].indirect(idx2[:]))
         wi_w = held([P, 2 * H], U8, "wi_w")
-        deal(wi_w[:].bitcast(U16), wi_raw[:].bitcast(U16), 8)
+        deal(nc.vector, wi_w[:].bitcast(U16), wi_raw[:].bitcast(U16), 8)
         wi_sc = held([P, H], U8, "wi_sc")
-        deal(wi_sc[:], wi_sc_raw[:], 16)
-        v_w = [gather_words(tab_w[0], idx, "v_w_0")]
+        deal(nc.vector, wi_sc[:], wi_sc_raw[:], 16)
+        v_w = [gather_words(tab_w[0], idx, ("v_w_0_0", "v_w_0_1"))]
         v_sc = held([P, S], U8, "v_sc")
         nc.vector.tensor_copy(v_sc[:], tab_sc[:].indirect(idx[:]))
         we_q = {}
-        for a in range(2):
-            we_q[a, 0] = quantise_we(a, 0, round_we(a, 0, [(nc.scalar, 0, P)]), 1)
+        we_q[0, 0] = quantise_we(round_we(nc.scalar, 0, 0, 0, PACK, "slot_a"), "tab_sc")
+        we_q[1, 0] = quantise_we(round_we(nc.scalar, 1, 0, 0, PACK, "slot_b"), "slot_a")
         neg_gain = held([P, 2 * PACK], F32, "neg_gain")
         nc.vector.tensor_scalar(out=neg_gain[:], in0=gain_sb[:].rearrange("p g t -> p (g t)"),
                                 scalar1=-1.0, scalar2=None, op0=ALU.mult)
-        v_w.append(gather_words(tab_w[1], idx, "v_w_1"))
+        v_w.append(gather_words(tab_w[1], idx, ("slot_b", "v_w_1_1")))
 
-        we_q[0, 1] = quantise_we(0, 1, round_we(0, 1, [(nc.gpsimd, 0, P)]), 1)
+        we_q[0, 1] = quantise_we(round_we(nc.gpsimd, 0, 1, 0, PACK, "we_bf_0_1"), "we_codes_0_1")
+        we_q[1, 1] = quantise_we(round_we(nc.vector, 1, 1, 0, 2, "we_bf_0_1"), "we_codes_1_1_a")
 
-        sig = {(g, half): held([P, HALF, PACK], F32, "sig_%d_%d" % (g, half) if half else "we_raw_%d_0" % g) for g in range(2) for half in range(2)}
-        lin = {(g, n): held([P, QUARTER, PACK], BF16, "we_bf_0_1" if (g, n) == (0, 3) else "lin_%d_%d" % (g, n))
+        sig = {(g, half): held([P, HALF // 2, PACK, 2], F32, "sig_%d_%d" % (g, half) if half else "we_raw_%d_0" % g) for g in range(2) for half in range(2)}
+        lin = {(g, n): held([P, 2, QUARTER, 2], BF16, "we_bf_0_1" if (g, n) == (0, 2) else "lin_%d_%d" % (g, n))
                for g in range(2) for n in range(S // QUARTER)}
         ng = neg_gain[:].rearrange("p (g t) -> p g t", g=2)
 
-        def drive(bank, kind, g, sub, start, stop):
-            js = slice(sub * SUB, (sub + 1) * SUB)
-            for t in range(PACK):
+        def drive(bank, kind, g, pair, n):
+            half, c = divmod(n * QUARTER, HALF)
+            width = SUB if kind == 2 else QUARTER
+            for e in range(2):
+                t = 2 * pair + e
                 u = g * PACK + t
-                if kind == 2:
-                    lhs, lhs_sc = wi_w[:, u * 2 * P:(u + 1) * 2 * P].bitcast(FP4X4), wi_sc[:, u * P:(u + 1) * P]
-                    rhs, rhs_sc = v2_w[:, js], v2_sc[:, js]
-                else:
-                    codes, scales = we_q[kind, g]
-                    lhs, lhs_sc = codes[:, t * P:(t + 1) * P].bitcast(FP8X4), scales[:, t * P:(t + 1) * P]
-                    rhs, rhs_sc = v_w[kind][:, js], v_sc[TAB_FIRST + 4 * kind:, js]
-                nc.tensor.matmul_mx(out=bank[:, t, :], lhsT=lhs, lhsT_scale=lhs_sc, rhs=rhs.bitcast(FP8X4),
-                                    rhs_scale=rhs_sc, start=(start and t == 0), stop=(stop and t == PACK - 1))
+                for first in range(0, QUARTER, width):
+                    cols = slice(c + first, c + first + width)
+                    js = slice(n * QUARTER + first, n * QUARTER + first + width)
+                    if kind == 2:
+                        lhs, lhs_sc = wi_w[:, u * 2 * P:(u + 1) * 2 * P].bitcast(FP4X4), wi_sc[:, u * P:(u + 1) * P]
+                        rhs, rhs_sc = v2_w[half][:, cols], v2_sc[:, js]
+                    else:
+                        codes, lhs_sc = we_q[kind, g][t]
+                        lhs = codes.bitcast(FP8X4)
+                        rhs, rhs_sc = v_w[kind][half][:, cols], v_sc[TAB_FIRST + 4 * kind:, js]
+                    nc.tensor.matmul_mx(out=bank[:, e, first:first + width], lhsT=lhs, lhsT_scale=lhs_sc,
+                                        rhs=rhs.bitcast(FP8X4), rhs_scale=rhs_sc,
+                                        start=(kind == 2 and e == 0 and first == 0), stop=(kind == 1 and e == 1))
 
-        def drain(bank, g, sub):
-            half, c = divmod(sub * SUB, HALF)
-            woven = bank[:].rearrange("p t j -> p j t")
-            nc.scalar.activation(out=sig[g, half][:, c:c + SUB, :], in_=woven, func=ACT.Sigmoid, bias=zero[:])
-            n, c = divmod(sub * SUB, QUARTER)
-            nc.vector.tensor_tensor(out=lin[g, n][:, c:c + SUB, :], in0=woven,
-                                    in1=ng[:, g:g + 1, :].to_broadcast([P, SUB, PACK]), op=ALU.mult)
+        def drain(bank, g, pair, n):
+            half, c = divmod(n * QUARTER, HALF)
+            ts = slice(2 * pair, 2 * pair + 2)
+            nc.scalar.activation(out=sig[g, half][:, c // 2:(c + QUARTER) // 2, ts, :],
+                                 in_=bank[:].rearrange("p e (c i) -> p c e i", i=2), func=ACT.Sigmoid, bias=zero[:])
+            nc.vector.tensor_tensor(out=lin[g, n][:, pair], in0=bank[:].rearrange("p e j -> p j e"),
+                                    in1=ng[:, g:g + 1, ts].to_broadcast([P, QUARTER, 2]), op=ALU.mult)
 
-        subs = S // SUB
-        banks = [psum.tile([P, PACK, SUB], F32, name="bank", tag="bank") for sub in range(subs)]
+        quarters = S // QUARTER
+        units = [(pair, n) for n in range(quarters) for pair in range(2)]
+        banks = [psum.tile([P, 2, QUARTER], F32, name="bank", tag="bank") for unit in units]
         for kind in (2, 0, 1):
-            for sub in range(subs):
-                drive(banks[sub], kind, 0, sub, kind == 2, kind == 1)
-        for sub in range(subs):
-            drain(banks[sub], 0, sub)
-        we_q[1, 1] = quantise_we(1, 1, round_we(1, 1, [(nc.gpsimd, 0, SPLIT), (nc.scalar, SPLIT, P)]), 1)
+            for bank, (pair, n) in zip(banks, units):
+                drive(bank, kind, 0, pair, n)
+        for bank, (pair, n) in zip(banks, units):
+            drain(bank, 0, pair, n)
+        we_q[1, 1].extend(quantise_we(round_we(nc.scalar, 1, 1, 2, PACK, "slot_a"), "we_codes_1_1_b"))
 
-        banks = [psum.tile([P, PACK, SUB], F32, name="bank", tag="bank") for sub in range(subs)]
-        for sub in range(subs):
-            kinds = (2, 0, 1) if sub < subs // 2 else (2, 1, 0)
-            for kind in kinds:
-                drive(banks[sub], kind, 1, sub, kind == kinds[0], kind == kinds[-1])
-        for sub in range(subs):
-            drain(banks[sub], 1, sub)
+        units = [(pair, n) for pair in range(2) for n in range(quarters)]
+        banks = [psum.tile([P, 2, QUARTER], F32, name="bank", tag="bank") for unit in units]
+        for bank, (pair, n) in zip(banks, units):
+            for kind in (2, 0, 1):
+                drive(bank, kind, 1, pair, n)
+        for bank, (pair, n) in zip(banks, units):
+            drain(bank, 1, pair, n)
 
-        wr_dealt = held([P, 2 * N + N // 4], I32, "we_bf_1_1")
+        wr_dealt = held([P, 2 * N + N // 4], I32, "slot_a")
         wr_w = [wr_dealt[:, a * N:(a + 1) * N] for a in range(2)]
         wr_sc = wr_dealt[:, 2 * N:].bitcast(U8)
-        deal(wr_sc, wr_sc_raw[:], 16)
+        deal(nc.gpsimd, wr_sc, wr_sc_raw[:], 16)
         for a in range(2):
-            deal(wr_w[a], wr_raw[a][:], 4)
+            deal(nc.gpsimd, wr_w[a], wr_raw[a][:], 4)
 
         floor = keep.tile([P, 1], F32, name="floor", tag="bias")
-        nc.gpsimd.memset(floor[:], FLOOR)
+        nc.vector.memset(floor[:], FLOOR)
         ys = [held([P, PACK, S], F32, "tab_w_%d" % g) for g in range(2)]
         woven = [held([P, S, PACK], BF16, "y_woven_%d" % g) for g in range(2)]
         y_codes = held([P, 2, S], I32, "y_codes")
@@ -231,18 +231,22 @@ def tile_list_cortical_softplus_currents_kernel(
         def logs(first, width):
             half, c = divmod(first, HALF)
             for g in range(2):
-                part = sig[g, half][:, c:c + width, :]
+                part = sig[g, half][:, c // 2:(c + width) // 2]
                 nc.scalar.activation(out=part, in_=part, func=ACT.Ln, bias=floor[:])
 
         def rates(first, width):
             h = ring.tile([P, 2, width, PACK], BF16, name="h", bufs=3, align_bytes=64)
             half, c = divmod(first, HALF)
             for g in range(2):
-                nc.vector.tensor_tensor(out=h[:, g], in0=sig[g, half][:, c:c + width, :],
-                                        in1=ng[:, g:g + 1, :].to_broadcast([P, width, PACK]), op=ALU.mult)
+                nc.vector.tensor_tensor(out=h[:, g].rearrange("p (c i) t -> p c i t", i=2),
+                                        in0=sig[g, half][:, c // 2:(c + width) // 2].rearrange("p c t i -> p c i t"),
+                                        in1=ng[:, g:g + 1, :].unsqueeze(2).to_broadcast([P, width // 2, 2, PACK]),
+                                        op=ALU.mult)
             n, c = divmod(first, QUARTER)
             for g in range(2):
-                nc.vector.tensor_tensor(out=h[:, g], in0=h[:, g], in1=lin[g, n][:, c:c + width, :], op=ALU.max)
+                pairs = h[:, g].rearrange("p j (a e) -> p j a e", e=2)
+                nc.vector.tensor_tensor(out=pairs, in0=pairs,
+                                        in1=lin[g, n][:, :, c:c + width, :].rearrange("p a j e -> p j a e"), op=ALU.max)
             codes = held([P, 2, width], U32, "h_codes_%d" % first)
             scales = held([P, 2, width], U8, "h_scales_%d" % first)
             nc.vector.quantize_mx(out=codes[:].rearrange("p g c -> p (g c)").bitcast(FP8X4),
@@ -255,12 +259,12 @@ def tile_list_cortical_softplus_currents_kernel(
                 rows = out_0[g * GROUP:(g + 1) * GROUP, js].rearrange("(p t) j -> p t j", t=PACK)
                 nc.sync.dma_start(out=rows, in_=ys[g][:, :, js])
 
-        late = []
+        held_banks = {}
 
-        def weave_banks():
-            for dst, src in late:
-                nc.scalar.copy(out=dst, in_=src)
-            late.clear()
+        def weave_banks(sub):
+            for g in range(2):
+                nc.scalar.copy(out=woven[g][:, sub * SUB:(sub + 1) * SUB, :],
+                               in_=held_banks[sub, g][:].rearrange("p t c -> p c t"))
 
         def currents(h_q, first, width):
             for c in range(0, width, SUB):
@@ -279,8 +283,7 @@ def tile_list_cortical_softplus_currents_kernel(
                                 rhs=codes[:, cols].bitcast(FP8X4), rhs_scale=scales[:, cols],
                                 start=(a == 0), stop=(a == 1))
                     nc.scalar.copy(out=ys[g][:, :, js], in_=bank[:])
-                    if sub in FROM_PSUM:
-                        late.append((woven[g][:, js, :], bank[:].rearrange("p t c -> p c t")))
+                    held_banks[sub, g] = bank
             store_currents(slice(first, first + width))
 
         def planes(first, width):
@@ -293,8 +296,10 @@ def tile_list_cortical_softplus_currents_kernel(
             for g in range(2):
                 nc.vector.quantize_mx(out=y_codes[:, g, js].bitcast(FP8X4), scales=y_scales[:, g, js],
                                       in_=woven[g][:, js, :].rearrange("p c t -> p (c t)"))
+
+        def store_words(first, last):
             words = out_1.rearrange("g p j t -> p g (j t)").bitcast(I32)
-            nc.sync.dma_start(out=words[:, :, js], in_=y_codes[:, :, js])
+            nc.sync.dma_start(out=words[:, :, first:last], in_=y_codes[:, :, first:last])
 
         def store_scales(first, last):
             cols = slice(first // 4, last // 4)
@@ -306,23 +311,24 @@ def tile_list_cortical_softplus_currents_kernel(
         count = len(CHUNKS)
         firsts = [sum(CHUNKS[:n]) for n in range(count)]
         h_q = {}
-        for n in range(AHEAD - 1):
-            logs(firsts[n], CHUNKS[n])
+        for n in range(AHEAD):
+            logs(firsts[n], SUB)
         for n in range(count):
-            h_q[n] = rates(firsts[n], CHUNKS[n])
-            if n < count - 2:
-                currents(h_q[n], firsts[n], CHUNKS[n])
-                weave_banks()
-            if n + AHEAD - 1 < count:
-                logs(firsts[n + AHEAD - 1], CHUNKS[n + AHEAD - 1])
-            if n == EARLY:
-                planes(0, firsts[2])
-        currents(h_q[count - 2], firsts[-2], CHUNKS[-2])
-        planes(firsts[2], CHUNKS[2])
-        currents(h_q[count - 1], firsts[-1], CHUNKS[-1])
-        weave_banks()
-        planes(firsts[3], CHUNKS[3])
-        store_scales(0, firsts[-2])
-        planes(firsts[-2], CHUNKS[-2])
-        planes(firsts[-1], CHUNKS[-1])
-        store_scales(firsts[-2], S)
+            h_q[n] = rates(firsts[n], SUB)
+            currents(h_q[n], firsts[n], SUB)
+            if n + AHEAD < count:
+                logs(firsts[n + AHEAD], SUB)
+            if n - 2 in FROM_PSUM:
+                weave_banks(n - 2)
+            if n - EARLY in (0, 1):
+                planes(firsts[n - EARLY], SUB)
+            if n - EARLY == 1:
+                store_words(0, firsts[2])
+        planes(firsts[2], 2 * SUB)
+        store_words(firsts[2], firsts[4])
+        for n in (5, 6, 4):
+            planes(firsts[n], SUB)
+        store_words(firsts[4], firsts[-1])
+        planes(firsts[-1], SUB)
+        store_words(firsts[-1], S)
+        store_scales(0, S)

@@ -57,8 +57,6 @@ def tile_list_cortical_softplus_currents_kernel(
         nc.vector.memset(tab2_sc[:].bitcast(I32), 0)
         nc.vector.memset(wi_sc_raw[:].bitcast(I32), 0)
         nc.vector.memset(wr_sc_raw[:].bitcast(I32), 0)
-        warm = held([P, 1], F32, "warm")
-        nc.scalar.activation(out=warm[:], in_=zero[:], func=ACT.Sigmoid)
 
         def load_we(a, g, first=0, last=PACK):
             rows = we[a * GROUP:(a + 1) * GROUP, g * GROUP:(g + 1) * GROUP].rearrange("(p i) c -> p i c", i=PACK)

@@ -20,10 +20,10 @@ T, T2, S, H, N = 4096, 2048, 1024, 1024, 1024
 HALF = 512
 QUARTER = 256
 SUB = 128
-CHUNKS = (128, 128, 128, 128, 128, 128, 128, 128)
+SPAN = 2 * SUB * PACK
 EARLY = 3
 AHEAD = 4
-FROM_PSUM = (2, 3, 4)
+FROM_PSUM = (2, 3)
 TAB_FIRST = 4
 WR_FIRST = 8
 FLOOR = 2.0 ** -60
@@ -149,18 +149,17 @@ def tile_list_cortical_softplus_currents_kernel(
         we_q = {}
         we_q[0, 0] = quantise_we(round_we(nc.scalar, 0, 0, 0, PACK, "slot_a"), "tab_sc")
         we_q[1, 0] = quantise_we(round_we(nc.scalar, 1, 0, 0, PACK, "slot_b"), "slot_a")
-        neg_gain = held([P, 2 * PACK], F32, "neg_gain")
-        nc.vector.tensor_scalar(out=neg_gain[:], in0=gain_sb[:].rearrange("p g t -> p (g t)"),
+        neg_gain = held([P, 2, 2, PACK], F32, "neg_gain")
+        nc.vector.tensor_scalar(out=neg_gain[:], in0=gain_sb[:].unsqueeze(2).to_broadcast([P, 2, 2, PACK]),
                                 scalar1=-1.0, scalar2=None, op0=ALU.mult)
         v_w.append(gather_words(tab_w[1], idx, ("slot_b", "v_w_1_1")))
 
         we_q[0, 1] = quantise_we(round_we(nc.gpsimd, 0, 1, 0, PACK, "we_bf_0_1"), "we_codes_0_1")
         we_q[1, 1] = quantise_we(round_we(nc.vector, 1, 1, 0, 2, "we_bf_0_1"), "we_codes_1_1_a")
 
-        sig = {(g, half): held([P, HALF // 2, PACK, 2], F32, "sig_%d_%d" % (g, half) if half else "we_raw_%d_0" % g) for g in range(2) for half in range(2)}
-        lin = {(g, n): held([P, 2, QUARTER, 2], BF16, "we_bf_0_1" if (g, n) == (0, 2) else "lin_%d_%d" % (g, n))
-               for g in range(2) for n in range(S // QUARTER)}
-        ng = neg_gain[:].rearrange("p (g t) -> p g t", g=2)
+        sig = [held([P, 2 * SPAN], F32, "sig_%d" % n if n > 1 else "we_raw_%d_0" % n) for n in range(S // QUARTER)]
+        lin = [held([P, 2 * SPAN], BF16, "we_bf_0_1" if n == 2 else "lin_%d" % n) for n in range(S // QUARTER)]
+        ng = neg_gain[:, :, 0, :]
 
         def drive(bank, kind, g, pair, n):
             half, c = divmod(n * QUARTER, HALF)
@@ -183,12 +182,13 @@ def tile_list_cortical_softplus_currents_kernel(
                                         start=(kind == 2 and e == 0 and first == 0), stop=(kind == 1 and e == 1))
 
         def drain(bank, g, pair, n):
-            half, c = divmod(n * QUARTER, HALF)
             ts = slice(2 * pair, 2 * pair + 2)
-            nc.scalar.activation(out=sig[g, half][:, c // 2:(c + QUARTER) // 2, ts, :],
-                                 in_=bank[:].rearrange("p e (c i) -> p c e i", i=2), func=ACT.Sigmoid, bias=zero[:])
-            nc.vector.tensor_tensor(out=lin[g, n][:, pair], in0=bank[:].rearrange("p e j -> p j e"),
-                                    in1=ng[:, g:g + 1, ts].to_broadcast([P, QUARTER, 2]), op=ALU.mult)
+            sig_out = sig[n][:].rearrange("p (k g c t i) -> p k g c t i", k=2, g=2, t=PACK, i=2)[:, :, g, :, ts, :]
+            nc.scalar.activation(out=sig_out, in_=bank[:].rearrange("p e (k c i) -> p k c e i", k=2, i=2),
+                                 func=ACT.Sigmoid, bias=zero[:])
+            lin_out = lin[n][:].rearrange("p (k a g j e) -> p k a g j e", k=2, a=2, g=2, e=2)[:, :, pair, g, :, :]
+            nc.vector.tensor_tensor(out=lin_out, in0=bank[:].rearrange("p e (k j) -> p k j e", k=2),
+                                    in1=ng[:, g:g + 1, ts].unsqueeze(1).to_broadcast([P, 2, SUB, 2]), op=ALU.mult)
 
         quarters = S // QUARTER
         units = [(pair, n) for n in range(quarters) for pair in range(2)]
@@ -217,116 +217,120 @@ def tile_list_cortical_softplus_currents_kernel(
 
         floor = keep.tile([P, 1], F32, name="floor", tag="bias")
         nc.vector.memset(floor[:], FLOOR)
-        ys = [held([P, PACK, S], F32, "tab_w_%d" % g) for g in range(2)]
-        woven = [held([P, S, PACK], BF16, "y_woven_%d" % g) for g in range(2)]
+        ys = [held([P, 4, 2, PACK, SUB], F32, "tab_w_%d" % half) for half in range(2)]
+        woven = held([P, 2, S, PACK], BF16, "y_woven")
         y_codes = held([P, 2, S], I32, "y_codes")
         y_scales = held([P, 2, S], U8, "y_scales")
+        both, apart = (slice(0, 2),), (slice(0, 1), slice(1, 2))
+        count = S // SUB
+        h, h_codes, h_scales, y_banks = {}, {}, {}, {}
 
-        def weave(woven, flat):
-            nc.vector.tensor_copy(out=woven.rearrange("p (c i) t -> p c t i", i=4),
-                                  in_=flat.rearrange("p t (c i) -> p c t i", i=4))
+        def stretch(tiles, n):
+            return tiles[n // 2][:, (n % 2) * SPAN:(n % 2 + 1) * SPAN]
 
-        def logs(first, width):
-            half, c = divmod(first, HALF)
-            for g in range(2):
-                part = sig[g, half][:, c // 2:(c + width) // 2]
+        def logs(n, parts):
+            for gs in parts:
+                part = stretch(sig, n).rearrange("p (g c) -> p g c", g=2)[:, gs]
                 nc.scalar.activation(out=part, in_=part, func=ACT.Ln, bias=floor[:])
 
-        def rates(first, width):
-            h = ring.tile([P, 2, width, PACK], BF16, name="h", bufs=3, align_bytes=64)
-            half, c = divmod(first, HALF)
-            for g in range(2):
-                nc.vector.tensor_tensor(out=h[:, g].rearrange("p (c i) t -> p c i t", i=2),
-                                        in0=sig[g, half][:, c // 2:(c + width) // 2].rearrange("p c t i -> p c i t"),
-                                        in1=ng[:, g:g + 1, :].unsqueeze(2).to_broadcast([P, width // 2, 2, PACK]),
+        def products(n, parts):
+            h[n] = ring.tile([P, SPAN], BF16, name="h", bufs=3, align_bytes=64)
+            for gs in parts:
+                src = stretch(sig, n).rearrange("p (g c t i) -> p g c i t", g=2, t=PACK, i=2)[:, gs]
+                nc.vector.tensor_tensor(out=h[n][:].rearrange("p (g c i t) -> p g c i t", g=2, t=PACK, i=2)[:, gs],
+                                        in0=src, in1=neg_gain[:, gs].unsqueeze(2).to_broadcast(src.shape),
                                         op=ALU.mult)
-            n, c = divmod(first, QUARTER)
+
+        def maxima(n, parts):
+            for gs in parts:
+                pairs = h[n][:].rearrange("p (g j a e) -> p g j a e", g=2, a=2, e=2)[:, gs]
+                other = stretch(lin, n).rearrange("p (a g j e) -> p g j a e", a=2, g=2, e=2)[:, gs]
+                nc.vector.tensor_tensor(out=pairs, in0=pairs, in1=other, op=ALU.max)
+
+        def quantise_h(n, parts):
+            h_codes[n] = held([P, 2 * SUB], U32, "h_codes_%d" % n)
+            h_scales[n] = held([P, 2 * SUB], U8, "h_scales_%d" % n)
+            for gs in parts:
+                cols = slice(gs.start * SUB, gs.stop * SUB)
+                nc.vector.quantize_mx(out=h_codes[n][:, cols].bitcast(FP8X4), scales=h_scales[n][:, cols],
+                                      in_=h[n][:, PACK * cols.start:PACK * cols.stop])
+
+        def currents(n):
             for g in range(2):
-                pairs = h[:, g].rearrange("p j (a e) -> p j a e", e=2)
-                nc.vector.tensor_tensor(out=pairs, in0=pairs,
-                                        in1=lin[g, n][:, :, c:c + width, :].rearrange("p a j e -> p j a e"), op=ALU.max)
-            codes = held([P, 2, width], U32, "h_codes_%d" % first)
-            scales = held([P, 2, width], U8, "h_scales_%d" % first)
-            nc.vector.quantize_mx(out=codes[:].rearrange("p g c -> p (g c)").bitcast(FP8X4),
-                                  scales=scales[:].rearrange("p g c -> p (g c)"),
-                                  in_=h[:].rearrange("p g c t -> p (g c t)"))
-            return [(codes[:, g, :], scales[:, g, :]) for g in range(2)]
-
-        def store_currents(js):
+                bank = psum.tile([P, PACK, SUB], F32, name="bank", tag="bank")
+                for t in range(PACK):
+                    u = g * PACK + t
+                    for a in range(2):
+                        nc.tensor.matmul_mx(
+                            out=bank[:, t, :], lhsT=wr_w[a][:, u * P:(u + 1) * P].bitcast(FP8X4),
+                            lhsT_scale=wr_sc[WR_FIRST + 4 * a:, u * P:(u + 1) * P],
+                            rhs=h_codes[n][:, a * SUB:(a + 1) * SUB].bitcast(FP8X4),
+                            rhs_scale=h_scales[n][:, a * SUB:(a + 1) * SUB], start=(a == 0), stop=(a == 1))
+                nc.scalar.copy(out=ys[n // 4][:, n % 4, g], in_=bank[:])
+                y_banks[n, g] = bank
             for g in range(2):
-                rows = out_0[g * GROUP:(g + 1) * GROUP, js].rearrange("(p t) j -> p t j", t=PACK)
-                nc.sync.dma_start(out=rows, in_=ys[g][:, :, js])
+                rows = out_0[g * GROUP:(g + 1) * GROUP, n * SUB:(n + 1) * SUB].rearrange("(p t) j -> p t j", t=PACK)
+                nc.sync.dma_start(out=rows, in_=ys[n // 4][:, n % 4, g])
 
-        held_banks = {}
-
-        def weave_banks(sub):
+        def weave_banks(n):
             for g in range(2):
-                nc.scalar.copy(out=woven[g][:, sub * SUB:(sub + 1) * SUB, :],
-                               in_=held_banks[sub, g][:].rearrange("p t c -> p c t"))
+                nc.scalar.copy(out=woven[:, g, n * SUB:(n + 1) * SUB, :], in_=y_banks[n, g][:].rearrange("p t c -> p c t"))
 
-        def currents(h_q, first, width):
-            for c in range(0, width, SUB):
-                cols = slice(c, c + SUB)
-                js = slice(first + c, first + c + SUB)
-                sub = (first + c) // SUB
-                for g in range(2):
-                    bank = psum.tile([P, PACK, SUB], F32, name="bank", tag="bank")
-                    for t in range(PACK):
-                        u = g * PACK + t
-                        for a in range(2):
-                            codes, scales = h_q[a]
-                            nc.tensor.matmul_mx(
-                                out=bank[:, t, :], lhsT=wr_w[a][:, u * P:(u + 1) * P].bitcast(FP8X4),
-                                lhsT_scale=wr_sc[WR_FIRST + 4 * a:, u * P:(u + 1) * P],
-                                rhs=codes[:, cols].bitcast(FP8X4), rhs_scale=scales[:, cols],
-                                start=(a == 0), stop=(a == 1))
-                    nc.scalar.copy(out=ys[g][:, :, js], in_=bank[:])
-                    held_banks[sub, g] = bank
-            store_currents(slice(first, first + width))
+        def weave(n, parts):
+            for gs in parts:
+                nc.vector.tensor_copy(
+                    out=woven[:, gs, n * SUB:(n + 1) * SUB, :].rearrange("p g (c i) t -> p g c t i", i=4),
+                    in_=ys[n // 4][:, n % 4, gs].rearrange("p g t (c i) -> p g c t i", i=4))
 
-        def planes(first, width):
-            js = slice(first, first + width)
-            rest = [sub for sub in range(first // SUB, (first + width) // SUB) if sub not in FROM_PSUM]
-            for g in range(2):
-                if rest:
-                    cols = slice(rest[0] * SUB, (rest[-1] + 1) * SUB)
-                    weave(woven[g][:, cols, :], ys[g][:, :, cols])
+        def quantise_y(first, last):
+            js = slice(first * SUB, last * SUB)
             for g in range(2):
                 nc.vector.quantize_mx(out=y_codes[:, g, js].bitcast(FP8X4), scales=y_scales[:, g, js],
-                                      in_=woven[g][:, js, :].rearrange("p c t -> p (c t)"))
+                                      in_=woven[:, g, js, :].rearrange("p c t -> p (c t)"))
 
         def store_words(first, last):
+            js = slice(first * SUB, last * SUB)
             words = out_1.rearrange("g p j t -> p g (j t)").bitcast(I32)
-            nc.sync.dma_start(out=words[:, :, first:last], in_=y_codes[:, :, first:last])
+            nc.sync.dma_start(out=words[:, :, js], in_=y_codes[:, :, js])
 
-        def store_scales(first, last):
-            cols = slice(first // 4, last // 4)
+        def store_scales():
             for r in range(4):
-                nc.sync.dma_start(
-                    out=out_2[:, r:16:4, :].bitcast(I32).rearrange("g q c -> q g c")[:, :, cols],
-                    in_=y_scales[r:P:32, :, :].bitcast(I32)[:, :, cols])
+                nc.sync.dma_start(out=out_2[:, r:16:4, :].bitcast(I32).rearrange("g q c -> q g c"),
+                                  in_=y_scales[r:P:32, :, :].bitcast(I32))
 
-        count = len(CHUNKS)
-        firsts = [sum(CHUNKS[:n]) for n in range(count)]
-        h_q = {}
-        for n in range(AHEAD):
-            logs(firsts[n], SUB)
+        logs(0, apart)
+        for n in range(1, AHEAD):
+            logs(n, both)
+        products(0, apart)
+        maxima(0, apart)
+        quantise_h(0, apart)
+        products(1, apart)
         for n in range(count):
-            h_q[n] = rates(firsts[n], SUB)
-            currents(h_q[n], firsts[n], SUB)
+            if n > 0:
+                maxima(n, apart if n == 1 else both)
+                if n + 1 < count:
+                    products(n + 1, both)
+                else:
+                    quantise_y(2, 4)
+                    store_words(2, 4)
+                quantise_h(n, both)
+            currents(n)
             if n + AHEAD < count:
-                logs(firsts[n + AHEAD], SUB)
+                logs(n + AHEAD, both)
             if n - 2 in FROM_PSUM:
                 weave_banks(n - 2)
             if n - EARLY in (0, 1):
-                planes(firsts[n - EARLY], SUB)
-            if n - EARLY == 1:
-                store_words(0, firsts[2])
-        planes(firsts[2], 2 * SUB)
-        store_words(firsts[2], firsts[4])
-        for n in (5, 6, 4):
-            planes(firsts[n], SUB)
-        store_words(firsts[4], firsts[-1])
-        planes(firsts[-1], SUB)
-        store_words(firsts[-1], S)
-        store_scales(0, S)
+                weave(n - EARLY, both)
+            if n - EARLY == 2:
+                quantise_y(0, 2)
+                store_words(0, 2)
+        weave(4, both)
+        weave(5, both)
+        weave(6, both)
+        quantise_y(4, 6)
+        quantise_y(6, 7)
+        store_words(4, 7)
+        weave(7, apart)
+        quantise_y(7, 8)
+        store_words(7, 8)
+        store_scales()

@@ -80,18 +80,17 @@ def tile_list_cortical_softplus_currents_kernel(
         tab_w = [held([P, T], I32, "tab_w_%d" % a) for a in range(2)]
         nc.sync.dma_start(idx2[:], offs2)
         load_words(tab2_w, tab2_words[0], 0, T2)
-        load_words(tab_w[0], tab_words[0], 0, T // 2)
+        load_we(0, 0)
         nc.sync.dma_start(idx[:], offs)
         load_plane(tab2_sc, tab2_scales[0], 0)
-        load_words(tab_w[0], tab_words[0], T // 2, T)
+        load_words(tab_w[0], tab_words[0], 0, T // 2)
         wi_raw = held([P, 2 * H], U8, "wi_raw")
         nc.sync.dma_start(out=wi_raw[:].bitcast(I32), in_=wi_words[0].bitcast(I32))
         load_plane(wi_sc_raw, wi_scales[0], 0)
-        load_we(0, 0, 0, 2)
+        load_words(tab_w[0], tab_words[0], T // 2, T)
         load_plane(tab_sc, tab_scales[0], TAB_FIRST)
-        load_we(0, 0, 2, 4)
-        load_plane(tab_sc, tab_scales[1], TAB_FIRST + 4)
         load_we(1, 0)
+        load_plane(tab_sc, tab_scales[1], TAB_FIRST + 4)
         load_words(tab_w[1], tab_words[1], 0, T // 2)
         gain_sb = held([P, 2, PACK], F32, "gain_sb")
         nc.sync.dma_start(out=gain_sb[:], in_=gain.rearrange("(g p t) -> p g t", g=2, t=PACK))
@@ -104,12 +103,13 @@ def tile_list_cortical_softplus_currents_kernel(
             load_words(wr_raw[a], wr_words[a], 0, N)
 
         def gather_words(table, offsets, names):
-            picked = [held([P, HALF], U32, name) for name in names]
-            cols = HALF // 16
-            for half in range(2):
-                nc.vector.tensor_copy(picked[half][:],
-                                      table[:].bitcast(U32).indirect(offsets[:, half * cols:(half + 1) * cols]))
-            return picked
+            width = S // len(names)
+            picked = [held([P, width], U32, name) for name in names]
+            cols = width // 16
+            for part, tile in enumerate(picked):
+                nc.vector.tensor_copy(tile[:],
+                                      table[:].bitcast(U32).indirect(offsets[:, part * cols:(part + 1) * cols]))
+            return [picked[c // width][:, c % width:c % width + QUARTER] for c in range(0, S, QUARTER)]
 
         def deal(engine, dealt, raw, run):
             engine.tensor_copy(
@@ -143,16 +143,16 @@ def tile_list_cortical_softplus_currents_kernel(
         deal(nc.vector, wi_w[:].bitcast(U16), wi_raw[:].bitcast(U16), 8)
         wi_sc = held([P, H], U8, "wi_sc")
         deal(nc.vector, wi_sc[:], wi_sc_raw[:], 16)
+        we_q = {}
+        we_q[0, 0] = quantise_we(round_we(nc.scalar, 0, 0, 0, PACK, "we_bf_0_0"), "we_codes_0_0")
         v_w = [gather_words(tab_w[0], idx, ("v_w_0_0", "v_w_0_1"))]
         v_sc = held([P, S], U8, "v_sc")
         nc.vector.tensor_copy(v_sc[:], tab_sc[:].indirect(idx[:]))
-        we_q = {}
-        we_q[0, 0] = quantise_we(round_we(nc.scalar, 0, 0, 0, PACK, "slot_a"), "tab_sc")
-        we_q[1, 0] = quantise_we(round_we(nc.scalar, 1, 0, 0, PACK, "slot_b"), "slot_a")
+        we_q[1, 0] = quantise_we(round_we(nc.scalar, 1, 0, 0, PACK, "slot_b"), "tab_sc")
         neg_gain = held([P, 2, 2, PACK], F32, "neg_gain")
         nc.vector.tensor_scalar(out=neg_gain[:], in0=gain_sb[:].unsqueeze(2).to_broadcast([P, 2, 2, PACK]),
                                 scalar1=-1.0, scalar2=None, op0=ALU.mult)
-        v_w.append(gather_words(tab_w[1], idx, ("slot_b", "v_w_1_1")))
+        v_w.append(gather_words(tab_w[1], idx, ("slot_b", "v_w_1_1", "v_w_1_2", "v_w_1_3")))
 
         we_q[0, 1] = quantise_we(round_we(nc.gpsimd, 0, 1, 0, PACK, "we_bf_0_1"), "we_codes_0_1")
         we_q[1, 1] = quantise_we(round_we(nc.vector, 1, 1, 0, 2, "we_bf_0_1"), "we_codes_1_1_a")
@@ -162,24 +162,20 @@ def tile_list_cortical_softplus_currents_kernel(
         ng = neg_gain[:, :, 0, :]
 
         def drive(bank, kind, g, pair, n):
-            half, c = divmod(n * QUARTER, HALF)
-            width = SUB if kind == 2 else QUARTER
+            js = slice(n * QUARTER, (n + 1) * QUARTER)
             for e in range(2):
                 t = 2 * pair + e
                 u = g * PACK + t
-                for first in range(0, QUARTER, width):
-                    cols = slice(c + first, c + first + width)
-                    js = slice(n * QUARTER + first, n * QUARTER + first + width)
-                    if kind == 2:
-                        lhs, lhs_sc = wi_w[:, u * 2 * P:(u + 1) * 2 * P].bitcast(FP4X4), wi_sc[:, u * P:(u + 1) * P]
-                        rhs, rhs_sc = v2_w[half][:, cols], v2_sc[:, js]
-                    else:
-                        codes, lhs_sc = we_q[kind, g][t]
-                        lhs = codes.bitcast(FP8X4)
-                        rhs, rhs_sc = v_w[kind][half][:, cols], v_sc[TAB_FIRST + 4 * kind:, js]
-                    nc.tensor.matmul_mx(out=bank[:, e, first:first + width], lhsT=lhs, lhsT_scale=lhs_sc,
-                                        rhs=rhs.bitcast(FP8X4), rhs_scale=rhs_sc,
-                                        start=(kind == 2 and e == 0 and first == 0), stop=(kind == 1 and e == 1))
+                if kind == 2:
+                    lhs, lhs_sc = wi_w[:, u * 2 * P:(u + 1) * 2 * P].bitcast(FP4X4), wi_sc[:, u * P:(u + 1) * P]
+                    rhs, rhs_sc = v2_w[n], v2_sc[:, js]
+                else:
+                    codes, lhs_sc = we_q[kind, g][t]
+                    lhs = codes.bitcast(FP8X4)
+                    rhs, rhs_sc = v_w[kind][n], v_sc[TAB_FIRST + 4 * kind:, js]
+                nc.tensor.matmul_mx(out=bank[:, e, :], lhsT=lhs, lhsT_scale=lhs_sc,
+                                    rhs=rhs.bitcast(FP8X4), rhs_scale=rhs_sc,
+                                    start=(kind == 2 and e == 0), stop=(kind == 1 and e == 1))
 
         def drain(bank, g, pair, n):
             ts = slice(2 * pair, 2 * pair + 2)
@@ -194,11 +190,11 @@ def tile_list_cortical_softplus_currents_kernel(
         units = [(pair, n) for n in range(quarters) for pair in range(2)]
         banks = [psum.tile([P, 2, QUARTER], F32, name="bank", tag="bank") for unit in units]
         for kind in (2, 0, 1):
-            for bank, (pair, n) in zip(banks, units):
-                drive(bank, kind, 0, pair, n)
+            for pair, n in (sorted(units) if kind == 0 else units):
+                drive(banks[units.index((pair, n))], kind, 0, pair, n)
         for bank, (pair, n) in zip(banks, units):
             drain(bank, 0, pair, n)
-        we_q[1, 1].extend(quantise_we(round_we(nc.scalar, 1, 1, 2, PACK, "slot_a"), "we_codes_1_1_b"))
+        we_q[1, 1].extend(quantise_we(round_we(nc.scalar, 1, 1, 2, PACK, "tab_sc"), "we_codes_1_1_b"))
 
         units = [(pair, n) for pair in range(2) for n in range(quarters)]
         banks = [psum.tile([P, 2, QUARTER], F32, name="bank", tag="bank") for unit in units]
@@ -208,7 +204,7 @@ def tile_list_cortical_softplus_currents_kernel(
         for bank, (pair, n) in zip(banks, units):
             drain(bank, 1, pair, n)
 
-        wr_dealt = held([P, 2 * N + N // 4], I32, "slot_a")
+        wr_dealt = held([P, 2 * N + N // 4], I32, "tab_sc")
         wr_w = [wr_dealt[:, a * N:(a + 1) * N] for a in range(2)]
         wr_sc = wr_dealt[:, 2 * N:].bitcast(U8)
         deal(nc.gpsimd, wr_sc, wr_sc_raw[:], 16)

@@ -80,20 +80,21 @@ def tile_list_cortical_softplus_currents_kernel(
         tab_w = [held([P, T], I32, "tab_w_%d" % a) for a in range(2)]
         nc.sync.dma_start(idx2[:], offs2)
         load_words(tab2_w, tab2_words[0], 0, T2)
-        load_we(0, 0)
-        nc.sync.dma_start(idx[:], offs)
-        load_plane(tab2_sc, tab2_scales[0], 0)
         load_words(tab_w[0], tab_words[0], 0, T // 2)
-        wi_raw = held([P, 2 * H], U8, "wi_raw")
-        nc.sync.dma_start(out=wi_raw[:].bitcast(I32), in_=wi_words[0].bitcast(I32))
-        load_plane(wi_sc_raw, wi_scales[0], 0)
-        load_words(tab_w[0], tab_words[0], T // 2, T)
-        load_plane(tab_sc, tab_scales[0], TAB_FIRST)
-        load_we(1, 0)
-        load_plane(tab_sc, tab_scales[1], TAB_FIRST + 4)
-        load_words(tab_w[1], tab_words[1], 0, T // 2)
         gain_sb = held([P, 2, PACK], F32, "gain_sb")
         nc.sync.dma_start(out=gain_sb[:], in_=gain.rearrange("(g p t) -> p g t", g=2, t=PACK))
+        load_plane(tab2_sc, tab2_scales[0], 0)
+        load_words(tab_w[0], tab_words[0], T // 2, T)
+        wi_raw = held([P, 2 * H], U8, "wi_raw")
+        nc.sync.dma_start(out=wi_raw[:].bitcast(I32), in_=wi_words[0].bitcast(I32))
+        nc.sync.dma_start(idx[:], offs)
+        load_plane(wi_sc_raw, wi_scales[0], 0)
+        load_we(0, 0, 0, 2)
+        load_plane(tab_sc, tab_scales[0], TAB_FIRST)
+        load_we(0, 0, 2, 4)
+        load_plane(tab_sc, tab_scales[1], TAB_FIRST + 4)
+        load_we(1, 0)
+        load_words(tab_w[1], tab_words[1], 0, T // 2)
         load_words(tab_w[1], tab_words[1], T // 2, T)
         load_we(0, 1)
         load_we(1, 1)
@@ -102,14 +103,16 @@ def tile_list_cortical_softplus_currents_kernel(
         for a in range(2):
             load_words(wr_raw[a], wr_words[a], 0, N)
 
-        def gather_words(table, offsets, names):
-            width = S // len(names)
-            picked = [held([P, width], U32, name) for name in names]
+        def gather_words(table, offsets, names, parts):
+            width = S // parts
             cols = width // 16
-            for part, tile in enumerate(picked):
+            picked = []
+            for part, name in names:
+                tile = held([P, width], U32, name)
                 nc.vector.tensor_copy(tile[:],
                                       table[:].bitcast(U32).indirect(offsets[:, part * cols:(part + 1) * cols]))
-            return [picked[c // width][:, c % width:c % width + QUARTER] for c in range(0, S, QUARTER)]
+                picked.extend(tile[:, c:c + QUARTER] for c in range(0, width, QUARTER))
+            return picked
 
         def deal(engine, dealt, raw, run):
             engine.tensor_copy(
@@ -136,23 +139,24 @@ def tile_list_cortical_softplus_currents_kernel(
             return [(codes[:, c:c + P], scales[:, c:c + P]) for c in range(0, width, P)]
 
         scale_tiles = []
-        v2_w = gather_words(tab2_w, idx2, ("v2_w_0", "v2_w_1"))
+        neg_gain = held([P, 2, 2, PACK], F32, "neg_gain")
+        nc.scalar.activation(out=neg_gain[:], in_=gain_sb[:].unsqueeze(2).to_broadcast([P, 2, 2, PACK]),
+                             func=ACT.Copy, scale=-1.0)
+        v2_w = gather_words(tab2_w, idx2, enumerate(("v2_w_0", "v2_w_1")), 2)
         v2_sc = held([P, S], U8, "v2_sc")
         nc.vector.tensor_copy(v2_sc[:], tab2_sc[:].indirect(idx2[:]))
         wi_w = held([P, 2 * H], U8, "wi_w")
         deal(nc.vector, wi_w[:].bitcast(U16), wi_raw[:].bitcast(U16), 8)
         wi_sc = held([P, H], U8, "wi_sc")
         deal(nc.vector, wi_sc[:], wi_sc_raw[:], 16)
-        we_q = {}
-        we_q[0, 0] = quantise_we(round_we(nc.scalar, 0, 0, 0, PACK, "we_bf_0_0"), "we_codes_0_0")
-        v_w = [gather_words(tab_w[0], idx, ("v_w_0_0", "v_w_0_1"))]
+        v_w = [gather_words(tab_w[0], idx, [(0, "wi_sc_raw")], 2)]
         v_sc = held([P, S], U8, "v_sc")
         nc.vector.tensor_copy(v_sc[:], tab_sc[:].indirect(idx[:]))
-        we_q[1, 0] = quantise_we(round_we(nc.scalar, 1, 0, 0, PACK, "slot_b"), "tab_sc")
-        neg_gain = held([P, 2, 2, PACK], F32, "neg_gain")
-        nc.vector.tensor_scalar(out=neg_gain[:], in0=gain_sb[:].unsqueeze(2).to_broadcast([P, 2, 2, PACK]),
-                                scalar1=-1.0, scalar2=None, op0=ALU.mult)
-        v_w.append(gather_words(tab_w[1], idx, ("slot_b", "v_w_1_1", "v_w_1_2", "v_w_1_3")))
+        we_q = {}
+        we_q[0, 0] = quantise_we(round_we(nc.scalar, 0, 0, 0, PACK, "slot_c"), "tab_sc")
+        v_w[0].extend(gather_words(tab_w[0], idx, [(1, "slot_c")], 2))
+        we_q[1, 0] = quantise_we(round_we(nc.scalar, 1, 0, 0, PACK, "slot_b"), "slot_a")
+        v_w.append(gather_words(tab_w[1], idx, enumerate(("slot_b", "v_w_1_1", "v_w_1_2", "v_w_1_3")), 4))
 
         we_q[0, 1] = quantise_we(round_we(nc.gpsimd, 0, 1, 0, PACK, "we_bf_0_1"), "we_codes_0_1")
         we_q[1, 1] = quantise_we(round_we(nc.vector, 1, 1, 0, 2, "we_bf_0_1"), "we_codes_1_1_a")
@@ -190,11 +194,11 @@ def tile_list_cortical_softplus_currents_kernel(
         units = [(pair, n) for n in range(quarters) for pair in range(2)]
         banks = [psum.tile([P, 2, QUARTER], F32, name="bank", tag="bank") for unit in units]
         for kind in (2, 0, 1):
-            for pair, n in (sorted(units) if kind == 0 else units):
-                drive(banks[units.index((pair, n))], kind, 0, pair, n)
+            for bank, (pair, n) in zip(banks, units):
+                drive(bank, kind, 0, pair, n)
         for bank, (pair, n) in zip(banks, units):
             drain(bank, 0, pair, n)
-        we_q[1, 1].extend(quantise_we(round_we(nc.scalar, 1, 1, 2, PACK, "tab_sc"), "we_codes_1_1_b"))
+        we_q[1, 1].extend(quantise_we(round_we(nc.scalar, 1, 1, 2, PACK, "slot_a"), "we_codes_1_1_b"))
 
         units = [(pair, n) for pair in range(2) for n in range(quarters)]
         banks = [psum.tile([P, 2, QUARTER], F32, name="bank", tag="bank") for unit in units]
@@ -204,7 +208,7 @@ def tile_list_cortical_softplus_currents_kernel(
         for bank, (pair, n) in zip(banks, units):
             drain(bank, 1, pair, n)
 
-        wr_dealt = held([P, 2 * N + N // 4], I32, "tab_sc")
+        wr_dealt = held([P, 2 * N + N // 4], I32, "slot_a")
         wr_w = [wr_dealt[:, a * N:(a + 1) * N] for a in range(2)]
         wr_sc = wr_dealt[:, 2 * N:].bitcast(U8)
         deal(nc.gpsimd, wr_sc, wr_sc_raw[:], 16)

@@ -122,8 +122,12 @@ def tile_list_cortical_softplus_currents_kernel(
 
         def round_we(engine, a, g, first, last, name):
             dealt = held([P, last - first, P, PACK], BF16, name)
-            dst = dealt[:].rearrange("p t m i -> p m t i")
-            src = we_raw[a, g][:].rearrange("p i (m t) -> p m t i", t=PACK)[:, :, first:last, :]
+            if engine is nc.vector:
+                dst = dealt[:].rearrange("p t m i -> p m i t")
+                src = we_raw[a, g][:].rearrange("p i (m t) -> p m i t", t=PACK)[:, :, :, first:last]
+            else:
+                dst = dealt[:].rearrange("p t m i -> p m t i")
+                src = we_raw[a, g][:].rearrange("p i (m t) -> p m t i", t=PACK)[:, :, first:last, :]
             if engine is nc.scalar:
                 engine.activation(out=dst, in_=src, func=ACT.Copy, scale=-1.0)
             else:
@@ -139,9 +143,8 @@ def tile_list_cortical_softplus_currents_kernel(
             return [(codes[:, c:c + P], scales[:, c:c + P]) for c in range(0, width, P)]
 
         scale_tiles = []
-        neg_gain = held([P, 2, 2, PACK], F32, "neg_gain")
-        nc.scalar.activation(out=neg_gain[:], in_=gain_sb[:].unsqueeze(2).to_broadcast([P, 2, 2, PACK]),
-                             func=ACT.Copy, scale=-1.0)
+        neg_gain = held([P, 2, PACK], F32, "neg_gain")
+        nc.scalar.activation(out=neg_gain[:], in_=gain_sb[:], func=ACT.Copy, scale=-1.0)
         v2_w = gather_words(tab2_w, idx2, enumerate(("v2_w_0", "v2_w_1")), 2)
         v2_sc = held([P, S], U8, "v2_sc")
         nc.vector.tensor_copy(v2_sc[:], tab2_sc[:].indirect(idx2[:]))
@@ -163,7 +166,7 @@ def tile_list_cortical_softplus_currents_kernel(
 
         sig = [held([P, 2 * SPAN], F32, "sig_%d" % n if n > 1 else "we_raw_%d_0" % n) for n in range(S // QUARTER)]
         lin = [held([P, 2 * SPAN], BF16, "we_bf_0_1" if n == 2 else "lin_%d" % n) for n in range(S // QUARTER)]
-        ng = neg_gain[:, :, 0, :]
+        ng = neg_gain[:]
 
         def drive(bank, kind, g, pair, n):
             js = slice(n * QUARTER, (n + 1) * QUARTER)
@@ -183,8 +186,9 @@ def tile_list_cortical_softplus_currents_kernel(
 
         def drain(bank, g, pair, n):
             ts = slice(2 * pair, 2 * pair + 2)
-            sig_out = sig[n][:].rearrange("p (k g c t i) -> p k g c t i", k=2, g=2, t=PACK, i=2)[:, :, g, :, ts, :]
-            nc.scalar.activation(out=sig_out, in_=bank[:].rearrange("p e (k c i) -> p k c e i", k=2, i=2),
+            order = "p (k a g j e) -> p k a g j e" if n else "p (k g a j e) -> p k a g j e"
+            sig_out = sig[n][:].rearrange(order, k=2, a=2, g=2, e=2)[:, :, pair, g, :, :]
+            nc.scalar.activation(out=sig_out, in_=bank[:].rearrange("p e (k j) -> p k j e", k=2),
                                  func=ACT.Sigmoid, bias=zero[:])
             lin_out = lin[n][:].rearrange("p (k a g j e) -> p k a g j e", k=2, a=2, g=2, e=2)[:, :, pair, g, :, :]
             nc.vector.tensor_tensor(out=lin_out, in0=bank[:].rearrange("p e (k j) -> p k j e", k=2),
@@ -236,9 +240,11 @@ def tile_list_cortical_softplus_currents_kernel(
         def products(n, parts):
             h[n] = ring.tile([P, SPAN], BF16, name="h", bufs=3, align_bytes=64)
             for gs in parts:
-                src = stretch(sig, n).rearrange("p (g c t i) -> p g c i t", g=2, t=PACK, i=2)[:, gs]
-                nc.vector.tensor_tensor(out=h[n][:].rearrange("p (g c i t) -> p g c i t", g=2, t=PACK, i=2)[:, gs],
-                                        in0=src, in1=neg_gain[:, gs].unsqueeze(2).to_broadcast(src.shape),
+                order = "p (a g j e) -> p g j a e" if n > 1 else "p (g a j e) -> p g j a e"
+                src = stretch(sig, n).rearrange(order, a=2, g=2, e=2)[:, gs]
+                factor = ng.rearrange("p g (a e) -> p g a e", e=2)[:, gs].unsqueeze(2).to_broadcast(src.shape)
+                nc.vector.tensor_tensor(out=h[n][:].rearrange("p (g j a e) -> p g j a e", g=2, a=2, e=2)[:, gs],
+                                        in0=src, in1=factor,
                                         op=ALU.mult)
 
         def maxima(n, parts):

@@ -71,8 +71,8 @@ def tile_list_cortical_softplus_currents_kernel(
                 rows = tile[32 * q + first:32 * q + first + 8, :]
                 nc.sync.dma_start(out=rows.bitcast(I32), in_=scales[:, 4 * q:4 * q + 4, :].bitcast(I32))
 
-        def load_plane(tile, scales, first):
-            for r in range(4):
+        def load_plane(tile, scales, first, rows):
+            for r in rows:
                 nc.sync.dma_start(out=tile[first + r:P:32, :].bitcast(I32), in_=scales[r:16:4, :].bitcast(I32))
 
         we_raw = {(a, g): held([P, PACK, GROUP], F32, "we_raw_%d_%d" % (a, g)) for a in range(2) for g in range(2)}
@@ -81,20 +81,20 @@ def tile_list_cortical_softplus_currents_kernel(
         nc.sync.dma_start(idx2[:], offs2)
         load_words(tab2_w, tab2_words[0], 0, T2)
         load_words(tab_w[0], tab_words[0], 0, T // 2)
-        gain_sb = held([P, 2, PACK], F32, "gain_sb")
-        nc.sync.dma_start(out=gain_sb[:], in_=gain.rearrange("(g p t) -> p g t", g=2, t=PACK))
-        load_plane(tab2_sc, tab2_scales[0], 0)
-        load_words(tab_w[0], tab_words[0], T // 2, T)
+        load_plane(tab2_sc, tab2_scales[0], 0, range(4))
+        nc.sync.dma_start(idx[:], offs)
         wi_raw = held([P, 2 * H], U8, "wi_raw")
         nc.sync.dma_start(out=wi_raw[:].bitcast(I32), in_=wi_words[0].bitcast(I32))
-        nc.sync.dma_start(idx[:], offs)
-        load_plane(wi_sc_raw, wi_scales[0], 0)
-        load_we(0, 0, 0, 2)
-        load_plane(tab_sc, tab_scales[0], TAB_FIRST)
-        load_we(0, 0, 2, 4)
-        load_plane(tab_sc, tab_scales[1], TAB_FIRST + 4)
+        load_words(tab_w[0], tab_words[0], T // 2, T)
+        load_plane(wi_sc_raw, wi_scales[0], 0, range(4))
+        load_plane(tab_sc, tab_scales[0], TAB_FIRST, range(2))
+        load_we(0, 0)
+        load_plane(tab_sc, tab_scales[0], TAB_FIRST, range(2, 4))
+        load_plane(tab_sc, tab_scales[1], TAB_FIRST + 4, range(4))
         load_we(1, 0)
         load_words(tab_w[1], tab_words[1], 0, T // 2)
+        gain_sb = held([P, 2, PACK], F32, "gain_sb")
+        nc.sync.dma_start(out=gain_sb[:], in_=gain.rearrange("(g p t) -> p g t", g=2, t=PACK))
         load_words(tab_w[1], tab_words[1], T // 2, T)
         load_we(0, 1)
         load_we(1, 1)
@@ -143,8 +143,6 @@ def tile_list_cortical_softplus_currents_kernel(
             return [(codes[:, c:c + P], scales[:, c:c + P]) for c in range(0, width, P)]
 
         scale_tiles = []
-        neg_gain = held([P, 2, PACK], F32, "neg_gain")
-        nc.scalar.activation(out=neg_gain[:], in_=gain_sb[:], func=ACT.Copy, scale=-1.0)
         v2_w = gather_words(tab2_w, idx2, enumerate(("v2_w_0", "v2_w_1")), 2)
         v2_sc = held([P, S], U8, "v2_sc")
         nc.vector.tensor_copy(v2_sc[:], tab2_sc[:].indirect(idx2[:]))
@@ -159,6 +157,8 @@ def tile_list_cortical_softplus_currents_kernel(
         we_q[0, 0] = quantise_we(round_we(nc.scalar, 0, 0, 0, PACK, "slot_c"), "tab_sc")
         v_w[0].extend(gather_words(tab_w[0], idx, [(1, "slot_c")], 2))
         we_q[1, 0] = quantise_we(round_we(nc.scalar, 1, 0, 0, PACK, "slot_b"), "slot_a")
+        neg_gain = held([P, 2, PACK], F32, "neg_gain")
+        nc.scalar.activation(out=neg_gain[:], in_=gain_sb[:], func=ACT.Copy, scale=-1.0)
         v_w.append(gather_words(tab_w[1], idx, enumerate(("slot_b", "v_w_1_1", "v_w_1_2", "v_w_1_3")), 4))
 
         we_q[0, 1] = quantise_we(round_we(nc.gpsimd, 0, 1, 0, PACK, "we_bf_0_1"), "we_codes_0_1")
@@ -317,20 +317,20 @@ def tile_list_cortical_softplus_currents_kernel(
                 if n + 1 < count:
                     products(n + 1, both)
                 else:
-                    quantise_y(2, 4)
-                    store_words(2, 4)
+                    weave(4, both)
                 quantise_h(n, both)
             currents(n)
             if n + AHEAD < count:
                 logs(n + AHEAD, both)
-            if n - 2 in FROM_PSUM:
-                weave_banks(n - 2)
+            if n - 3 in FROM_PSUM:
+                weave_banks(n - 3)
             if n - EARLY in (0, 1):
                 weave(n - EARLY, both)
             if n - EARLY == 2:
                 quantise_y(0, 2)
                 store_words(0, 2)
-        weave(4, both)
+        quantise_y(2, 4)
+        store_words(2, 4)
         weave(5, both)
         weave(6, both)
         quantise_y(4, 6)

@@ -24,7 +24,6 @@ SPAN = 2 * SUB * PACK
 EARLY = 3
 AHEAD = 4
 FROM_PSUM = (2, 3)
-TAB_FIRST = 4
 WR_FIRST = 8
 FLOOR = 2.0 ** -60
 FLOPS = 5368709120
@@ -55,8 +54,10 @@ def tile_list_cortical_softplus_currents_kernel(
         nc.gpsimd.memset(zero[:], 0.0)
         nc.gpsimd.memset(tab_sc[:].bitcast(I32), 0)
         nc.vector.memset(tab2_sc[:].bitcast(I32), 0)
-        nc.vector.memset(wi_sc_raw[:].bitcast(I32), 0)
-        nc.vector.memset(wr_sc_raw[:].bitcast(I32), 0)
+        v2_sc = held([P, S], U8, "v2_sc")
+        v_sc = [held([P, S], U8, "v_sc_%d" % a) for a in range(2)]
+        for plane in [v2_sc, wi_sc_raw, wr_sc_raw] + v_sc:
+            nc.vector.memset(plane[:].bitcast(I32), 0)
 
         def load_we(a, g, first=0, last=PACK):
             rows = we[a * GROUP:(a + 1) * GROUP, g * GROUP:(g + 1) * GROUP].rearrange("(p i) c -> p i c", i=PACK)
@@ -71,28 +72,35 @@ def tile_list_cortical_softplus_currents_kernel(
                 rows = tile[32 * q + first:32 * q + first + 8, :]
                 nc.sync.dma_start(out=rows.bitcast(I32), in_=scales[:, 4 * q:4 * q + 4, :].bitcast(I32))
 
-        def load_plane(tile, scales, first, rows):
+        def load_plane(tile, scales, rows=range(4)):
             for r in rows:
-                nc.sync.dma_start(out=tile[first + r:P:32, :].bitcast(I32), in_=scales[r:16:4, :].bitcast(I32))
+                nc.sync.dma_start(out=tile[r:P:32, :].bitcast(I32), in_=scales[r:16:4, :].bitcast(I32))
 
         we_raw = {(a, g): held([P, PACK, GROUP], F32, "we_raw_%d_%d" % (a, g)) for a in range(2) for g in range(2)}
         tab2_w = held([P, T2], I32, "tab2_w")
         tab_w = [held([P, T], I32, "tab_w_%d" % a) for a in range(2)]
         nc.sync.dma_start(idx2[:], offs2)
-        load_words(tab2_w, tab2_words[0], 0, T2)
-        load_words(tab_w[0], tab_words[0], 0, T // 2)
-        load_plane(tab2_sc, tab2_scales[0], 0, range(4))
+        load_words(tab2_w, tab2_words[0], 0, T2 // 2)
+        nc.sync.dma_start(out=tab2_sc[0:P:8, :].bitcast(I32), in_=tab2_scales[0].bitcast(I32))
         nc.sync.dma_start(idx[:], offs)
+        nc.sync.dma_start(out=tab_sc[0:P:4, :].bitcast(I32), in_=tab_scales.rearrange("a q c -> (a q) c").bitcast(I32))
+        load_words(tab2_w, tab2_words[0], T2 // 2, T2)
+        load_words(tab_w[0], tab_words[0], 0, T // 2)
         wi_raw = held([P, 2 * H], U8, "wi_raw")
         nc.sync.dma_start(out=wi_raw[:].bitcast(I32), in_=wi_words[0].bitcast(I32))
-        load_words(tab_w[0], tab_words[0], T // 2, T)
-        load_plane(wi_sc_raw, wi_scales[0], 0, range(4))
-        load_plane(tab_sc, tab_scales[0], TAB_FIRST, range(2))
+        load_plane(wi_sc_raw, wi_scales[0], range(2))
         load_we(0, 0)
-        load_plane(tab_sc, tab_scales[0], TAB_FIRST, range(2, 4))
-        load_plane(tab_sc, tab_scales[1], TAB_FIRST + 4, range(4))
+        v2_rows = held([P, S], U8, "v2_rows")
+        nc.vector.tensor_copy(v2_rows[:], tab2_sc[:].indirect(idx2[:]))
+        v_rows = held([P, S], U8, "v_rows")
+        nc.vector.tensor_copy(v_rows[:], tab_sc[:].indirect(idx[:]))
+        load_plane(v2_sc, v2_rows[0:P:8, :])
+        load_plane(wi_sc_raw, wi_scales[0], range(2, 4))
+        load_words(tab_w[0], tab_words[0], T // 2, T)
+        load_plane(v_sc[0], v_rows[0:P // 2:4, :])
         load_we(1, 0)
         load_words(tab_w[1], tab_words[1], 0, T // 2)
+        load_plane(v_sc[1], v_rows[P // 2:P:4, :])
         gain_sb = held([P, 2, PACK], F32, "gain_sb")
         nc.sync.dma_start(out=gain_sb[:], in_=gain.rearrange("(g p t) -> p g t", g=2, t=PACK))
         load_words(tab_w[1], tab_words[1], T // 2, T)
@@ -143,18 +151,15 @@ def tile_list_cortical_softplus_currents_kernel(
             return [(codes[:, c:c + P], scales[:, c:c + P]) for c in range(0, width, P)]
 
         scale_tiles = []
-        v2_w = gather_words(tab2_w, idx2, enumerate(("v2_w_0", "v2_w_1")), 2)
-        v2_sc = held([P, S], U8, "v2_sc")
-        nc.vector.tensor_copy(v2_sc[:], tab2_sc[:].indirect(idx2[:]))
+        v2_w = gather_words(tab2_w, idx2, [(0, "tab_sc")], 2)
         wi_w = held([P, 2 * H], U8, "wi_w")
         deal(nc.vector, wi_w[:].bitcast(U16), wi_raw[:].bitcast(U16), 8)
         wi_sc = held([P, H], U8, "wi_sc")
         deal(nc.vector, wi_sc[:], wi_sc_raw[:], 16)
-        v_w = [gather_words(tab_w[0], idx, [(0, "wi_sc_raw")], 2)]
-        v_sc = held([P, S], U8, "v_sc")
-        nc.vector.tensor_copy(v_sc[:], tab_sc[:].indirect(idx[:]))
+        v2_w.extend(gather_words(tab2_w, idx2, [(1, "wi_sc_raw")], 2))
+        v_w = [gather_words(tab_w[0], idx, [(0, "wi_raw")], 2)]
         we_q = {}
-        we_q[0, 0] = quantise_we(round_we(nc.scalar, 0, 0, 0, PACK, "slot_c"), "tab_sc")
+        we_q[0, 0] = quantise_we(round_we(nc.scalar, 0, 0, 0, PACK, "slot_c"), "we_codes_0_0")
         v_w[0].extend(gather_words(tab_w[0], idx, [(1, "slot_c")], 2))
         we_q[1, 0] = quantise_we(round_we(nc.scalar, 1, 0, 0, PACK, "slot_b"), "slot_a")
         neg_gain = held([P, 2, PACK], F32, "neg_gain")
@@ -179,7 +184,7 @@ def tile_list_cortical_softplus_currents_kernel(
                 else:
                     codes, lhs_sc = we_q[kind, g][t]
                     lhs = codes.bitcast(FP8X4)
-                    rhs, rhs_sc = v_w[kind][n], v_sc[TAB_FIRST + 4 * kind:, js]
+                    rhs, rhs_sc = v_w[kind][n], v_sc[kind][:, js]
                 nc.tensor.matmul_mx(out=bank[:, e, :], lhsT=lhs, lhsT_scale=lhs_sc,
                                     rhs=rhs.bitcast(FP8X4), rhs_scale=rhs_sc,
                                     start=(kind == 2 and e == 0), stop=(kind == 1 and e == 1))

@@ -17,15 +17,14 @@ P = 128
 PACK = 4
 GROUP = P * PACK
 T, T2, S, H, N = 4096, 2048, 1024, 1024, 1024
-HALF = 512
 QUARTER = 256
 SUB = 128
 SPAN = 2 * SUB * PACK
-EARLY = 3
 AHEAD = 4
-FROM_PSUM = (2, 3)
+LAG = 2
 WR_FIRST = 8
 FLOOR = 2.0 ** -60
+KNEE = 16.0
 FLOPS = 5368709120
 
 
@@ -37,7 +36,8 @@ def tile_list_cortical_softplus_currents_kernel(
     with ExitStack() as ctx:
         lists = ctx.enter_context(tc.tile_pool(name="lists", bufs=1))
         keep = ctx.enter_context(tc.tile_pool(name="keep", bufs=1))
-        ring = ctx.enter_context(tc.tile_pool(name="ring", bufs=4))
+        late = ctx.enter_context(tc.tile_pool(name="late", bufs=1))
+        ring = ctx.enter_context(tc.tile_pool(name="ring", bufs=3))
         psum = ctx.enter_context(tc.psum_pool(name="psum", bufs=8))
 
         def held(shape, dtype, name):
@@ -59,9 +59,11 @@ def tile_list_cortical_softplus_currents_kernel(
         for plane in [v2_sc, wi_sc_raw, wr_sc_raw] + v_sc:
             nc.vector.memset(plane[:].bitcast(I32), 0)
 
-        def load_we(a, g, first=0, last=PACK):
-            rows = we[a * GROUP:(a + 1) * GROUP, g * GROUP:(g + 1) * GROUP].rearrange("(p i) c -> p i c", i=PACK)
-            nc.sync.dma_start(out=we_raw[a, g][:, first:last, :], in_=rows[:, first:last, :])
+        def load_we(a, first, width, name):
+            raw = held([P, PACK, width], F32, name)
+            rows = we[a * GROUP:(a + 1) * GROUP, first:first + width].rearrange("(p i) c -> p i c", i=PACK)
+            nc.sync.dma_start(out=raw[:], in_=rows)
+            return raw
 
         def load_words(tile, words, first, last):
             src = words.rearrange("p c i -> p (c i)").bitcast(I32)
@@ -76,7 +78,6 @@ def tile_list_cortical_softplus_currents_kernel(
             for r in rows:
                 nc.sync.dma_start(out=tile[r:P:32, :].bitcast(I32), in_=scales[r:16:4, :].bitcast(I32))
 
-        we_raw = {(a, g): held([P, PACK, GROUP], F32, "we_raw_%d_%d" % (a, g)) for a in range(2) for g in range(2)}
         tab2_w = held([P, T2], I32, "tab2_w")
         tab_w = [held([P, T], I32, "tab_w_%d" % a) for a in range(2)]
         nc.sync.dma_start(idx2[:], offs2)
@@ -89,7 +90,7 @@ def tile_list_cortical_softplus_currents_kernel(
         wi_raw = held([P, 2 * H], U8, "wi_raw")
         nc.sync.dma_start(out=wi_raw[:].bitcast(I32), in_=wi_words[0].bitcast(I32))
         load_plane(wi_sc_raw, wi_scales[0], range(2))
-        load_we(0, 0)
+        raw_0_0 = load_we(0, 0, GROUP, "we_raw_0_0")
         v2_rows = held([P, S], U8, "v2_rows")
         nc.vector.tensor_copy(v2_rows[:], tab2_sc[:].indirect(idx2[:]))
         v_rows = held([P, S], U8, "v_rows")
@@ -98,29 +99,24 @@ def tile_list_cortical_softplus_currents_kernel(
         load_plane(wi_sc_raw, wi_scales[0], range(2, 4))
         load_words(tab_w[0], tab_words[0], T // 2, T)
         load_plane(v_sc[0], v_rows[0:P // 2:4, :])
-        load_we(1, 0)
+        raw_1_0 = load_we(1, 0, GROUP, "we_raw_1_0")
         load_words(tab_w[1], tab_words[1], 0, T // 2)
         load_plane(v_sc[1], v_rows[P // 2:P:4, :])
         gain_sb = held([P, 2, PACK], F32, "gain_sb")
         nc.sync.dma_start(out=gain_sb[:], in_=gain.rearrange("(g p t) -> p g t", g=2, t=PACK))
         load_words(tab_w[1], tab_words[1], T // 2, T)
-        load_we(0, 1)
-        load_we(1, 1)
+        raw_0_1 = load_we(0, GROUP, GROUP, "we_raw_0_1")
+        raw_1_1 = load_we(1, GROUP, GROUP, "we_raw_1_1")
         load_plane_pair(wr_sc_raw, wr_scales, WR_FIRST)
         wr_raw = [held([P, N], I32, "wr_raw_%d" % a) for a in range(2)]
         for a in range(2):
             load_words(wr_raw[a], wr_words[a], 0, N)
 
-        def gather_words(table, offsets, names, parts):
-            width = S // parts
+        def gather_words(table, offsets, part, name, width=S // 2):
+            tile = held([P, width], U32, name)
             cols = width // 16
-            picked = []
-            for part, name in names:
-                tile = held([P, width], U32, name)
-                nc.vector.tensor_copy(tile[:],
-                                      table[:].bitcast(U32).indirect(offsets[:, part * cols:(part + 1) * cols]))
-                picked.extend(tile[:, c:c + QUARTER] for c in range(0, width, QUARTER))
-            return picked
+            nc.vector.tensor_copy(tile[:], table[:].bitcast(U32).indirect(offsets[:, part * cols:(part + 1) * cols]))
+            return [tile[:, c:c + QUARTER] for c in range(0, width, QUARTER)]
 
         def deal(engine, dealt, raw, run):
             engine.tensor_copy(
@@ -128,50 +124,55 @@ def tile_list_cortical_softplus_currents_kernel(
                 in_=raw.rearrange("p (g c i t) -> p g c t i", g=2, t=PACK, i=run),
             )
 
-        def round_we(engine, a, g, first, last, name):
-            dealt = held([P, last - first, P, PACK], BF16, name)
+        def round_we(engine, dealt, raw, first):
+            last = first + dealt.shape[1]
             if engine is nc.vector:
-                dst = dealt[:].rearrange("p t m i -> p m i t")
-                src = we_raw[a, g][:].rearrange("p i (m t) -> p m i t", t=PACK)[:, :, :, first:last]
+                dst = dealt.rearrange("p t m i -> p m i t")
+                src = raw[:].rearrange("p i (m t) -> p m i t", t=PACK)[:, :, :, first:last]
             else:
-                dst = dealt[:].rearrange("p t m i -> p m t i")
-                src = we_raw[a, g][:].rearrange("p i (m t) -> p m t i", t=PACK)[:, :, first:last, :]
+                dst = dealt.rearrange("p t m i -> p m t i")
+                src = raw[:].rearrange("p i (m t) -> p m t i", t=PACK)[:, :, first:last, :]
             if engine is nc.scalar:
                 engine.activation(out=dst, in_=src, func=ACT.Copy, scale=-1.0)
             else:
                 engine.tensor_scalar(out=dst, in0=src, scalar1=-1.0, scalar2=0.0, op0=ALU.mult, op1=ALU.add)
-            return dealt[:].rearrange("p t m i -> p (t m i)")
 
-        def quantise_we(rounded, name):
-            width = rounded.shape[1] // PACK
-            codes = held([P, width], U32, name)
-            scales = held([P, width], U8, "scales_%d" % len(scale_tiles))
-            scale_tiles.append(scales)
-            nc.vector.quantize_mx(out=codes[:].bitcast(FP8X4), scales=scales[:], in_=rounded)
+        def quantise_we(dealt, name):
+            width = dealt.shape[1] * P
+            codes = held([P, width], U32, name + "_codes")
+            scales = held([P, width], U8, name + "_scales")
+            nc.vector.quantize_mx(out=codes[:].bitcast(FP8X4), scales=scales[:],
+                                  in_=dealt.rearrange("p t m i -> p (t m i)"))
             return [(codes[:, c:c + P], scales[:, c:c + P]) for c in range(0, width, P)]
 
-        scale_tiles = []
-        v2_w = gather_words(tab2_w, idx2, [(0, "tab_sc")], 2)
+        v2_w = gather_words(tab2_w, idx2, 0, "tab_sc")
         wi_w = held([P, 2 * H], U8, "wi_w")
         deal(nc.vector, wi_w[:].bitcast(U16), wi_raw[:].bitcast(U16), 8)
         wi_sc = held([P, H], U8, "wi_sc")
         deal(nc.vector, wi_sc[:], wi_sc_raw[:], 16)
-        v2_w.extend(gather_words(tab2_w, idx2, [(1, "wi_sc_raw")], 2))
-        v_w = [gather_words(tab_w[0], idx, [(0, "wi_raw")], 2)]
+        v2_w.extend(gather_words(tab2_w, idx2, 1, "wi_sc_raw"))
+        v_w = [gather_words(tab_w[0], idx, 0, "wi_raw")]
         we_q = {}
-        we_q[0, 0] = quantise_we(round_we(nc.scalar, 0, 0, 0, PACK, "slot_c"), "we_codes_0_0")
-        v_w[0].extend(gather_words(tab_w[0], idx, [(1, "slot_c")], 2))
-        we_q[1, 0] = quantise_we(round_we(nc.scalar, 1, 0, 0, PACK, "slot_b"), "slot_a")
-        neg_gain = held([P, 2, PACK], F32, "neg_gain")
-        nc.scalar.activation(out=neg_gain[:], in_=gain_sb[:], func=ACT.Copy, scale=-1.0)
-        v_w.append(gather_words(tab_w[1], idx, enumerate(("slot_b", "v_w_1_1", "v_w_1_2", "v_w_1_3")), 4))
+        dealt_0_0 = held([P, PACK, P, PACK], BF16, "dealt_0_0")
+        round_we(nc.scalar, dealt_0_0[:], raw_0_0, 0)
+        we_q[0, 0] = quantise_we(dealt_0_0[:], "we_0_0")
+        v_w[0].extend(gather_words(tab_w[0], idx, 1, "dealt_0_0"))
+        dealt_1_0 = held([P, PACK, P, PACK], BF16, "dealt_1_0")
+        round_we(nc.scalar, dealt_1_0[:], raw_1_0, 0)
+        we_q[1, 0] = quantise_we(dealt_1_0[:], "dealt_1_1_b")
+        slope = held([P, 2 * PACK, 2], F32, "slope")
+        nc.scalar.activation(out=slope[:], func=ACT.Copy, scale=1.0 / KNEE,
+                             in_=gain_sb[:].rearrange("p g t -> p (g t)").unsqueeze(2).to_broadcast([P, 2 * PACK, 2]))
+        v_w.append([gather_words(tab_w[1], idx, n, name, QUARTER)[0]
+                    for n, name in enumerate(("dealt_1_0", "v_w_1_1", "v_w_1_2", "v_w_1_3"))])
 
-        we_q[0, 1] = quantise_we(round_we(nc.gpsimd, 0, 1, 0, PACK, "we_bf_0_1"), "we_codes_0_1")
-        we_q[1, 1] = quantise_we(round_we(nc.vector, 1, 1, 0, 2, "we_bf_0_1"), "we_codes_1_1_a")
+        dealt_0_1 = late.tile([P, PACK, P, PACK], BF16, name="dealt_0_1", align_bytes=64, offset=0)
+        round_we(nc.gpsimd, dealt_0_1[:], raw_0_1, 0)
+        early = late.tile([P, 2, P, PACK], BF16, name="early", align_bytes=64, offset=4096)
 
-        sig = [held([P, 2 * SPAN], F32, "sig_%d" % n if n > 1 else "we_raw_%d_0" % n) for n in range(S // QUARTER)]
-        lin = [held([P, 2 * SPAN], BF16, "we_bf_0_1" if n == 2 else "lin_%d" % n) for n in range(S // QUARTER)]
-        ng = neg_gain[:]
+        quarters = S // QUARTER
+        sig = [held([P, 2 * SPAN], F32, "sig_%d" % n if n > 1 else "we_raw_%d_0" % n) for n in range(quarters)]
+        factor = {}
 
         def drive(bank, kind, g, pair, n):
             js = slice(n * QUARTER, (n + 1) * QUARTER)
@@ -190,24 +191,34 @@ def tile_list_cortical_softplus_currents_kernel(
                                     start=(kind == 2 and e == 0), stop=(kind == 1 and e == 1))
 
         def drain(bank, g, pair, n):
-            ts = slice(2 * pair, 2 * pair + 2)
-            order = "p (k a g j e) -> p k a g j e" if n else "p (k g a j e) -> p k a g j e"
-            sig_out = sig[n][:].rearrange(order, k=2, a=2, g=2, e=2)[:, :, pair, g, :, :]
+            sig_out = sig[n][:].rearrange("p (k a g j e) -> p k a g j e", k=2, a=2, g=2, e=2)[:, :, pair, g, :, :]
             nc.scalar.activation(out=sig_out, in_=bank[:].rearrange("p e (k j) -> p k j e", k=2),
                                  func=ACT.Sigmoid, bias=zero[:])
-            lin_out = lin[n][:].rearrange("p (k a g j e) -> p k a g j e", k=2, a=2, g=2, e=2)[:, :, pair, g, :, :]
-            nc.vector.tensor_tensor(out=lin_out, in0=bank[:].rearrange("p e (k j) -> p k j e", k=2),
-                                    in1=ng[:, g:g + 1, ts].unsqueeze(1).to_broadcast([P, 2, SUB, 2]), op=ALU.mult)
+            out = factor[n][:].rearrange("p (g j a c) -> p g j a c", g=2, a=2, c=4)[:, g, :, pair, :]
+            first = g * PACK + 2 * pair
+            slopes = slope[:, first:first + 2, :].rearrange("p e k -> p (e k)").unsqueeze(1).to_broadcast([P, SUB, 4])
+            nc.vector.scalar_tensor_tensor(out=out, in0=bank[:].rearrange("p e (k j) -> p j (e k)", k=2),
+                                           scalar=-KNEE, in1=slopes, op0=ALU.min, op1=ALU.mult)
 
-        quarters = S // QUARTER
         units = [(pair, n) for n in range(quarters) for pair in range(2)]
         banks = [psum.tile([P, 2, QUARTER], F32, name="bank", tag="bank") for unit in units]
         for kind in (2, 0, 1):
             for bank, (pair, n) in zip(banks, units):
                 drive(bank, kind, 0, pair, n)
-        for bank, (pair, n) in zip(banks, units):
-            drain(bank, 0, pair, n)
-        we_q[1, 1].extend(quantise_we(round_we(nc.scalar, 1, 1, 2, PACK, "slot_a"), "we_codes_1_1_b"))
+        factor[0] = held([P, 2 * SPAN], F32, "tab2_w")
+        factor[1] = held([P, 2 * SPAN], F32, "factor_1")
+        for u in range(4):
+            drain(banks[u], 0, *units[u])
+        round_we(nc.vector, early[:], raw_1_1, 0)
+        we_q[0, 1] = quantise_we(dealt_0_1[:], "we_0_1")
+        we_q[1, 1] = quantise_we(early[:], "we_1_1_a")
+        factor[2] = late.tile([P, 2 * SPAN], F32, name="factor_2", align_bytes=64, offset=0)
+        factor[3] = held([P, 2 * SPAN], F32, "factor_3")
+        for u in range(4, 8):
+            drain(banks[u], 0, *units[u])
+        final = held([P, 2, P, PACK], BF16, "dealt_1_1_b_codes")
+        round_we(nc.scalar, final[:], raw_1_1, 2)
+        we_q[1, 1].extend(quantise_we(final[:], "we_1_1_b"))
 
         units = [(pair, n) for pair in range(2) for n in range(quarters)]
         banks = [psum.tile([P, 2, QUARTER], F32, name="bank", tag="bank") for unit in units]
@@ -217,7 +228,7 @@ def tile_list_cortical_softplus_currents_kernel(
         for bank, (pair, n) in zip(banks, units):
             drain(bank, 1, pair, n)
 
-        wr_dealt = held([P, 2 * N + N // 4], I32, "slot_a")
+        wr_dealt = held([P, 2 * N + N // 4], I32, "dealt_1_1_b_codes")
         wr_w = [wr_dealt[:, a * N:(a + 1) * N] for a in range(2)]
         wr_sc = wr_dealt[:, 2 * N:].bitcast(U8)
         deal(nc.gpsimd, wr_sc, wr_sc_raw[:], 16)
@@ -227,44 +238,35 @@ def tile_list_cortical_softplus_currents_kernel(
         floor = keep.tile([P, 1], F32, name="floor", tag="bias")
         nc.vector.memset(floor[:], FLOOR)
         ys = [held([P, 4, 2, PACK, SUB], F32, "tab_w_%d" % half) for half in range(2)]
-        woven = held([P, 2, S, PACK], BF16, "y_woven")
+        woven = [held([P, 2, S // 2, PACK], BF16, name) for name in ("we_raw_0_1", "we_raw_1_1")]
         y_codes = held([P, 2, S], I32, "y_codes")
         y_scales = held([P, 2, S], U8, "y_scales")
         both, apart = (slice(0, 2),), (slice(0, 1), slice(1, 2))
         count = S // SUB
-        h, h_codes, h_scales, y_banks = {}, {}, {}, {}
-
-        def stretch(tiles, n):
-            return tiles[n // 2][:, (n % 2) * SPAN:(n % 2 + 1) * SPAN]
+        lns, h, h_codes, h_scales = {}, {}, {}, {}
 
         def logs(n, parts):
+            lns[n] = ring.tile([P, SPAN], F32, name="lns", bufs=AHEAD + 1, align_bytes=64)
+            src = sig[n // 2][:, (n % 2) * SPAN:(n % 2 + 1) * SPAN].rearrange("p (a g j e) -> p g j a e", a=2, g=2, e=2)
+            dst = lns[n][:].rearrange("p (g j a e) -> p g j a e", g=2, a=2, e=2)
             for gs in parts:
-                part = stretch(sig, n).rearrange("p (g c) -> p g c", g=2)[:, gs]
-                nc.scalar.activation(out=part, in_=part, func=ACT.Ln, bias=floor[:])
+                nc.scalar.activation(out=dst[:, gs], in_=src[:, gs], func=ACT.Ln, bias=floor[:])
 
-        def products(n, parts):
-            h[n] = ring.tile([P, SPAN], BF16, name="h", bufs=3, align_bytes=64)
+        def rates(n, parts):
+            h[n] = ring.tile([P, 2, SPAN // 2], BF16, name="h", align_bytes=64)
+            other = factor[n // 2][:].rearrange("p (g c k) -> p g c k", g=2, k=2)[:, :, :, n % 2]
             for gs in parts:
-                order = "p (a g j e) -> p g j a e" if n > 1 else "p (g a j e) -> p g j a e"
-                src = stretch(sig, n).rearrange(order, a=2, g=2, e=2)[:, gs]
-                factor = ng.rearrange("p g (a e) -> p g a e", e=2)[:, gs].unsqueeze(2).to_broadcast(src.shape)
-                nc.vector.tensor_tensor(out=h[n][:].rearrange("p (g j a e) -> p g j a e", g=2, a=2, e=2)[:, gs],
-                                        in0=src, in1=factor,
-                                        op=ALU.mult)
-
-        def maxima(n, parts):
-            for gs in parts:
-                pairs = h[n][:].rearrange("p (g j a e) -> p g j a e", g=2, a=2, e=2)[:, gs]
-                other = stretch(lin, n).rearrange("p (a g j e) -> p g j a e", a=2, g=2, e=2)[:, gs]
-                nc.vector.tensor_tensor(out=pairs, in0=pairs, in1=other, op=ALU.max)
+                nc.vector.scalar_tensor_tensor(
+                    out=h[n][:, gs], in0=lns[n][:].rearrange("p (g c) -> p g c", g=2)[:, gs], scalar=-KNEE,
+                    in1=other[:, gs], op0=ALU.max, op1=ALU.mult)
 
         def quantise_h(n, parts):
-            h_codes[n] = held([P, 2 * SUB], U32, "h_codes_%d" % n)
-            h_scales[n] = held([P, 2 * SUB], U8, "h_scales_%d" % n)
+            h_codes[n] = ring.tile([P, 2, SUB], U32, name="h_codes", bufs=4, align_bytes=64)
+            h_scales[n] = ring.tile([P, 2, SUB], U8, name="h_scales", bufs=4, align_bytes=64)
             for gs in parts:
-                cols = slice(gs.start * SUB, gs.stop * SUB)
-                nc.vector.quantize_mx(out=h_codes[n][:, cols].bitcast(FP8X4), scales=h_scales[n][:, cols],
-                                      in_=h[n][:, PACK * cols.start:PACK * cols.stop])
+                nc.vector.quantize_mx(out=h_codes[n][:, gs].rearrange("p g c -> p (g c)").bitcast(FP8X4),
+                                      scales=h_scales[n][:, gs].rearrange("p g c -> p (g c)"),
+                                      in_=h[n][:, gs].rearrange("p g c -> p (g c)"))
 
         def currents(n):
             for g in range(2):
@@ -275,29 +277,26 @@ def tile_list_cortical_softplus_currents_kernel(
                         nc.tensor.matmul_mx(
                             out=bank[:, t, :], lhsT=wr_w[a][:, u * P:(u + 1) * P].bitcast(FP8X4),
                             lhsT_scale=wr_sc[WR_FIRST + 4 * a:, u * P:(u + 1) * P],
-                            rhs=h_codes[n][:, a * SUB:(a + 1) * SUB].bitcast(FP8X4),
-                            rhs_scale=h_scales[n][:, a * SUB:(a + 1) * SUB], start=(a == 0), stop=(a == 1))
+                            rhs=h_codes[n][:, a, :].bitcast(FP8X4),
+                            rhs_scale=h_scales[n][:, a, :], start=(a == 0), stop=(a == 1))
                 nc.scalar.copy(out=ys[n // 4][:, n % 4, g], in_=bank[:])
-                y_banks[n, g] = bank
             for g in range(2):
                 rows = out_0[g * GROUP:(g + 1) * GROUP, n * SUB:(n + 1) * SUB].rearrange("(p t) j -> p t j", t=PACK)
                 nc.sync.dma_start(out=rows, in_=ys[n // 4][:, n % 4, g])
 
-        def weave_banks(n):
-            for g in range(2):
-                nc.scalar.copy(out=woven[:, g, n * SUB:(n + 1) * SUB, :], in_=y_banks[n, g][:].rearrange("p t c -> p c t"))
-
         def weave(n, parts):
+            js = slice((n % 4) * SUB, (n % 4 + 1) * SUB)
             for gs in parts:
                 nc.vector.tensor_copy(
-                    out=woven[:, gs, n * SUB:(n + 1) * SUB, :].rearrange("p g (c i) t -> p g c t i", i=4),
+                    out=woven[n // 4][:, gs, js, :].rearrange("p g (c i) t -> p g c t i", i=4),
                     in_=ys[n // 4][:, n % 4, gs].rearrange("p g t (c i) -> p g c t i", i=4))
 
         def quantise_y(first, last):
             js = slice(first * SUB, last * SUB)
+            part = slice((first % 4) * SUB, (first % 4 + last - first) * SUB)
             for g in range(2):
                 nc.vector.quantize_mx(out=y_codes[:, g, js].bitcast(FP8X4), scales=y_scales[:, g, js],
-                                      in_=woven[:, g, js, :].rearrange("p c t -> p (c t)"))
+                                      in_=woven[first // 4][:, g, part, :].rearrange("p c t -> p (c t)"))
 
         def store_words(first, last):
             js = slice(first * SUB, last * SUB)
@@ -312,26 +311,22 @@ def tile_list_cortical_softplus_currents_kernel(
         logs(0, apart)
         for n in range(1, AHEAD):
             logs(n, both)
-        products(0, apart)
-        maxima(0, apart)
+        rates(0, apart)
         quantise_h(0, apart)
-        products(1, apart)
+        rates(1, both)
         for n in range(count):
             if n > 0:
-                maxima(n, apart if n == 1 else both)
                 if n + 1 < count:
-                    products(n + 1, both)
+                    rates(n + 1, both)
                 else:
-                    weave(4, both)
+                    weave(n - 1 - LAG, both)
                 quantise_h(n, both)
             currents(n)
             if n + AHEAD < count:
                 logs(n + AHEAD, both)
-            if n - 3 in FROM_PSUM:
-                weave_banks(n - 3)
-            if n - EARLY in (0, 1):
-                weave(n - EARLY, both)
-            if n - EARLY == 2:
+            if LAG <= n < count - 2:
+                weave(n - LAG, both)
+            if n - LAG == 2:
                 quantise_y(0, 2)
                 store_words(0, 2)
         quantise_y(2, 4)

@@ -191,9 +191,8 @@ def tile_list_cortical_softplus_currents_kernel(
                                     start=(kind == 2 and e == 0), stop=(kind == 1 and e == 1))
 
         def drain(bank, g, pair, n):
-            sig_out = sig[n][:].rearrange("p (k a g j e) -> p k a g j e", k=2, a=2, g=2, e=2)[:, :, pair, g, :, :]
-            nc.scalar.activation(out=sig_out, in_=bank[:].rearrange("p e (k j) -> p k j e", k=2),
-                                 func=ACT.Sigmoid, bias=zero[:])
+            sig_out = sig[n][:].rearrange("p (g a j e) -> p g a j e", g=2, a=2, e=2)[:, g, pair]
+            nc.scalar.activation(out=sig_out, in_=bank[:].rearrange("p e j -> p j e"), func=ACT.Sigmoid, bias=zero[:])
             out = factor[n][:].rearrange("p (g j a c) -> p g j a c", g=2, a=2, c=4)[:, g, :, pair, :]
             first = g * PACK + 2 * pair
             slopes = slope[:, first:first + 2, :].rearrange("p e k -> p (e k)").unsqueeze(1).to_broadcast([P, SUB, 4])
@@ -237,106 +236,142 @@ def tile_list_cortical_softplus_currents_kernel(
 
         floor = keep.tile([P, 1], F32, name="floor", tag="bias")
         nc.vector.memset(floor[:], FLOOR)
-        ys = [held([P, 4, 2, PACK, SUB], F32, "tab_w_%d" % half) for half in range(2)]
+        ys = [held([P, 2, 2, PACK, QUARTER], F32, "tab_w_%d" % half) for half in range(2)]
         woven = [held([P, 2, S // 2, PACK], BF16, name) for name in ("we_raw_0_1", "we_raw_1_1")]
         y_codes = held([P, 2, S], I32, "y_codes")
-        y_scales = held([P, 2, S], U8, "y_scales")
-        both, apart = (slice(0, 2),), (slice(0, 1), slice(1, 2))
-        count = S // SUB
+        y_scales = held([P, S], U8, "y_scales")
+        whole = slice(0, QUARTER)
+        halves = (slice(0, SUB), slice(SUB, QUARTER))
         lns, h, h_codes, h_scales = {}, {}, {}, {}
+        for n in range(quarters):
+            h_codes[n] = held([P, 2, QUARTER], U32, "h_codes_%d" % n)
+            h_scales[n] = held([P, 2, QUARTER], U8, "h_scales_%d" % n)
 
-        def logs(n, parts):
-            lns[n] = ring.tile([P, SPAN], F32, name="lns", bufs=AHEAD + 1, align_bytes=64)
-            src = sig[n // 2][:, (n % 2) * SPAN:(n % 2 + 1) * SPAN].rearrange("p (a g j e) -> p g j a e", a=2, g=2, e=2)
-            dst = lns[n][:].rearrange("p (g j a e) -> p g j a e", g=2, a=2, e=2)
-            for gs in parts:
-                nc.scalar.activation(out=dst[:, gs], in_=src[:, gs], func=ACT.Ln, bias=floor[:])
+        def logs(n, g, js):
+            if js.start == 0:
+                lns[n, g] = ring.tile([P, QUARTER, 2, 2], F32, name="lns", bufs=5, align_bytes=64)
+            src = sig[n][:].rearrange("p (g a j e) -> p g j a e", g=2, a=2, e=2)[:, g, js]
+            nc.scalar.activation(out=lns[n, g][:, js], in_=src, func=ACT.Ln, bias=floor[:])
 
-        def rates(n, parts):
-            h[n] = ring.tile([P, 2, SPAN // 2], BF16, name="h", align_bytes=64)
-            other = factor[n // 2][:].rearrange("p (g c k) -> p g c k", g=2, k=2)[:, :, :, n % 2]
-            for gs in parts:
-                nc.vector.scalar_tensor_tensor(
-                    out=h[n][:, gs], in0=lns[n][:].rearrange("p (g c) -> p g c", g=2)[:, gs], scalar=-KNEE,
-                    in1=other[:, gs], op0=ALU.max, op1=ALU.mult)
+        def rates(n, g, js):
+            if js.start == 0:
+                h[n, g] = ring.tile([P, 2, SUB * PACK], BF16, name="h", bufs=4, align_bytes=64)
+            ks = slice(js.start // SUB, js.stop // SUB)
+            other = factor[n][:].rearrange("p (g c k) -> p g k c", g=2, k=2)[:, g, ks]
+            nc.vector.scalar_tensor_tensor(
+                out=h[n, g][:, ks], in0=lns[n, g][:].rearrange("p (k j) a e -> p k (j a e)", k=2)[:, ks],
+                scalar=-KNEE, in1=other, op0=ALU.max, op1=ALU.mult)
 
-        def quantise_h(n, parts):
-            h_codes[n] = ring.tile([P, 2, SUB], U32, name="h_codes", bufs=4, align_bytes=64)
-            h_scales[n] = ring.tile([P, 2, SUB], U8, name="h_scales", bufs=4, align_bytes=64)
-            for gs in parts:
-                nc.vector.quantize_mx(out=h_codes[n][:, gs].rearrange("p g c -> p (g c)").bitcast(FP8X4),
-                                      scales=h_scales[n][:, gs].rearrange("p g c -> p (g c)"),
-                                      in_=h[n][:, gs].rearrange("p g c -> p (g c)"))
+        def quantise_h(n, g, js):
+            ks = slice(js.start // SUB, js.stop // SUB)
+            nc.vector.quantize_mx(out=h_codes[n][:, g, js].bitcast(FP8X4), scales=h_scales[n][:, g, js],
+                                  in_=h[n, g][:, ks].rearrange("p k c -> p (k c)"))
 
-        def currents(n):
-            for g in range(2):
-                bank = psum.tile([P, PACK, SUB], F32, name="bank", tag="bank")
-                for t in range(PACK):
-                    u = g * PACK + t
-                    for a in range(2):
-                        nc.tensor.matmul_mx(
-                            out=bank[:, t, :], lhsT=wr_w[a][:, u * P:(u + 1) * P].bitcast(FP8X4),
-                            lhsT_scale=wr_sc[WR_FIRST + 4 * a:, u * P:(u + 1) * P],
-                            rhs=h_codes[n][:, a, :].bitcast(FP8X4),
-                            rhs_scale=h_scales[n][:, a, :], start=(a == 0), stop=(a == 1))
-                nc.scalar.copy(out=ys[n // 4][:, n % 4, g], in_=bank[:])
-            for g in range(2):
-                rows = out_0[g * GROUP:(g + 1) * GROUP, n * SUB:(n + 1) * SUB].rearrange("(p t) j -> p t j", t=PACK)
-                nc.sync.dma_start(out=rows, in_=ys[n // 4][:, n % 4, g])
+        def current(out, u, a, n, js, start, stop):
+            nc.tensor.matmul_mx(
+                out=out, lhsT=wr_w[a][:, u * P:(u + 1) * P].bitcast(FP8X4),
+                lhsT_scale=wr_sc[WR_FIRST + 4 * a:, u * P:(u + 1) * P],
+                rhs=h_codes[n][:, a, js].bitcast(FP8X4), rhs_scale=h_scales[n][:, a, js], start=start, stop=stop)
 
-        def weave(n, parts):
-            js = slice((n % 4) * SUB, (n % 4 + 1) * SUB)
-            for gs in parts:
-                nc.vector.tensor_copy(
-                    out=woven[n // 4][:, gs, js, :].rearrange("p g (c i) t -> p g c t i", i=4),
-                    in_=ys[n // 4][:, n % 4, gs].rearrange("p g t (c i) -> p g c t i", i=4))
+        def store_y(n, g, ts, js):
+            rows = out_0[g * GROUP:(g + 1) * GROUP, n * QUARTER:(n + 1) * QUARTER].rearrange("(p t) j -> p t j", t=PACK)
+            nc.sync.dma_start(out=rows[:, ts, js], in_=ys[n // 2][:, n % 2, g, ts, js])
 
-        def quantise_y(first, last):
-            js = slice(first * SUB, last * SUB)
-            part = slice((first % 4) * SUB, (first % 4 + last - first) * SUB)
-            for g in range(2):
-                nc.vector.quantize_mx(out=y_codes[:, g, js].bitcast(FP8X4), scales=y_scales[:, g, js],
-                                      in_=woven[first // 4][:, g, part, :].rearrange("p c t -> p (c t)"))
+        def narrow(n, g, js):
+            bank = psum.tile([P, PACK, SUB], F32, name="bank", tag="bank")
+            for t in range(PACK):
+                for a in range(2):
+                    current(bank[:, t, :], g * PACK + t, a, n, js, a == 0, a == 1)
+            nc.scalar.copy(out=ys[n // 2][:, n % 2, g, :, js], in_=bank[:])
+            store_y(n, g, slice(0, PACK), js)
 
-        def store_words(first, last):
-            js = slice(first * SUB, last * SUB)
+        def wide(n, g):
+            pair_banks = [psum.tile([P, 2, QUARTER], F32, name="bank", tag="bank") for pair in range(2)]
+            for a in range(2):
+                for pair in range(2):
+                    for e in range(2):
+                        current(pair_banks[pair][:, e, :], g * PACK + 2 * pair + e, a, n, whole,
+                                a == 0 and e == 0, a == 1 and e == 1)
+            for pair in range(2):
+                ts = slice(2 * pair, 2 * pair + 2)
+                nc.scalar.copy(out=ys[n // 2][:, n % 2, g, ts, :], in_=pair_banks[pair][:])
+                store_y(n, g, ts, whole)
+
+        def weave(n, gs, js):
+            first = (n % 2) * QUARTER
+            nc.vector.tensor_copy(
+                out=woven[n // 2][:, gs, first + js.start:first + js.stop, :].rearrange("p g (c i) t -> p g c t i", i=4),
+                in_=ys[n // 2][:, n % 2, gs, :, js].rearrange("p g t (c i) -> p g c t i", i=4))
+
+        def quantise_y(n, g):
+            js = slice(n * QUARTER, (n + 1) * QUARTER)
+            part = slice((n % 2) * QUARTER, (n % 2 + 1) * QUARTER)
+            nc.vector.quantize_mx(out=y_codes[:, g, js].bitcast(FP8X4), scales=y_scales[4 * g:, js],
+                                  in_=woven[n // 2][:, g, part, :].rearrange("p c t -> p (c t)"))
+
+        def store_words(n):
+            js = slice(n * QUARTER, (n + 1) * QUARTER)
             words = out_1.rearrange("g p j t -> p g (j t)").bitcast(I32)
             nc.sync.dma_start(out=words[:, :, js], in_=y_codes[:, :, js])
 
         def store_scales():
-            for r in range(4):
-                nc.sync.dma_start(out=out_2[:, r:16:4, :].bitcast(I32).rearrange("g q c -> q g c"),
-                                  in_=y_scales[r:P:32, :, :].bitcast(I32))
+            for q in range(4):
+                nc.sync.dma_start(out=out_2[:, 4 * q:4 * q + 4, :].bitcast(I32),
+                                  in_=y_scales[32 * q:32 * q + 8, :].bitcast(I32))
 
-        logs(0, apart)
-        for n in range(1, AHEAD):
-            logs(n, both)
-        rates(0, apart)
-        quantise_h(0, apart)
-        rates(1, both)
-        for n in range(count):
-            if n > 0:
-                if n + 1 < count:
-                    rates(n + 1, both)
-                else:
-                    weave(n - 1 - LAG, both)
-                quantise_h(n, both)
-            currents(n)
-            if n + AHEAD < count:
-                logs(n + AHEAD, both)
-            if LAG <= n < count - 2:
-                weave(n - LAG, both)
-            if n - LAG == 2:
-                quantise_y(0, 2)
-                store_words(0, 2)
-        quantise_y(2, 4)
-        store_words(2, 4)
-        weave(5, both)
-        weave(6, both)
-        quantise_y(4, 6)
-        quantise_y(6, 7)
-        store_words(4, 7)
-        weave(7, apart)
-        quantise_y(7, 8)
-        store_words(7, 8)
+        both, group = slice(0, 2), (slice(0, 1), slice(1, 2))
+        for js in halves:
+            for g in range(2):
+                logs(0, g, js)
+        for g in range(2):
+            logs(1, g, whole)
+        for js in halves:
+            for g in range(2):
+                rates(0, g, js)
+            for g in range(2):
+                quantise_h(0, g, js)
+        for g in range(2):
+            narrow(0, g, halves[0])
+        logs(2, 0, whole)
+        for g in range(2):
+            rates(1, g, whole)
+        for g in range(2):
+            quantise_h(1, g, whole)
+        for g in range(2):
+            narrow(0, g, halves[1])
+        logs(2, 1, whole)
+        weave(0, both, halves[0])
+        rates(2, 0, whole)
+        weave(0, both, halves[1])
+        quantise_h(2, 0, whole)
+        wide(1, 0)
+        logs(3, 0, whole)
+        rates(2, 1, whole)
+        quantise_y(0, 0)
+        quantise_h(2, 1, whole)
+        quantise_y(0, 1)
+        store_words(0)
+        wide(1, 1)
+        logs(3, 1, whole)
+        rates(3, 0, whole)
+        weave(1, group[0], whole)
+        quantise_h(3, 0, whole)
+        wide(2, 0)
+        wide(2, 1)
+        rates(3, 1, whole)
+        quantise_y(1, 0)
+        quantise_h(3, 1, whole)
+        wide(3, 0)
+        wide(3, 1)
+        weave(1, group[1], whole)
+        last = (1, 1)
+        for n in (2, 3):
+            for g in range(2):
+                weave(n, group[g], whole)
+                quantise_y(*last)
+                if last[1] == 1:
+                    store_words(last[0])
+                last = (n, g)
+        quantise_y(*last)
+        store_words(3)
         store_scales()

@@ -23,6 +23,7 @@ SPAN = 2 * SUB * PACK
 AHEAD = 4
 LAG = 2
 WR_FIRST = 8
+V_FIRST = (4, 8)
 FLOOR = 2.0 ** -60
 KNEE = 16.0
 FLOPS = 5368709120
@@ -74,9 +75,9 @@ def tile_list_cortical_softplus_currents_kernel(
                 rows = tile[32 * q + first:32 * q + first + 8, :]
                 nc.sync.dma_start(out=rows.bitcast(I32), in_=scales[:, 4 * q:4 * q + 4, :].bitcast(I32))
 
-        def load_plane(tile, scales, rows=range(4)):
+        def load_plane(tile, scales, rows=range(4), first=0):
             for r in rows:
-                nc.sync.dma_start(out=tile[r:P:32, :].bitcast(I32), in_=scales[r:16:4, :].bitcast(I32))
+                nc.sync.dma_start(out=tile[first + r:P:32, :].bitcast(I32), in_=scales[r:16:4, :].bitcast(I32))
 
         tab2_w = held([P, T2], I32, "tab2_w")
         tab_w = [held([P, T], I32, "tab_w_%d" % a) for a in range(2)]
@@ -98,10 +99,10 @@ def tile_list_cortical_softplus_currents_kernel(
         load_plane(v2_sc, v2_rows[0:P:8, :])
         load_plane(wi_sc_raw, wi_scales[0], range(2, 4))
         load_words(tab_w[0], tab_words[0], T // 2, T)
-        load_plane(v_sc[0], v_rows[0:P // 2:4, :])
+        load_plane(v_sc[0], v_rows[0:P // 2:4, :], first=V_FIRST[0])
         raw_1_0 = load_we(1, 0, GROUP, "we_raw_1_0")
         load_words(tab_w[1], tab_words[1], 0, T // 2)
-        load_plane(v_sc[1], v_rows[P // 2:P:4, :])
+        load_plane(v_sc[1], v_rows[P // 2:P:4, :], first=V_FIRST[1])
         gain_sb = held([P, 2, PACK], F32, "gain_sb")
         nc.sync.dma_start(out=gain_sb[:], in_=gain.rearrange("(g p t) -> p g t", g=2, t=PACK))
         load_words(tab_w[1], tab_words[1], T // 2, T)
@@ -185,7 +186,7 @@ def tile_list_cortical_softplus_currents_kernel(
                 else:
                     codes, lhs_sc = we_q[kind, g][t]
                     lhs = codes.bitcast(FP8X4)
-                    rhs, rhs_sc = v_w[kind][n], v_sc[kind][:, js]
+                    rhs, rhs_sc = v_w[kind][n], v_sc[kind][V_FIRST[kind]:, js]
                 nc.tensor.matmul_mx(out=bank[:, e, :], lhsT=lhs, lhsT_scale=lhs_sc,
                                     rhs=rhs.bitcast(FP8X4), rhs_scale=rhs_sc,
                                     start=(kind == 2 and e == 0), stop=(kind == 1 and e == 1))
@@ -309,10 +310,10 @@ def tile_list_cortical_softplus_currents_kernel(
             nc.vector.quantize_mx(out=y_codes[:, g, js].bitcast(FP8X4), scales=y_scales[4 * g:, js],
                                   in_=woven[n // 2][:, g, part, :].rearrange("p c t -> p (c t)"))
 
-        def store_words(n):
+        def store_words(n, gs=slice(0, 2)):
             js = slice(n * QUARTER, (n + 1) * QUARTER)
             words = out_1.rearrange("g p j t -> p g (j t)").bitcast(I32)
-            nc.sync.dma_start(out=words[:, :, js], in_=y_codes[:, :, js])
+            nc.sync.dma_start(out=words[:, gs, js], in_=y_codes[:, gs, js])
 
         def store_scales():
             for q in range(4):
@@ -364,14 +365,18 @@ def tile_list_cortical_softplus_currents_kernel(
         wide(3, 0)
         wide(3, 1)
         weave(1, group[1], whole)
-        last = (1, 1)
-        for n in (2, 3):
-            for g in range(2):
-                weave(n, group[g], whole)
-                quantise_y(*last)
-                if last[1] == 1:
-                    store_words(last[0])
-                last = (n, g)
-        quantise_y(*last)
-        store_words(3)
+        weave(2, group[0], whole)
+        quantise_y(1, 1)
+        store_words(1)
+        weave(2, group[1], whole)
+        quantise_y(2, 0)
+        weave(3, group[0], whole)
+        quantise_y(2, 1)
+        store_words(2)
+        weave(3, group[1], halves[0])
+        nc.scalar.copy(out=woven[1][:, 1, QUARTER + SUB:, :].rearrange("p (c i) t -> p c t i", i=4),
+                       in_=ys[1][:, 1, 1, :, SUB:].rearrange("p t (c i) -> p c t i", i=4))
+        for g in range(2):
+            quantise_y(3, g)
+            store_words(3, group[g])
         store_scales()

@@ -84,9 +84,9 @@ def tile_list_cortical_softplus_currents_kernel(
         nc.sync.dma_start(idx2[:], offs2)
         load_words(tab2_w, tab2_words[0], 0, T2 // 2)
         nc.sync.dma_start(out=tab2_sc[0:P:8, :].bitcast(I32), in_=tab2_scales[0].bitcast(I32))
+        load_words(tab2_w, tab2_words[0], T2 // 2, T2)
         nc.sync.dma_start(idx[:], offs)
         nc.sync.dma_start(out=tab_sc[0:P:4, :].bitcast(I32), in_=tab_scales.rearrange("a q c -> (a q) c").bitcast(I32))
-        load_words(tab2_w, tab2_words[0], T2 // 2, T2)
         load_words(tab_w[0], tab_words[0], 0, T // 2)
         wi_raw = held([P, 2 * H], U8, "wi_raw")
         nc.sync.dma_start(out=wi_raw[:].bitcast(I32), in_=wi_words[0].bitcast(I32))
@@ -103,8 +103,8 @@ def tile_list_cortical_softplus_currents_kernel(
         raw_1_0 = load_we(1, 0, GROUP, "we_raw_1_0")
         load_words(tab_w[1], tab_words[1], 0, T // 2)
         load_plane(v_sc[1], v_rows[P // 2:P:4, :], first=V_FIRST[1])
-        gain_sb = held([P, 2, PACK], F32, "gain_sb")
-        nc.sync.dma_start(out=gain_sb[:], in_=gain.rearrange("(g p t) -> p g t", g=2, t=PACK))
+        gain_sb = held([P, 2, 2 * PACK], F32, "gain_sb")
+        nc.sync.dma_start(out=gain_sb[:, :, 0:PACK], in_=gain.rearrange("(g p t) -> p g t", g=2, t=PACK))
         load_words(tab_w[1], tab_words[1], T // 2, T)
         raw_0_1 = load_we(0, GROUP, GROUP, "we_raw_0_1")
         raw_1_1 = load_we(1, GROUP, GROUP, "we_raw_1_1")
@@ -162,8 +162,8 @@ def tile_list_cortical_softplus_currents_kernel(
         round_we(nc.scalar, dealt_1_0[:], raw_1_0, 0)
         we_q[1, 0] = quantise_we(dealt_1_0[:], "dealt_1_1_b")
         slope = held([P, 2 * PACK, 2], F32, "slope")
-        nc.scalar.activation(out=slope[:], func=ACT.Copy, scale=1.0 / KNEE,
-                             in_=gain_sb[:].rearrange("p g t -> p (g t)").unsqueeze(2).to_broadcast([P, 2 * PACK, 2]))
+        nc.scalar.activation(out=slope[:].rearrange("p (g t) k -> p g t k", g=2), func=ACT.Copy, scale=1.0 / KNEE,
+                             in_=gain_sb[:, :, 0:PACK].unsqueeze(3).to_broadcast([P, 2, PACK, 2]))
         v_w.append([gather_words(tab_w[1], idx, n, name, QUARTER)[0]
                     for n, name in enumerate(("dealt_1_0", "v_w_1_1", "v_w_1_2", "v_w_1_3"))])
 

@@ -280,9 +280,9 @@ def tile_list_cortical_softplus_currents_kernel(
 
         def narrow(n, g, js):
             bank = psum.tile([P, PACK, SUB], F32, name="bank", tag="bank")
-            for t in range(PACK):
-                for a in range(2):
-                    current(bank[:, t, :], g * PACK + t, a, n, js, a == 0, a == 1)
+            for a in range(2):
+                for t in range(PACK):
+                    current(bank[:, t, :], g * PACK + t, a, n, js, a == 0 and t == 0, a == 1 and t == PACK - 1)
             nc.scalar.copy(out=ys[n // 2][:, n % 2, g, :, js], in_=bank[:])
             store_y(n, g, slice(0, PACK), js)
 

@@ -20,8 +20,6 @@ T, T2, S, H, N = 4096, 2048, 1024, 1024, 1024
 QUARTER = 256
 SUB = 128
 SPAN = 2 * SUB * PACK
-AHEAD = 4
-LAG = 2
 WR_FIRST = 8
 V_FIRST = (4, 8)
 FLOOR = 2.0 ** -60
@@ -169,7 +167,6 @@ def tile_list_cortical_softplus_currents_kernel(
 
         dealt_0_1 = late.tile([P, PACK, P, PACK], BF16, name="dealt_0_1", align_bytes=64, offset=0)
         round_we(nc.gpsimd, dealt_0_1[:], raw_0_1, 0)
-        early = late.tile([P, 2, P, PACK], BF16, name="early", align_bytes=64, offset=4096)
 
         quarters = S // QUARTER
         sig = [held([P, 2 * SPAN], F32, "sig_%d" % n if n > 1 else "we_raw_%d_0" % n) for n in range(quarters)]
@@ -209,9 +206,11 @@ def tile_list_cortical_softplus_currents_kernel(
         factor[1] = held([P, 2 * SPAN], F32, "factor_1")
         for u in range(4):
             drain(banks[u], 0, *units[u])
+        early = late.tile([P, 2, P, PACK], BF16, name="early", align_bytes=64, offset=4096)
         round_we(nc.vector, early[:], raw_1_1, 0)
-        we_q[0, 1] = quantise_we(dealt_0_1[:], "we_0_1")
+        we_q[0, 1] = quantise_we(dealt_0_1[:, 0:2], "we_0_1_a")
         we_q[1, 1] = quantise_we(early[:], "we_1_1_a")
+        we_q[0, 1].extend(quantise_we(dealt_0_1[:, 2:4], "we_0_1_b"))
         factor[2] = late.tile([P, 2 * SPAN], F32, name="factor_2", align_bytes=64, offset=0)
         factor[3] = held([P, 2 * SPAN], F32, "factor_3")
         for u in range(4, 8):

@@ -136,9 +136,10 @@ def tile_list_cortical_softplus_currents_kernel(
             else:
                 engine.tensor_scalar(out=dst, in0=src, scalar1=-1.0, scalar2=0.0, op0=ALU.mult, op1=ALU.add)
 
-        def quantise_we(dealt, name):
+        def quantise_we(dealt, name, codes=None):
             width = dealt.shape[1] * P
-            codes = held([P, width], U32, name + "_codes")
+            if codes is None:
+                codes = held([P, width], U32, name + "_codes")
             scales = held([P, width], U8, name + "_scales")
             nc.vector.quantize_mx(out=codes[:].bitcast(FP8X4), scales=scales[:],
                                   in_=dealt.rearrange("p t m i -> p (t m i)"))
@@ -166,7 +167,8 @@ def tile_list_cortical_softplus_currents_kernel(
                     for n, name in enumerate(("dealt_1_0", "v_w_1_1", "v_w_1_2", "v_w_1_3"))])
 
         dealt_0_1 = late.tile([P, PACK, P, PACK], BF16, name="dealt_0_1", align_bytes=64, offset=0)
-        round_we(nc.gpsimd, dealt_0_1[:], raw_0_1, 0)
+        for first in (0, 2):
+            round_we(nc.gpsimd, dealt_0_1[:, first:first + 2], raw_0_1, first)
 
         quarters = S // QUARTER
         sig = [held([P, 2 * SPAN], F32, "sig_%d" % n if n > 1 else "we_raw_%d_0" % n) for n in range(quarters)]
@@ -189,8 +191,14 @@ def tile_list_cortical_softplus_currents_kernel(
                                     start=(kind == 2 and e == 0), stop=(kind == 1 and e == 1))
 
         def drain(bank, g, pair, n):
+            sigmoid(bank, g, pair, n)
+            linear(bank, g, pair, n)
+
+        def sigmoid(bank, g, pair, n):
             sig_out = sig[n][:].rearrange("p (g a j e) -> p g a j e", g=2, a=2, e=2)[:, g, pair]
             nc.scalar.activation(out=sig_out, in_=bank[:].rearrange("p e j -> p j e"), func=ACT.Sigmoid, bias=zero[:])
+
+        def linear(bank, g, pair, n):
             out = factor[n][:].rearrange("p (g j a c) -> p g j a c", g=2, a=2, c=4)[:, g, :, pair, :]
             first = g * PACK + 2 * pair
             slopes = slope[:, first:first + 2, :].rearrange("p e k -> p (e k)").unsqueeze(1).to_broadcast([P, SUB, 4])
@@ -206,18 +214,22 @@ def tile_list_cortical_softplus_currents_kernel(
         factor[1] = held([P, 2 * SPAN], F32, "factor_1")
         for u in range(4):
             drain(banks[u], 0, *units[u])
-        early = late.tile([P, 2, P, PACK], BF16, name="early", align_bytes=64, offset=4096)
-        round_we(nc.vector, early[:], raw_1_1, 0)
+        early = late.tile([P, 2, P, PACK], BF16, name="early", align_bytes=64, offset=7680)
         we_q[0, 1] = quantise_we(dealt_0_1[:, 0:2], "we_0_1_a")
-        we_q[1, 1] = quantise_we(early[:], "we_1_1_a")
+        round_we(nc.vector, early[:], raw_1_1, 0)
         we_q[0, 1].extend(quantise_we(dealt_0_1[:, 2:4], "we_0_1_b"))
+        we_q[1, 1] = quantise_we(early[:], "we_1_1_a")
         factor[2] = late.tile([P, 2 * SPAN], F32, name="factor_2", align_bytes=64, offset=0)
-        factor[3] = held([P, 2 * SPAN], F32, "factor_3")
+        factor[3] = late.tile([P, 2 * SPAN], F32, name="factor_3", align_bytes=64, offset=9216)
         for u in range(4, 8):
-            drain(banks[u], 0, *units[u])
+            sigmoid(banks[u], 0, *units[u])
         final = held([P, 2, P, PACK], BF16, "dealt_1_1_b_codes")
         round_we(nc.scalar, final[:], raw_1_1, 2)
-        we_q[1, 1].extend(quantise_we(final[:], "we_1_1_b"))
+        for u in range(4, 6):
+            linear(banks[u], 0, *units[u])
+        we_q[1, 1].extend(quantise_we(final[:], "we_1_1_b", late.tile([P, 2 * P], U32, name="last_codes", align_bytes=64, offset=8192)))
+        for u in range(6, 8):
+            linear(banks[u], 0, *units[u])
 
         units = [(pair, n) for pair in range(2) for n in range(quarters)]
         banks = [psum.tile([P, 2, QUARTER], F32, name="bank", tag="bank") for unit in units]
@@ -235,7 +247,7 @@ def tile_list_cortical_softplus_currents_kernel(
             deal(nc.gpsimd, wr_w[a], wr_raw[a][:], 4)
 
         floor = keep.tile([P, 1], F32, name="floor", tag="bias")
-        nc.vector.memset(floor[:], FLOOR)
+        nc.gpsimd.memset(floor[:], FLOOR)
         ys = [held([P, 2, 2, PACK, QUARTER], F32, "tab_w_%d" % half) for half in range(2)]
         woven = [held([P, 2, S // 2, PACK], BF16, name) for name in ("we_raw_0_1", "we_raw_1_1")]
         y_codes = held([P, 2, S], I32, "y_codes")

@@ -24,6 +24,7 @@ WR_FIRST = 8
 V_FIRST = (4, 8)
 FLOOR = 2.0 ** -60
 KNEE = 16.0
+LOG_SLOTS = 5
 FLOPS = 5368709120
 
 
@@ -49,8 +50,10 @@ def tile_list_cortical_softplus_currents_kernel(
         tab2_sc = held([P, T2], U8, "tab2_sc")
         wi_sc_raw = held([P, H], U8, "wi_sc_raw")
         wr_sc_raw = held([P, N], U8, "wr_sc_raw")
-        zero = keep.tile([P, 1], F32, name="zero", tag="bias")
+        zero = held([P, 1], F32, "lns")
         nc.gpsimd.memset(zero[:], 0.0)
+        floor = held([P, 1], F32, "floor")
+        nc.gpsimd.memset(floor[:], FLOOR)
         nc.gpsimd.memset(tab_sc[:].bitcast(I32), 0)
         nc.vector.memset(tab2_sc[:].bitcast(I32), 0)
         v2_sc = held([P, S], U8, "v2_sc")
@@ -58,8 +61,11 @@ def tile_list_cortical_softplus_currents_kernel(
         for plane in [v2_sc, wi_sc_raw, wr_sc_raw] + v_sc:
             nc.vector.memset(plane[:].bitcast(I32), 0)
 
-        def load_we(a, first, width, name):
-            raw = held([P, PACK, width], F32, name)
+        def load_we(a, first, width, name, offset=None):
+            if offset is None:
+                raw = held([P, PACK, width], F32, name)
+            else:
+                raw = late.tile([P, PACK, width], F32, name=name, align_bytes=64, offset=offset)
             rows = we[a * GROUP:(a + 1) * GROUP, first:first + width].rearrange("(p i) c -> p i c", i=PACK)
             nc.sync.dma_start(out=raw[:], in_=rows)
             return raw
@@ -104,7 +110,7 @@ def tile_list_cortical_softplus_currents_kernel(
         gain_sb = held([P, 2, 2 * PACK], F32, "gain_sb")
         nc.sync.dma_start(out=gain_sb[:, :, 0:PACK], in_=gain.rearrange("(g p t) -> p g t", g=2, t=PACK))
         load_words(tab_w[1], tab_words[1], T // 2, T)
-        raw_0_1 = load_we(0, GROUP, GROUP, "we_raw_0_1")
+        raw_0_1 = load_we(0, GROUP, GROUP, "we_raw_0_1", 7168)
         raw_1_1 = load_we(1, GROUP, GROUP, "we_raw_1_1")
         load_plane_pair(wr_sc_raw, wr_scales, WR_FIRST)
         wr_raw = [held([P, N], I32, "wr_raw_%d" % a) for a in range(2)]
@@ -167,8 +173,7 @@ def tile_list_cortical_softplus_currents_kernel(
                     for n, name in enumerate(("dealt_1_0", "v_w_1_1", "v_w_1_2", "v_w_1_3"))])
 
         dealt_0_1 = late.tile([P, PACK, P, PACK], BF16, name="dealt_0_1", align_bytes=64, offset=0)
-        for first in (0, 2):
-            round_we(nc.gpsimd, dealt_0_1[:, first:first + 2], raw_0_1, first)
+        round_we(nc.gpsimd, dealt_0_1[:], raw_0_1, 0)
 
         quarters = S // QUARTER
         sig = [held([P, 2 * SPAN], F32, "sig_%d" % n if n > 1 else "we_raw_%d_0" % n) for n in range(quarters)]
@@ -246,8 +251,7 @@ def tile_list_cortical_softplus_currents_kernel(
         for a in range(2):
             deal(nc.gpsimd, wr_w[a], wr_raw[a][:], 4)
 
-        floor = keep.tile([P, 1], F32, name="floor", tag="bias")
-        nc.gpsimd.memset(floor[:], FLOOR)
+        lns_all = held([P, LOG_SLOTS, QUARTER, 2, 2], F32, "lns")
         ys = [held([P, 2, 2, PACK, QUARTER], F32, "tab_w_%d" % half) for half in range(2)]
         woven = [held([P, 2, S // 2, PACK], BF16, name) for name in ("we_raw_0_1", "we_raw_1_1")]
         y_codes = held([P, 2, S], I32, "y_codes")
@@ -261,7 +265,7 @@ def tile_list_cortical_softplus_currents_kernel(
 
         def logs(n, g, js):
             if js.start == 0:
-                lns[n, g] = ring.tile([P, QUARTER, 2, 2], F32, name="lns", bufs=5, align_bytes=64)
+                lns[n, g] = lns_all[:, len(lns) % LOG_SLOTS]
             src = sig[n][:].rearrange("p (g a j e) -> p g j a e", g=2, a=2, e=2)[:, g, js]
             nc.scalar.activation(out=lns[n, g][:, js], in_=src, func=ACT.Ln, bias=floor[:])
 
@@ -271,7 +275,7 @@ def tile_list_cortical_softplus_currents_kernel(
             ks = slice(js.start // SUB, js.stop // SUB)
             other = factor[n][:].rearrange("p (g c k) -> p g k c", g=2, k=2)[:, g, ks]
             nc.vector.scalar_tensor_tensor(
-                out=h[n, g][:, ks], in0=lns[n, g][:].rearrange("p (k j) a e -> p k (j a e)", k=2)[:, ks],
+                out=h[n, g][:, ks], in0=lns[n, g].rearrange("p (k j) a e -> p k (j a e)", k=2)[:, ks],
                 scalar=-KNEE, in1=other, op0=ALU.max, op1=ALU.mult)
 
         def quantise_h(n, g, js):

@@ -60,6 +60,8 @@ def tile_list_cortical_softplus_currents_kernel(
         v_sc = [held([P, S], U8, "v_sc_%d" % a) for a in range(2)]
         for plane in [v2_sc, wi_sc_raw, wr_sc_raw] + v_sc:
             nc.vector.memset(plane[:].bitcast(I32), 0)
+        gain_rows = held([P, P], F32, "gain_rows")
+        nc.vector.memset(gain_rows[:], 0.0)
 
         def load_we(a, first, width, name, offset=None):
             if offset is None:
@@ -107,8 +109,7 @@ def tile_list_cortical_softplus_currents_kernel(
         raw_1_0 = load_we(1, 0, GROUP, "we_raw_1_0")
         load_words(tab_w[1], tab_words[1], 0, T // 2)
         load_plane(v_sc[1], v_rows[P // 2:P:4, :], first=V_FIRST[1])
-        gain_sb = held([P, 2, 2 * PACK], F32, "gain_sb")
-        nc.sync.dma_start(out=gain_sb[:, :, 0:PACK], in_=gain.rearrange("(g p t) -> p g t", g=2, t=PACK))
+        nc.sync.dma_start(out=gain_rows[0:P:16, :], in_=gain.rearrange("(g q c) -> q g c", g=2, q=4))
         load_words(tab_w[1], tab_words[1], T // 2, T)
         raw_0_1 = load_we(0, GROUP, GROUP, "we_raw_0_1", 7168)
         raw_1_1 = load_we(1, GROUP, GROUP, "we_raw_1_1")
@@ -166,9 +167,15 @@ def tile_list_cortical_softplus_currents_kernel(
         dealt_1_0 = held([P, PACK, P, PACK], BF16, "dealt_1_0")
         round_we(nc.scalar, dealt_1_0[:], raw_1_0, 0)
         we_q[1, 0] = quantise_we(dealt_1_0[:], "dealt_1_1_b")
+        gain_dealt = held([P, P], F32, "gain_dealt")
+        nc.vector.tensor_copy(out=gain_dealt[:].rearrange("p (t i) -> p t i", t=PACK),
+                              in_=gain_rows[:].rearrange("p (i t) -> p t i", t=PACK))
+        gain_cols = held([P, P], F32, "gain_cols")
+        nc.vector.transpose(gain_cols[:], gain_dealt[:])
         slope = held([P, 2 * PACK, 2], F32, "slope")
         nc.scalar.activation(out=slope[:].rearrange("p (g t) k -> p g t k", g=2), func=ACT.Copy, scale=1.0 / KNEE,
-                             in_=gain_sb[:, :, 0:PACK].unsqueeze(3).to_broadcast([P, 2, PACK, 2]))
+                             in_=gain_cols[:].rearrange("p (t g c) -> p g t c", t=PACK, g=2)[:, :, :, 0:1]
+                             .to_broadcast([P, 2, PACK, 2]))
         v_w.append([gather_words(tab_w[1], idx, n, name, QUARTER)[0]
                     for n, name in enumerate(("dealt_1_0", "v_w_1_1", "v_w_1_2", "v_w_1_3"))])
 

@@ -21,7 +21,6 @@ QUARTER = 256
 SUB = 128
 SPAN = 2 * SUB * PACK
 WR_FIRST = 8
-V_FIRST = (4, 8)
 FLOOR = 2.0 ** -60
 KNEE = 16.0
 LOG_SLOTS = 5
@@ -58,7 +57,7 @@ def tile_list_cortical_softplus_currents_kernel(
         nc.vector.memset(tab2_sc[:].bitcast(I32), 0)
         v2_sc = held([P, S], U8, "v2_sc")
         v_sc = [held([P, S], U8, "v_sc_%d" % a) for a in range(2)]
-        for plane in [v2_sc, wi_sc_raw, wr_sc_raw] + v_sc:
+        for plane in (wi_sc_raw, wr_sc_raw):
             nc.vector.memset(plane[:].bitcast(I32), 0)
         gain_rows = held([P, P], F32, "gain_rows")
         nc.vector.memset(gain_rows[:], 0.0)
@@ -87,12 +86,12 @@ def tile_list_cortical_softplus_currents_kernel(
 
         tab2_w = held([P, T2], I32, "tab2_w")
         tab_w = [held([P, T], I32, "tab_w_%d" % a) for a in range(2)]
-        nc.sync.dma_start(idx2[:], offs2)
         load_words(tab2_w, tab2_words[0], 0, T2 // 2)
+        nc.sync.dma_start(idx2[:], offs2)
         nc.sync.dma_start(out=tab2_sc[0:P:8, :].bitcast(I32), in_=tab2_scales[0].bitcast(I32))
         load_words(tab2_w, tab2_words[0], T2 // 2, T2)
         nc.sync.dma_start(idx[:], offs)
-        nc.sync.dma_start(out=tab_sc[0:P:4, :].bitcast(I32), in_=tab_scales.rearrange("a q c -> (a q) c").bitcast(I32))
+        nc.sync.dma_start(out=tab_sc[0:P:4, :].bitcast(I32), in_=tab_scales.rearrange("a q c -> q a c").bitcast(I32))
         load_words(tab_w[0], tab_words[0], 0, T // 2)
         wi_raw = held([P, 2 * H], U8, "wi_raw")
         nc.sync.dma_start(out=wi_raw[:].bitcast(I32), in_=wi_words[0].bitcast(I32))
@@ -100,17 +99,19 @@ def tile_list_cortical_softplus_currents_kernel(
         raw_0_0 = load_we(0, 0, GROUP, "we_raw_0_0")
         v2_rows = held([P, S], U8, "v2_rows")
         nc.vector.tensor_copy(v2_rows[:], tab2_sc[:].indirect(idx2[:]))
+        nc.vector.tensor_copy(out=v2_sc[:].bitcast(I32), in_=v2_rows[:].bitcast(I32))
         v_rows = held([P, S], U8, "v_rows")
         nc.vector.tensor_copy(v_rows[:], tab_sc[:].indirect(idx[:]))
-        load_plane(v2_sc, v2_rows[0:P:8, :])
+        for plane in v_sc:
+            nc.vector.tensor_copy(out=plane[:].bitcast(I32), in_=v_rows[:].bitcast(I32))
+        load_plane(v2_sc, v2_rows[0:P:8, :], range(1, 4))
         load_plane(wi_sc_raw, wi_scales[0], range(2, 4))
         load_words(tab_w[0], tab_words[0], T // 2, T)
-        load_plane(v_sc[0], v_rows[0:P // 2:4, :], first=V_FIRST[0])
+        load_plane(v_sc[0], v_rows[0:P:8, :], range(1, 4))
         raw_1_0 = load_we(1, 0, GROUP, "we_raw_1_0")
-        load_words(tab_w[1], tab_words[1], 0, T // 2)
-        load_plane(v_sc[1], v_rows[P // 2:P:4, :], first=V_FIRST[1])
+        load_plane(v_sc[1], v_rows[4:P:8, :], range(1, 4), first=4)
         nc.sync.dma_start(out=gain_rows[0:P:16, :], in_=gain.rearrange("(g q c) -> q g c", g=2, q=4))
-        load_words(tab_w[1], tab_words[1], T // 2, T)
+        load_words(tab_w[1], tab_words[1], 0, T)
         raw_0_1 = load_we(0, GROUP, GROUP, "we_raw_0_1", 7168)
         raw_1_1 = load_we(1, GROUP, GROUP, "we_raw_1_1")
         load_plane_pair(wr_sc_raw, wr_scales, WR_FIRST)
@@ -168,14 +169,15 @@ def tile_list_cortical_softplus_currents_kernel(
         round_we(nc.scalar, dealt_1_0[:], raw_1_0, 0)
         we_q[1, 0] = quantise_we(dealt_1_0[:], "dealt_1_1_b")
         gain_dealt = held([P, P], F32, "gain_dealt")
-        nc.vector.tensor_copy(out=gain_dealt[:].rearrange("p (t i) -> p t i", t=PACK),
-                              in_=gain_rows[:].rearrange("p (i t) -> p t i", t=PACK))
+        nc.vector.tensor_scalar(out=gain_dealt[:].rearrange("p (t i) -> p t i", t=PACK),
+                                in0=gain_rows[:].rearrange("p (i t) -> p t i", t=PACK),
+                                scalar1=1.0 / KNEE, scalar2=0.0, op0=ALU.mult, op1=ALU.add)
         gain_cols = held([P, P], F32, "gain_cols")
         nc.vector.transpose(gain_cols[:], gain_dealt[:])
         slope = held([P, 2 * PACK, 2], F32, "slope")
-        nc.scalar.activation(out=slope[:].rearrange("p (g t) k -> p g t k", g=2), func=ACT.Copy, scale=1.0 / KNEE,
-                             in_=gain_cols[:].rearrange("p (t g c) -> p g t c", t=PACK, g=2)[:, :, :, 0:1]
-                             .to_broadcast([P, 2, PACK, 2]))
+        nc.vector.tensor_copy(out=slope[:].rearrange("p (g t) k -> p g t k", g=2),
+                              in_=gain_cols[:].rearrange("p (t g c) -> p g t c", t=PACK, g=2)[:, :, :, 0:1]
+                              .to_broadcast([P, 2, PACK, 2]))
         v_w.append([gather_words(tab_w[1], idx, n, name, QUARTER)[0]
                     for n, name in enumerate(("dealt_1_0", "v_w_1_1", "v_w_1_2", "v_w_1_3"))])
 
@@ -197,7 +199,7 @@ def tile_list_cortical_softplus_currents_kernel(
                 else:
                     codes, lhs_sc = we_q[kind, g][t]
                     lhs = codes.bitcast(FP8X4)
-                    rhs, rhs_sc = v_w[kind][n], v_sc[kind][V_FIRST[kind]:, js]
+                    rhs, rhs_sc = v_w[kind][n], v_sc[kind][4 * kind:, js]
                 nc.tensor.matmul_mx(out=bank[:, e, :], lhsT=lhs, lhsT_scale=lhs_sc,
                                     rhs=rhs.bitcast(FP8X4), rhs_scale=rhs_sc,
                                     start=(kind == 2 and e == 0), stop=(kind == 1 and e == 1))

@@ -264,7 +264,7 @@ def tile_list_cortical_softplus_currents_kernel(
         ys = [held([P, 2, 2, PACK, QUARTER], F32, "tab_w_%d" % half) for half in range(2)]
         woven = [held([P, 2, S // 2, PACK], BF16, name) for name in ("we_raw_0_1", "we_raw_1_1")]
         y_codes = held([P, 2, S], I32, "y_codes")
-        y_scales = held([P, S], U8, "y_scales")
+        y_scales = held([P, 2, S], U8, "y_scales")
         whole = slice(0, QUARTER)
         halves = (slice(0, SUB), slice(SUB, QUARTER))
         lns, h, h_codes, h_scales = {}, {}, {}, {}
@@ -331,7 +331,7 @@ def tile_list_cortical_softplus_currents_kernel(
         def quantise_y(n, g):
             js = slice(n * QUARTER, (n + 1) * QUARTER)
             part = slice((n % 2) * QUARTER, (n % 2 + 1) * QUARTER)
-            nc.vector.quantize_mx(out=y_codes[:, g, js].bitcast(FP8X4), scales=y_scales[4 * g:, js],
+            nc.vector.quantize_mx(out=y_codes[:, g, js].bitcast(FP8X4), scales=y_scales[:, g, js],
                                   in_=woven[n // 2][:, g, part, :].rearrange("p c t -> p (c t)"))
 
         def store_words(n, gs=slice(0, 2)):
@@ -340,9 +340,10 @@ def tile_list_cortical_softplus_currents_kernel(
             nc.sync.dma_start(out=words[:, gs, js], in_=y_codes[:, gs, js])
 
         def store_scales():
-            for q in range(4):
-                nc.sync.dma_start(out=out_2[:, 4 * q:4 * q + 4, :].bitcast(I32),
-                                  in_=y_scales[32 * q:32 * q + 8, :].bitcast(I32))
+            for r in range(4):
+                queue = nc.scalar if r % 2 else nc.sync
+                queue.dma_start(out=out_2[:, r:16:4, :].rearrange("g q c -> q g c").bitcast(I32),
+                                in_=y_scales[r:P:32].bitcast(I32))
 
         both, group = slice(0, 2), (slice(0, 1), slice(1, 2))
         for js in halves:

from contextlib import ExitStack

import concourse.mybir as mybir

F32 = mybir.dt.float32
BF16 = mybir.dt.bfloat16
I32 = mybir.dt.int32
U32 = mybir.dt.uint32
U16 = mybir.dt.uint16
U8 = mybir.dt.uint8
FP8X4 = mybir.dt.float8_e4m3fn_x4
FP4X4 = mybir.dt.float4_e2m1fn_x4
ACT = mybir.ActivationFunctionType
ALU = mybir.AluOpType

P = 128
PACK = 4
GROUP = P * PACK
T, T2, S, H, N = 4096, 2048, 1024, 1024, 1024
QUARTER = 256
SUB = 128
SPAN = 2 * SUB * PACK
WR_FIRST = 8
FLOOR = 2.0 ** -60
KNEE = 16.0
LOG_SLOTS = 5
FLOPS = 5368709120


def tile_list_cortical_softplus_currents_kernel(
    tc, tab_words, tab_scales, tab2_words, tab2_scales, offs, offs2, we, wi_words, wi_scales, gain,
    wr_words, wr_scales, out_0, out_1, out_2,
):
    nc = tc.nc
    with ExitStack() as ctx:
        lists = ctx.enter_context(tc.tile_pool(name="lists", bufs=1))
        keep = ctx.enter_context(tc.tile_pool(name="keep", bufs=1))
        late = ctx.enter_context(tc.tile_pool(name="late", bufs=1))
        ring = ctx.enter_context(tc.tile_pool(name="ring", bufs=3))
        psum = ctx.enter_context(tc.psum_pool(name="psum", bufs=8))

        def held(shape, dtype, name):
            return keep.tile(shape, dtype, name=name, align_bytes=64)

        idx = lists.tile([P, S // 16], U16, name="idx")
        idx2 = lists.tile([P, S // 16], U16, name="idx2")

        tab_sc = held([P, T], U8, "tab_sc")
        tab2_sc = held([P, T2], U8, "tab2_sc")
        wi_sc_raw = held([P, H], U8, "wi_sc_raw")
        wr_sc_raw = held([P, N], U8, "wr_sc_raw")
        zero = held([P, 1], F32, "lns")
        nc.gpsimd.memset(zero[:], 0.0)
        floor = held([P, 1], F32, "floor")
        nc.gpsimd.memset(floor[:], FLOOR)
        nc.gpsimd.memset(tab_sc[:].bitcast(I32), 0)
        nc.vector.memset(tab2_sc[:].bitcast(I32), 0)
        v2_sc = held([P, S], U8, "v2_sc")
        v_sc = [held([P, S], U8, "v_sc_%d" % a) for a in range(2)]
        for plane in (wi_sc_raw, wr_sc_raw):
            nc.vector.memset(plane[:].bitcast(I32), 0)
        gain_rows = held([P, P], F32, "gain_rows")
        nc.vector.memset(gain_rows[:], 0.0)

        def load_we(a, first, width, name, offset=None):
            if offset is None:
                raw = held([P, PACK, width], F32, name)
            else:
                raw = late.tile([P, PACK, width], F32, name=name, align_bytes=64, offset=offset)
            rows = we[a * GROUP:(a + 1) * GROUP, first:first + width].rearrange("(p i) c -> p i c", i=PACK)
            nc.sync.dma_start(out=raw[:], in_=rows)
            return raw

        def load_words(tile, words, first, last):
            src = words.rearrange("p c i -> p (c i)").bitcast(I32)
            nc.sync.dma_start(out=tile[:, first:last], in_=src[:, first:last])

        def load_plane_pair(tile, scales, first):
            for q in range(4):
                rows = tile[32 * q + first:32 * q + first + 8, :]
                nc.sync.dma_start(out=rows.bitcast(I32), in_=scales[:, 4 * q:4 * q + 4, :].bitcast(I32))

        def load_plane(tile, scales, rows=range(4), first=0):
            for r in rows:
                nc.sync.dma_start(out=tile[first + r:P:32, :].bitcast(I32), in_=scales[r:16:4, :].bitcast(I32))

        tab2_w = held([P, T2], I32, "tab2_w")
        tab_w = [held([P, T], I32, "tab_w_%d" % a) for a in range(2)]
        load_words(tab2_w, tab2_words[0], 0, T2 // 2)
        nc.sync.dma_start(idx2[:], offs2)
        nc.sync.dma_start(out=tab2_sc[0:P:8, :].bitcast(I32), in_=tab2_scales[0].bitcast(I32))
        load_words(tab2_w, tab2_words[0], T2 // 2, T2)
        nc.sync.dma_start(idx[:], offs)
        nc.sync.dma_start(out=tab_sc[0:P:4, :].bitcast(I32), in_=tab_scales.rearrange("a q c -> q a c").bitcast(I32))
        load_words(tab_w[0], tab_words[0], 0, T // 2)
        wi_raw = held([P, 2 * H], U8, "wi_raw")
        nc.sync.dma_start(out=wi_raw[:].bitcast(I32), in_=wi_words[0].bitcast(I32))
        load_plane(wi_sc_raw, wi_scales[0], range(2))
        raw_0_0 = load_we(0, 0, GROUP, "we_raw_0_0")
        v2_rows = held([P, S], U8, "v2_rows")
        nc.vector.tensor_copy(v2_rows[:], tab2_sc[:].indirect(idx2[:]))
        nc.vector.tensor_copy(out=v2_sc[:].bitcast(I32), in_=v2_rows[:].bitcast(I32))
        v_rows = held([P, S], U8, "v_rows")
        nc.vector.tensor_copy(v_rows[:], tab_sc[:].indirect(idx[:]))
        for plane in v_sc:
            nc.vector.tensor_copy(out=plane[:].bitcast(I32), in_=v_rows[:].bitcast(I32))
        load_plane(v2_sc, v2_rows[0:P:8, :], range(1, 4))
        load_plane(wi_sc_raw, wi_scales[0], range(2, 4))
        load_words(tab_w[0], tab_words[0], T // 2, T)
        load_plane(v_sc[0], v_rows[0:P:8, :], range(1, 4))
        raw_1_0 = load_we(1, 0, GROUP, "we_raw_1_0")
        load_plane(v_sc[1], v_rows[4:P:8, :], range(1, 4), first=4)
        nc.sync.dma_start(out=gain_rows[0:P:16, :], in_=gain.rearrange("(g q c) -> q g c", g=2, q=4))
        load_words(tab_w[1], tab_words[1], 0, T)
        raw_0_1 = load_we(0, GROUP, GROUP, "we_raw_0_1", 7168)
        raw_1_1 = load_we(1, GROUP, GROUP, "we_raw_1_1")
        load_plane_pair(wr_sc_raw, wr_scales, WR_FIRST)
        wr_raw = [held([P, N], I32, "wr_raw_%d" % a) for a in range(2)]
        for a in range(2):
            load_words(wr_raw[a], wr_words[a], 0, N)

        def gather_words(table, offsets, part, name, width=S // 2):
            tile = held([P, width], U32, name)
            cols = width // 16
            nc.vector.tensor_copy(tile[:], table[:].bitcast(U32).indirect(offsets[:, part * cols:(part + 1) * cols]))
            return [tile[:, c:c + QUARTER] for c in range(0, width, QUARTER)]

        def deal(engine, dealt, raw, run):
            engine.tensor_copy(
                out=dealt.rearrange("p (g t c i) -> p g c t i", g=2, t=PACK, i=run),
                in_=raw.rearrange("p (g c i t) -> p g c t i", g=2, t=PACK, i=run),
            )

        def round_we(engine, dealt, raw, first):
            last = first + dealt.shape[1]
            if engine is nc.vector:
                dst = dealt.rearrange("p t m i -> p m i t")
                src = raw[:].rearrange("p i (m t) -> p m i t", t=PACK)[:, :, :, first:last]
            else:
                dst = dealt.rearrange("p t m i -> p m t i")
                src = raw[:].rearrange("p i (m t) -> p m t i", t=PACK)[:, :, first:last, :]
            if engine is nc.scalar:
                engine.activation(out=dst, in_=src, func=ACT.Copy, scale=-1.0)
            else:
                engine.tensor_scalar(out=dst, in0=src, scalar1=-1.0, scalar2=0.0, op0=ALU.mult, op1=ALU.add)

        def quantise_we(dealt, name, codes=None):
            width = dealt.shape[1] * P
            if codes is None:
                codes = held([P, width], U32, name + "_codes")
            scales = held([P, width], U8, name + "_scales")
            nc.vector.quantize_mx(out=codes[:].bitcast(FP8X4), scales=scales[:],
                                  in_=dealt.rearrange("p t m i -> p (t m i)"))
            return [(codes[:, c:c + P], scales[:, c:c + P]) for c in range(0, width, P)]

        v2_w = gather_words(tab2_w, idx2, 0, "tab_sc")
        wi_w = held([P, 2 * H], U8, "wi_w")
        deal(nc.vector, wi_w[:].bitcast(U16), wi_raw[:].bitcast(U16), 8)
        wi_sc = held([P, H], U8, "wi_sc")
        deal(nc.vector, wi_sc[:], wi_sc_raw[:], 16)
        v2_w.extend(gather_words(tab2_w, idx2, 1, "wi_sc_raw"))
        v_w = [gather_words(tab_w[0], idx, 0, "wi_raw")]
        we_q = {}
        dealt_0_0 = held([P, PACK, P, PACK], BF16, "dealt_0_0")
        round_we(nc.scalar, dealt_0_0[:], raw_0_0, 0)
        we_q[0, 0] = quantise_we(dealt_0_0[:], "we_0_0")
        v_w[0].extend(gather_words(tab_w[0], idx, 1, "dealt_0_0"))
        dealt_1_0 = held([P, PACK, P, PACK], BF16, "dealt_1_0")
        round_we(nc.scalar, dealt_1_0[:], raw_1_0, 0)
        we_q[1, 0] = quantise_we(dealt_1_0[:], "dealt_1_1_b")
        gain_dealt = held([P, P], F32, "gain_dealt")
        nc.vector.tensor_scalar(out=gain_dealt[:].rearrange("p (t i) -> p t i", t=PACK),
                                in0=gain_rows[:].rearrange("p (i t) -> p t i", t=PACK),
                                scalar1=1.0 / KNEE, scalar2=0.0, op0=ALU.mult, op1=ALU.add)
        gain_cols = held([P, P], F32, "gain_cols")
        nc.vector.transpose(gain_cols[:], gain_dealt[:])
        slope = held([P, 2 * PACK, 2], F32, "slope")
        nc.vector.tensor_copy(out=slope[:].rearrange("p (g t) k -> p g t k", g=2),
                              in_=gain_cols[:].rearrange("p (t g c) -> p g t c", t=PACK, g=2)[:, :, :, 0:1]
                              .to_broadcast([P, 2, PACK, 2]))
        v_w.append([gather_words(tab_w[1], idx, n, name, QUARTER)[0]
                    for n, name in enumerate(("dealt_1_0", "v_w_1_1", "v_w_1_2", "v_w_1_3"))])

        dealt_0_1 = late.tile([P, PACK, P, PACK], BF16, name="dealt_0_1", align_bytes=64, offset=0)
        round_we(nc.gpsimd, dealt_0_1[:], raw_0_1, 0)

        quarters = S // QUARTER
        sig = [held([P, 2 * SPAN], F32, "sig_%d" % n if n > 1 else "we_raw_%d_0" % n) for n in range(quarters)]
        factor = {}

        def drive(bank, kind, g, pair, n):
            js = slice(n * QUARTER, (n + 1) * QUARTER)
            for e in range(2):
                t = 2 * pair + e
                u = g * PACK + t
                if kind == 2:
                    lhs, lhs_sc = wi_w[:, u * 2 * P:(u + 1) * 2 * P].bitcast(FP4X4), wi_sc[:, u * P:(u + 1) * P]
                    rhs, rhs_sc = v2_w[n], v2_sc[:, js]
                else:
                    codes, lhs_sc = we_q[kind, g][t]
                    lhs = codes.bitcast(FP8X4)
                    rhs, rhs_sc = v_w[kind][n], v_sc[kind][4 * kind:, js]
                nc.tensor.matmul_mx(out=bank[:, e, :], lhsT=lhs, lhsT_scale=lhs_sc,
                                    rhs=rhs.bitcast(FP8X4), rhs_scale=rhs_sc,
                                    start=(kind == 2 and e == 0), stop=(kind == 1 and e == 1))

        def drain(bank, g, pair, n):
            sigmoid(bank, g, pair, n)
            linear(bank, g, pair, n)

        def sigmoid(bank, g, pair, n):
            sig_out = sig[n][:].rearrange("p (g a j e) -> p g a j e", g=2, a=2, e=2)[:, g, pair]
            nc.scalar.activation(out=sig_out, in_=bank[:].rearrange("p e j -> p j e"), func=ACT.Sigmoid, bias=zero[:])

        def linear(bank, g, pair, n):
            out = factor[n][:].rearrange("p (g j a c) -> p g j a c", g=2, a=2, c=4)[:, g, :, pair, :]
            first = g * PACK + 2 * pair
            slopes = slope[:, first:first + 2, :].rearrange("p e k -> p (e k)").unsqueeze(1).to_broadcast([P, SUB, 4])
            nc.vector.scalar_tensor_tensor(out=out, in0=bank[:].rearrange("p e (k j) -> p j (e k)", k=2),
                                           scalar=-KNEE, in1=slopes, op0=ALU.min, op1=ALU.mult)

        units = [(pair, n) for n in range(quarters) for pair in range(2)]
        banks = [psum.tile([P, 2, QUARTER], F32, name="bank", tag="bank") for unit in units]
        for kind in (2, 0, 1):
            for bank, (pair, n) in zip(banks, units):
                drive(bank, kind, 0, pair, n)
        factor[0] = held([P, 2 * SPAN], F32, "tab2_w")
        factor[1] = held([P, 2 * SPAN], F32, "factor_1")
        for u in range(4):
            drain(banks[u], 0, *units[u])
        early = late.tile([P, 2, P, PACK], BF16, name="early", align_bytes=64, offset=7680)
        we_q[0, 1] = quantise_we(dealt_0_1[:, 0:2], "we_0_1_a")
        round_we(nc.vector, early[:], raw_1_1, 0)
        we_q[0, 1].extend(quantise_we(dealt_0_1[:, 2:4], "we_0_1_b"))
        we_q[1, 1] = quantise_we(early[:], "we_1_1_a")
        factor[2] = late.tile([P, 2 * SPAN], F32, name="factor_2", align_bytes=64, offset=0)
        factor[3] = late.tile([P, 2 * SPAN], F32, name="factor_3", align_bytes=64, offset=9216)
        for u in range(4, 8):
            sigmoid(banks[u], 0, *units[u])
        final = held([P, 2, P, PACK], BF16, "dealt_1_1_b_codes")
        round_we(nc.scalar, final[:], raw_1_1, 2)
        for u in range(4, 6):
            linear(banks[u], 0, *units[u])
        we_q[1, 1].extend(quantise_we(final[:], "we_1_1_b", late.tile([P, 2 * P], U32, name="last_codes", align_bytes=64, offset=8192)))
        for u in range(6, 8):
            linear(banks[u], 0, *units[u])

        units = [(pair, n) for pair in range(2) for n in range(quarters)]
        banks = [psum.tile([P, 2, QUARTER], F32, name="bank", tag="bank") for unit in units]
        for bank, (pair, n) in zip(banks, units):
            for kind in (2, 0, 1):
                drive(bank, kind, 1, pair, n)
        for bank, (pair, n) in zip(banks, units):
            drain(bank, 1, pair, n)

        wr_dealt = held([P, 2 * N + N // 4], I32, "dealt_1_1_b_codes")
        wr_w = [wr_dealt[:, a * N:(a + 1) * N] for a in range(2)]
        wr_sc = wr_dealt[:, 2 * N:].bitcast(U8)
        deal(nc.gpsimd, wr_sc, wr_sc_raw[:], 16)
        for a in range(2):
            deal(nc.gpsimd, wr_w[a], wr_raw[a][:], 4)

        lns_all = held([P, LOG_SLOTS, QUARTER, 2, 2], F32, "lns")
        ys = [held([P, 2, 2, PACK, QUARTER], F32, "tab_w_%d" % half) for half in range(2)]
        woven = [held([P, 2, S // 2, PACK], BF16, name) for name in ("we_raw_0_1", "we_raw_1_1")]
        y_codes = held([P, 2, S], I32, "y_codes")
        y_scales = held([P, 2, S], U8, "y_scales")
        whole = slice(0, QUARTER)
        halves = (slice(0, SUB), slice(SUB, QUARTER))
        lns, h, h_codes, h_scales = {}, {}, {}, {}
        for n in range(quarters):
            h_codes[n] = held([P, 2, QUARTER], U32, "h_codes_%d" % n)
            h_scales[n] = held([P, 2, QUARTER], U8, "h_scales_%d" % n)

        def logs(n, g, js):
            if js.start == 0:
                lns[n, g] = lns_all[:, len(lns) % LOG_SLOTS]
            src = sig[n][:].rearrange("p (g a j e) -> p g j a e", g=2, a=2, e=2)[:, g, js]
            nc.scalar.activation(out=lns[n, g][:, js], in_=src, func=ACT.Ln, bias=floor[:])

        def rates(n, g, js):
            if js.start == 0:
                h[n, g] = ring.tile([P, 2, SUB * PACK], BF16, name="h", bufs=4, align_bytes=64)
            ks = slice(js.start // SUB, js.stop // SUB)
            other = factor[n][:].rearrange("p (g c k) -> p g k c", g=2, k=2)[:, g, ks]
            nc.vector.scalar_tensor_tensor(
                out=h[n, g][:, ks], in0=lns[n, g].rearrange("p (k j) a e -> p k (j a e)", k=2)[:, ks],
                scalar=-KNEE, in1=other, op0=ALU.max, op1=ALU.mult)

        def quantise_h(n, g, js):
            ks = slice(js.start // SUB, js.stop // SUB)
            nc.vector.quantize_mx(out=h_codes[n][:, g, js].bitcast(FP8X4), scales=h_scales[n][:, g, js],
                                  in_=h[n, g][:, ks].rearrange("p k c -> p (k c)"))

        def current(out, u, a, n, js, start, stop):
            nc.tensor.matmul_mx(
                out=out, lhsT=wr_w[a][:, u * P:(u + 1) * P].bitcast(FP8X4),
                lhsT_scale=wr_sc[WR_FIRST + 4 * a:, u * P:(u + 1) * P],
                rhs=h_codes[n][:, a, js].bitcast(FP8X4), rhs_scale=h_scales[n][:, a, js], start=start, stop=stop)

        def store_y(n, g, ts, js):
            rows = out_0[g * GROUP:(g + 1) * GROUP, n * QUARTER:(n + 1) * QUARTER].rearrange("(p t) j -> p t j", t=PACK)
            nc.sync.dma_start(out=rows[:, ts, js], in_=ys[n // 2][:, n % 2, g, ts, js])

        def narrow(n, g, js):
            bank = psum.tile([P, PACK, SUB], F32, name="bank", tag="bank")
            for a in range(2):
                for t in range(PACK):
                    current(bank[:, t, :], g * PACK + t, a, n, js, a == 0 and t == 0, a == 1 and t == PACK - 1)
            nc.scalar.copy(out=ys[n // 2][:, n % 2, g, :, js], in_=bank[:])
            store_y(n, g, slice(0, PACK), js)

        def wide(n, g):
            pair_banks = [psum.tile([P, 2, QUARTER], F32, name="bank", tag="bank") for pair in range(2)]
            for a in range(2):
                for pair in range(2):
                    for e in range(2):
                        current(pair_banks[pair][:, e, :], g * PACK + 2 * pair + e, a, n, whole,
                                a == 0 and e == 0, a == 1 and e == 1)
            for pair in range(2):
                ts = slice(2 * pair, 2 * pair + 2)
                nc.scalar.copy(out=ys[n // 2][:, n % 2, g, ts, :], in_=pair_banks[pair][:])
                store_y(n, g, ts, whole)

        def weave(n, gs, js):
            first = (n % 2) * QUARTER
            nc.vector.tensor_copy(
                out=woven[n // 2][:, gs, first + js.start:first + js.stop, :].rearrange("p g (c i) t -> p g c t i", i=4),
                in_=ys[n // 2][:, n % 2, gs, :, js].rearrange("p g t (c i) -> p g c t i", i=4))

        def quantise_y(n, g):
            js = slice(n * QUARTER, (n + 1) * QUARTER)
            part = slice((n % 2) * QUARTER, (n % 2 + 1) * QUARTER)
            nc.vector.quantize_mx(out=y_codes[:, g, js].bitcast(FP8X4), scales=y_scales[:, g, js],
                                  in_=woven[n // 2][:, g, part, :].rearrange("p c t -> p (c t)"))

        def store_words(n, gs=slice(0, 2)):
            js = slice(n * QUARTER, (n + 1) * QUARTER)
            words = out_1.rearrange("g p j t -> p g (j t)").bitcast(I32)
            nc.sync.dma_start(out=words[:, gs, js], in_=y_codes[:, gs, js])

        def store_scales():
            for r in range(4):
                queue = nc.scalar if r % 2 else nc.sync
                queue.dma_start(out=out_2[:, r:16:4, :].rearrange("g q c -> q g c").bitcast(I32),
                                in_=y_scales[r:P:32].bitcast(I32))

        both, group = slice(0, 2), (slice(0, 1), slice(1, 2))
        for js in halves:
            for g in range(2):
                logs(0, g, js)
        for g in range(2):
            logs(1, g, whole)
        for js in halves:
            for g in range(2):
                rates(0, g, js)
            for g in range(2):
                quantise_h(0, g, js)
        for g in range(2):
            narrow(0, g, halves[0])
        logs(2, 0, whole)
        for g in range(2):
            rates(1, g, whole)
        for g in range(2):
            quantise_h(1, g, whole)
        for g in range(2):
            narrow(0, g, halves[1])
        logs(2, 1, whole)
        weave(0, both, halves[0])
        rates(2, 0, whole)
        weave(0, both, halves[1])
        quantise_h(2, 0, whole)
        wide(1, 0)
        logs(3, 0, whole)
        rates(2, 1, whole)
        quantise_y(0, 0)
        quantise_h(2, 1, whole)
        quantise_y(0, 1)
        store_words(0)
        wide(1, 1)
        logs(3, 1, whole)
        rates(3, 0, whole)
        weave(1, group[0], whole)
        quantise_h(3, 0, whole)
        wide(2, 0)
        wide(2, 1)
        rates(3, 1, whole)
        quantise_y(1, 0)
        quantise_h(3, 1, whole)
        wide(3, 0)
        wide(3, 1)
        weave(1, group[1], whole)
        weave(2, group[0], whole)
        quantise_y(1, 1)
        store_words(1)
        weave(2, group[1], whole)
        quantise_y(2, 0)
        weave(3, group[0], whole)
        quantise_y(2, 1)
        store_words(2)
        weave(3, group[1], halves[0])
        nc.scalar.copy(out=woven[1][:, 1, QUARTER + SUB:, :].rearrange("p (c i) t -> p c t i", i=4),
                       in_=ys[1][:, 1, 1, :, SUB:].rearrange("p t (c i) -> p c t i", i=4))
        for g in range(2):
            quantise_y(3, g)
            store_words(3, group[g])
        store_scales()
